import numpy as np
import ml_dtypes


def mxq(x, axis, fmt="e4m3"):
    dtype, down = {"e4m3": (ml_dtypes.float8_e4m3fn, 7), "e5m2": (ml_dtypes.float8_e5m2, 14)}[fmt]
    v = np.moveaxis(np.asarray(x, np.float32).astype(ml_dtypes.bfloat16).astype(np.float64), axis, -1)
    blocks = v.reshape(v.shape[:-1] + (-1, 32))
    amax = np.abs(blocks).max(-1, keepdims=True)
    byte = np.maximum(np.where(amax > 0, np.frexp(amax)[1] - 1 + 127, 0) - down, 1)
    scale = np.exp2(byte - 127.0)
    codes = (blocks / scale).astype(np.float32).astype(dtype).astype(np.float64)
    return np.moveaxis((codes * scale).reshape(v.shape), -1, axis)


WIDE = False


def mx_kscale(k):
    if not WIDE:
        return np.ones(k)
    levels = np.array([24, -24, 12, -12, 0])
    if k % 512:
        return np.exp2(np.random.permutation(np.resize(levels, k // 32))).repeat(32)
    a = np.empty((k // 512, 16))
    for p in range(k // 512):
        a[p, :8] = np.random.permutation(np.resize(levels, 8))
        for g in range(8):
            far = levels[np.abs(levels - a[p, g]) >= 10]
            a[p, g + 8] = far[np.random.randint(len(far))]
    return np.exp2(a.ravel()).repeat(32)


def f64(x):
    return np.asarray(x).astype(np.float64)


def striped(idx):
    return np.tile(idx.reshape(-1, 16).T, (8, 1)).astype(np.uint16)


def unstriped(offs):
    return offs[:16].T.reshape(-1).astype(np.int64)


E2M1 = np.array([0.0, 0.5, 1.0, 1.5, 2.0, 3.0, 4.0, 6.0, -0.0, -0.5, -1.0, -1.5, -2.0, -3.0, -4.0, -6.0])


def pack_weight(w, fmt):
    k, n = w.shape
    w = f64(np.asarray(w, np.float32).astype(ml_dtypes.bfloat16)).reshape(k // 32, 32, n)
    amax = np.abs(w).max(1)
    if fmt == "e4m3":
        byte = np.frexp(amax)[1] - 1 + 127 - 7
    else:
        mant, ex = np.frexp(amax / 6.0)
        byte = np.where(mant > 0.5, ex, ex - 1) + 127
    byte = np.clip(np.where(amax > 0, byte, 1), 1, 254)
    scaled = (w * np.exp2(127.0 - byte)[:, None, :]).reshape(k, n).astype(np.float32)
    by_word = np.ascontiguousarray(scaled.reshape(k // 512, 128, 4, n).transpose(0, 1, 3, 2))
    if fmt == "e4m3":
        words = by_word.astype(ml_dtypes.float8_e4m3fn).view(np.uint8)
    else:
        c = by_word.astype(ml_dtypes.float4_e2m1fn).view(np.uint8) & 0xF
        words = (c[..., 0::2] | (c[..., 1::2] << 4)).reshape(k // 512, 128, 2 * n)
    return np.ascontiguousarray(words), np.ascontiguousarray(byte.astype(np.uint8).reshape(k // 512, 16, n))


def unpack_weight(words, scales, fmt):
    g, _, n = scales.shape
    words = np.ascontiguousarray(words).reshape(g, 128, n, -1)
    if fmt == "e4m3":
        vals = words.view(ml_dtypes.float8_e4m3fn).astype(np.float64)
    else:
        nib = np.empty((g, 128, n, 4), np.uint8)
        nib[..., 0::2] = words & 0xF
        nib[..., 1::2] = words >> 4
        vals = E2M1[nib]
    vals = vals * np.repeat(np.exp2(scales.astype(np.float64) - 127.0), 8, axis=1)[..., None]
    return vals.transpose(0, 1, 3, 2).reshape(g * 512, n)


def pack_table4(v):
    words, scales = pack_weight(v, "e2m1")
    g, t = words.shape[0] // 2, v.shape[1]
    return np.ascontiguousarray(words.reshape(g, 2, 128, t, 2).transpose(0, 2, 3, 1, 4).reshape(g, 128, t, 4)), scales


def unpack_table4(words, scales):
    g, _, t, _ = words.shape
    return unpack_weight(words.reshape(g, 128, t, 2, 2).transpose(0, 3, 1, 2, 4).reshape(2 * g, 128, 2 * t), scales, "e2m1")


K, L, R, N, T, J = 512, 1024, 512, 512, 4096, 2048


def setup_inputs():
    n = np.random.standard_normal
    s = mx_kscale(K)[:, None]
    s2 = mx_kscale(L)[:, None]
    u = mx_kscale(R)[:, None]
    p_tab = pack_weight(n((K, T)) * s, "e4m3")
    p_tab2 = pack_table4(n((L, T)) * s2)
    p_nr = pack_weight(n((R, N)) / np.sqrt(R) / u, "e4m3")
    p_ni = pack_weight(n((R, N)) / np.sqrt(R) / u, "e2m1")
    return {
        "tab_words": p_tab[0],
        "tab_scales": p_tab[1],
        "tab2_words": p_tab2[0],
        "tab2_scales": p_tab2[1],
        "wer": (n((K, R)) / np.sqrt(K) / s * u.T).astype(np.float32),
        "wei": (n((K, R)) / np.sqrt(K) / s * u.T).astype(np.float32),
        "wrr": (n((L, R)) / np.sqrt(L) / s2).astype(np.float32),
        "wri": (n((L, R)) / np.sqrt(L) / s2).astype(np.float32),
        "nr_words": p_nr[0],
        "nr_scales": p_nr[1],
        "ni_words": p_ni[0],
        "ni_scales": p_ni[1],
        "offs": striped(np.random.permutation(T)[:J]),
        "offs2": striped(np.random.permutation(T)[:J]),
    }


def reference(tab_words, tab_scales, tab2_words, tab2_scales, wer, wei, wrr, wri, nr_words, nr_scales, ni_words, ni_scales, offs, offs2):
    idx = unstriped(offs)
    idx2 = unstriped(offs2)
    tab_ = unpack_weight(tab_words, tab_scales, "e4m3")[:, idx]
    tab2_ = unpack_table4(tab2_words, tab2_scales)[:, idx2]
    wer_ = mxq(f64(wer), 0, "e4m3")
    aer = wer_.T @ tab_
    wei_ = mxq(f64(wei), 0, "e4m3")
    aei = wei_.T @ tab_
    wrr_ = mxq(f64(wrr), 0, "e4m3")
    arr = wrr_.T @ tab2_
    wri_ = mxq(f64(wri), 0, "e4m3")
    ari = wri_.T @ tab2_
    hr = aer * arr - aei * ari
    hi = aer * ari + aei * arr
    hr_ = mxq(hr, 0, "e4m3")
    hi_ = mxq(hi, 0, "e4m3")
    nr_ = unpack_weight(nr_words, nr_scales, "e4m3")
    ni_ = unpack_weight(ni_words, ni_scales, "e2m1")
    y = nr_.T @ hr_ + ni_.T @ hi_
    return y

@@ -1,0 +1,221 @@
+from contextlib import ExitStack
+
+import concourse.mybir as mybir
+
+K, L, R, N, T, J = 512, 1024, 512, 512, 4096, 2048
+FLOPS = 2 * J * R * (2 * K + 2 * L + 2 * N)
+
+F32 = mybir.dt.float32
+BF16 = mybir.dt.bfloat16
+I32 = mybir.dt.int32
+U32 = mybir.dt.uint32
+U16 = mybir.dt.uint16
+U8 = mybir.dt.uint8
+FP8X4 = mybir.dt.float8_e4m3fn_x4
+FP4X4 = mybir.dt.float4_e2m1fn_x4
+MULT = mybir.AluOpType.mult
+ADD = mybir.AluOpType.add
+
+P = 128
+PACK = 4
+BLK = 128
+NBLK = J // BLK
+SLICE = 512
+LAG = 2
+
+
+def tile_list_ckg_none_kernel(
+    tc, tab_words, tab_scales, tab2_words, tab2_scales, wer, wei, wrr, wri,
+    nr_words, nr_scales, ni_words, ni_scales, offs, offs2, out,
+):
+    nc = tc.nc
+    with ExitStack() as ctx:
+        keep = ctx.enter_context(tc.tile_pool(name="keep", bufs=1))
+        work = ctx.enter_context(tc.tile_pool(name="work", bufs=2))
+        work3 = ctx.enter_context(tc.tile_pool(name="work3", bufs=3))
+        psum1 = ctx.enter_context(tc.psum_pool(name="psum1", bufs=1))
+        psum2 = ctx.enter_context(tc.psum_pool(name="psum2", bufs=2))
+
+        list1 = keep.tile([P, J // 16], U16, name="list1")
+        list2 = keep.tile([P, J // 16], U16, name="list2")
+        t1_words = keep.tile([P, T], I32, name="t1_words", align_bytes=64)
+        t2_words = keep.tile([P, T], I32, name="t2_words", align_bytes=64)
+        t1_scales = keep.tile([P, T], U8, name="t1_scales", align_bytes=64)
+        t2_scales = keep.tile([P, T], U8, name="t2_scales", align_bytes=64)
+        e_words = keep.tile([P, J], U32, name="e_words", align_bytes=64)
+        e_scales = keep.tile([P, J], U8, name="e_scales", align_bytes=64)
+        r_pairs = keep.tile([P, J], U32, name="r_pairs", align_bytes=64)
+        r_words = keep.tile([P, 2, 2 * J], U8, name="r_words", align_bytes=64)
+        r_scales0 = keep.tile([P, J], U8, name="r_scales0", align_bytes=64)
+        r_scales1 = keep.tile([P, J], U8, name="r_scales1", align_bytes=64)
+        r_scales = [r_scales0, r_scales1]
+        nr_w = keep.tile([P, N], I32, name="nr_w", align_bytes=64)
+        nr_s = keep.tile([P, N], U8, name="nr_s", align_bytes=64)
+        ni_w = keep.tile([P, 2 * N], U8, name="ni_w", align_bytes=64)
+        ni_s = keep.tile([P, N], U8, name="ni_s", align_bytes=64)
+
+        names = ["er", "ei", "rr0", "rr1", "ri0", "ri1"]
+        src = {"er": wer, "ei": wei, "rr0": wrr[0:512, :], "rr1": wrr[512:1024, :],
+               "ri0": wri[0:512, :], "ri1": wri[512:1024, :]}
+        raw = {n: keep.tile([P, PACK, R], F32, name="raw_" + n, align_bytes=64) for n in names}
+        wb = {n: keep.tile([P, PACK * R], BF16, name="wb_" + n, align_bytes=64) for n in names}
+        wq = {n: keep.tile([P, R], U32, name="wq_" + n, align_bytes=64) for n in names}
+        ws = {n: keep.tile([P, R], U8, name="ws_" + n, align_bytes=64) for n in names}
+
+        def load_plane(plane, rows):
+            for q in range(4):
+                nc.sync.dma_start(
+                    out=plane[32 * q : 32 * q + 32, :].bitcast(I32),
+                    in_=rows[4 * q : 4 * q + 4, :].bitcast(I32).partition_broadcast(8),
+                )
+
+        def load_w(n):
+            nc.sync.dma_start(out=raw[n][:], in_=src[n].rearrange("(p j) r -> p j r", j=PACK))
+
+        def cast_w(n):
+            nc.scalar.copy(
+                out=wb[n][:].rearrange("p (t m j) -> p m j t", t=PACK, j=PACK),
+                in_=raw[n][:].rearrange("p j (m t) -> p m j t", t=PACK),
+            )
+
+        def quant_w(n):
+            nc.vector.quantize_mx(out=wq[n][:].bitcast(FP8X4), scales=ws[n][:], in_=wb[n][:])
+
+        nc.vector.memset(r_scales1[:].bitcast(I32), 0)
+
+        nc.sync.dma_start(list1[:], offs)
+        load_plane(t1_scales, tab_scales[0])
+        load_w("er")
+        nc.sync.dma_start(list2[:], offs2)
+        load_w("ei")
+        rows2 = tab2_scales.rearrange("a q t -> (a q) t").bitcast(I32)
+        for q in range(4):
+            nc.sync.dma_start(out=t2_scales[32 * q : 32 * q + 16, :].bitcast(I32), in_=rows2[4 * q : 4 * q + 16, :])
+            nc.sync.dma_start(out=t2_scales[32 * q + 16 : 32 * q + 32, :].bitcast(I32), in_=rows2[4 * q + 4 : 4 * q + 20, :])
+        nc.sync.dma_start(out=t1_words[:], in_=tab_words[0].rearrange("p t i -> p (t i)").bitcast(I32))
+        load_w("rr0")
+        nc.sync.dma_start(out=t2_words[:], in_=tab2_words[0].rearrange("p t i -> p (t i)").bitcast(I32))
+        load_w("rr1")
+        load_w("ri0")
+        load_w("ri1")
+        nc.sync.dma_start(out=nr_w[:], in_=nr_words[0].rearrange("p n i -> p (n i)").bitcast(I32))
+        nc.sync.dma_start(out=ni_w[:].bitcast(I32), in_=ni_words[0].bitcast(I32))
+        load_plane(nr_s, nr_scales[0])
+        load_plane(ni_s, ni_scales[0])
+
+        nc.vector.tensor_copy(e_scales[:], t1_scales[:].indirect(list1[:]))
+        cast_w("er")
+        cast_w("ei")
+        nc.vector.tensor_copy(r_scales0[:], t2_scales[:].indirect(list2[:]))
+        nc.scalar.dma_start(out=r_scales1[0:100, :].bitcast(I32), in_=r_scales0[28:128, :].bitcast(I32))
+        quant_w("er")
+        quant_w("ei")
+        for s in range(J // SLICE):
+            cols = slice(s * SLICE, (s + 1) * SLICE)
+            nc.vector.tensor_copy(
+                e_words[:, cols], t1_words[:].bitcast(U32).indirect(list1[:, s * SLICE // 16 : (s + 1) * SLICE // 16]))
+        cast_w("rr0")
+        quant_w("rr0")
+        r16 = r_words[:].bitcast(U16)
+
+        def gather2(s):
+            cols = slice(s * SLICE, (s + 1) * SLICE)
+            nc.vector.tensor_copy(
+                r_pairs[:, cols], t2_words[:].bitcast(U32).indirect(list2[:, s * SLICE // 16 : (s + 1) * SLICE // 16]))
+
+        def part2(s):
+            cols = slice(s * SLICE, (s + 1) * SLICE)
+            nc.vector.tensor_copy(r16[:, :, cols], r_pairs[:, cols].bitcast(U16).rearrange("p (n d) -> p d n", d=2))
+
+        gather2(0)
+        gather2(1)
+        part2(0)
+        cast_w("rr1")
+        quant_w("rr1")
+        gather2(2)
+        part2(1)
+        cast_w("ri0")
+        gather2(3)
+        part2(2)
+        quant_w("ri0")
+        cast_w("ri1")
+        part2(3)
+        quant_w("ri1")
+
+        out_v = out.rearrange("(t p) j -> p t j", p=P)
+        h_tiles = {}
+
+        def project_e(bank, n, k):
+            tok = slice(k * BLK, (k + 1) * BLK)
+            for t in range(PACK):
+                m = slice(t * P, (t + 1) * P)
+                nc.tensor.matmul_mx(
+                    out=bank[:, t * BLK : (t + 1) * BLK], lhsT=wq[n][:, m].bitcast(FP8X4), lhsT_scale=ws[n][:, m],
+                    rhs=e_words[:, tok].bitcast(FP8X4), rhs_scale=e_scales[:, tok], start=True, stop=True)
+
+        def project_r(bank, n, k):
+            tok = slice(k * BLK, (k + 1) * BLK)
+            for t in range(PACK):
+                m = slice(t * P, (t + 1) * P)
+                for a in range(2):
+                    w = n + str(a)
+                    nc.tensor.matmul_mx(
+                        out=bank[:, t * BLK : (t + 1) * BLK], lhsT=wq[w][:, m].bitcast(FP8X4), lhsT_scale=ws[w][:, m],
+                        rhs=r_words[:, a, 2 * k * BLK : 2 * (k + 1) * BLK].bitcast(FP4X4),
+                        rhs_scale=r_scales[a][:, tok], start=(a == 0), stop=(a == 1))
+
+        def inter(bank):
+            return bank[:].rearrange("p (t n) -> p n t", t=PACK)
+
+        def products(k):
+            a_ps = psum1.tile([P, PACK * BLK], F32, name="a_ps")
+            b_ps = psum1.tile([P, PACK * BLK], F32, name="b_ps")
+            c_ps = psum2.tile([P, PACK * BLK], F32, name="c_ps")
+            d_ps = psum2.tile([P, PACK * BLK], F32, name="d_ps")
+            ab = work3.tile([P, 2, BLK, PACK], F32, name="ab")
+            project_e(a_ps, "er", k)
+            nc.scalar.copy(out=ab[:, 0], in_=inter(a_ps))
+            project_e(b_ps, "ei", k)
+            nc.scalar.copy(out=ab[:, 1], in_=inter(b_ps))
+            project_r(c_ps, "rr", k)
+            project_r(d_ps, "ri", k)
+            pc = work.tile([P, 2, BLK, PACK], F32, name="pc")
+            pd = work.tile([P, 2, BLK, PACK], F32, name="pd")
+            nc.vector.tensor_tensor(pc[:], inter(c_ps).unsqueeze(1).to_broadcast([P, 2, BLK, PACK]), ab[:], MULT)
+            nc.vector.scalar_tensor_tensor(pd[:, 0], inter(d_ps), -1.0, ab[:, 1], MULT, MULT)
+            nc.vector.tensor_tensor(pd[:, 1], inter(d_ps), ab[:, 0], MULT)
+            h = work3.tile([P, 2 * BLK * PACK], BF16, name="h", align_bytes=64)
+            eng = nc.vector if k == NBLK - 1 else nc.gpsimd
+            return (eng, h, pc, pd)
+
+        def combine(k, eng, h, pc, pd):
+            eng.tensor_tensor(h[:], pc[:].rearrange("p c n t -> p (c n t)"), pd[:].rearrange("p c n t -> p (c n t)"), ADD)
+            h_tiles[k] = h
+
+        def score(k):
+            hq = work.tile([P, 2 * BLK], U32, name="hq", align_bytes=64)
+            hs = work.tile([P, 2 * BLK], U8, name="hs", align_bytes=64)
+            nc.vector.quantize_mx(out=hq[:].bitcast(FP8X4), scales=hs[:], in_=h_tiles[k][:])
+            y_ps = psum2.tile([P, PACK * BLK], F32, name="y_ps")
+            for t in range(N // P):
+                m = slice(t * P, (t + 1) * P)
+                o = y_ps[:, t * BLK : (t + 1) * BLK]
+                nc.tensor.matmul_mx(out=o, lhsT=nr_w[:, m].bitcast(FP8X4), lhsT_scale=nr_s[:, m],
+                                    rhs=hq[:, 0:BLK].bitcast(FP8X4), rhs_scale=hs[:, 0:BLK], start=True, stop=False)
+                nc.tensor.matmul_mx(out=o, lhsT=ni_w[:, 2 * t * P : 2 * (t + 1) * P].bitcast(FP4X4), lhsT_scale=ni_s[:, m],
+                                    rhs=hq[:, BLK : 2 * BLK].bitcast(FP8X4), rhs_scale=hs[:, BLK : 2 * BLK],
+                                    start=False, stop=True)
+            y = work3.tile([P, N // P, BLK], F32, name="y")
+            nc.scalar.copy(out=y[:].rearrange("p t n -> p (t n)"), in_=y_ps[:])
+            nc.sync.dma_start(out=out_v[:, :, k * BLK : (k + 1) * BLK], in_=y[:])
+
+        for k in range(NBLK):
+            st = products(k)
+            if k < NBLK - 1:
+                combine(k, *st)
+            if k >= LAG:
+                score(k - LAG)
+            if k == NBLK - 1:
+                combine(k, *st)
+        for k in range(NBLK - LAG, NBLK):
+            score(k)

@@ -31,6 +31,7 @@ def tile_list_ckg_none_kernel(
     nc = tc.nc
     with ExitStack() as ctx:
         keep = ctx.enter_context(tc.tile_pool(name="keep", bufs=1))
+        stage = ctx.enter_context(tc.tile_pool(name="stage", bufs=1))
         work = ctx.enter_context(tc.tile_pool(name="work", bufs=2))
         work3 = ctx.enter_context(tc.tile_pool(name="work3", bufs=3))
         psum1 = ctx.enter_context(tc.psum_pool(name="psum1", bufs=1))
@@ -42,9 +43,7 @@ def tile_list_ckg_none_kernel(
         t2_words = keep.tile([P, T], I32, name="t2_words", align_bytes=64)
         t1_scales = keep.tile([P, T], U8, name="t1_scales", align_bytes=64)
         t2_scales = keep.tile([P, T], U8, name="t2_scales", align_bytes=64)
-        e_words = keep.tile([P, J], U32, name="e_words", align_bytes=64)
         e_scales = keep.tile([P, J], U8, name="e_scales", align_bytes=64)
-        r_pairs = keep.tile([P, J], U32, name="r_pairs", align_bytes=64)
         r_words = keep.tile([P, 2, 2 * J], U8, name="r_words", align_bytes=64)
         r_scales0 = keep.tile([P, J], U8, name="r_scales0", align_bytes=64)
         r_scales1 = keep.tile([P, J], U8, name="r_scales1", align_bytes=64)
@@ -54,12 +53,14 @@ def tile_list_ckg_none_kernel(
         ni_w = keep.tile([P, 2 * N], U8, name="ni_w", align_bytes=64)
         ni_s = keep.tile([P, N], U8, name="ni_s", align_bytes=64)
 
-        names = ["er", "ei", "rr0", "rr1", "ri0", "ri1"]
+        names = ["rr0", "rr1", "ri0", "ri1", "er", "ei"]
+        names2 = ["ri0", "ri1", "er", "ei"]
         src = {"er": wer, "ei": wei, "rr0": wrr[0:512, :], "rr1": wrr[512:1024, :],
                "ri0": wri[0:512, :], "ri1": wri[512:1024, :]}
-        raw = {n: keep.tile([P, PACK, R], F32, name="raw_" + n, align_bytes=64) for n in names}
-        wb = {n: keep.tile([P, PACK * R], BF16, name="wb_" + n, align_bytes=64) for n in names}
-        wq = {n: keep.tile([P, R], U32, name="wq_" + n, align_bytes=64) for n in names}
+        raw = {n: stage.tile([P, PACK, R], F32, name="raw_" + n, align_bytes=64, offset=i * 8192) for i, n in enumerate(names)}
+        wb = {n: keep.tile([P, PACK * R], BF16, name="wb_" + n, tag="wb_" + n, align_bytes=64) for n in names}
+        r_pairs = [keep.tile([P, SLICE], U32, name="pairs%d" % s, tag="slot%d" % s, align_bytes=64) for s in range(4)]
+        wq = {n: keep.tile([P, R], U32, name="wq_" + n, align_bytes=64) for n in names[:2]}
         ws = {n: keep.tile([P, R], U8, name="ws_" + n, align_bytes=64) for n in names}
 
         def load_plane(plane, rows):
@@ -68,6 +69,12 @@ def tile_list_ckg_none_kernel(
                     out=plane[32 * q : 32 * q + 32, :].bitcast(I32),
                     in_=rows[4 * q : 4 * q + 4, :].bitcast(I32).partition_broadcast(8),
                 )
+
+        def load_words(tile, words):
+            rows = words[0].rearrange("p t i -> p (t i)").bitcast(I32)
+            for half in range(2):
+                cols = slice(half * T // 2, (half + 1) * T // 2)
+                nc.sync.dma_start(out=tile[:, cols], in_=rows[:, cols])
 
         def load_w(n):
             nc.sync.dma_start(out=raw[n][:], in_=src[n].rearrange("(p j) r -> p j r", j=PACK))
@@ -79,68 +86,72 @@ def tile_list_ckg_none_kernel(
             )
 
         def quant_w(n):
+            if n not in wq:
+                wq[n] = keep.tile([P, R], U32, name="wq_" + n, tag="slot%d" % (names2.index(n)), align_bytes=64)
             nc.vector.quantize_mx(out=wq[n][:].bitcast(FP8X4), scales=ws[n][:], in_=wb[n][:])
 
         nc.vector.memset(r_scales1[:].bitcast(I32), 0)
 
         nc.sync.dma_start(list1[:], offs)
         load_plane(t1_scales, tab_scales[0])
-        load_w("er")
+        load_w("rr0")
         nc.sync.dma_start(list2[:], offs2)
-        load_w("ei")
+        load_w("rr1")
         rows2 = tab2_scales.rearrange("a q t -> (a q) t").bitcast(I32)
         for q in range(4):
             nc.sync.dma_start(out=t2_scales[32 * q : 32 * q + 16, :].bitcast(I32), in_=rows2[4 * q : 4 * q + 16, :])
             nc.sync.dma_start(out=t2_scales[32 * q + 16 : 32 * q + 32, :].bitcast(I32), in_=rows2[4 * q + 4 : 4 * q + 20, :])
-        nc.sync.dma_start(out=t1_words[:], in_=tab_words[0].rearrange("p t i -> p (t i)").bitcast(I32))
-        load_w("rr0")
-        nc.sync.dma_start(out=t2_words[:], in_=tab2_words[0].rearrange("p t i -> p (t i)").bitcast(I32))
-        load_w("rr1")
+        load_words(t2_words, tab2_words)
         load_w("ri0")
         load_w("ri1")
+        load_w("er")
+        load_w("ei")
+        load_words(t1_words, tab_words)
         nc.sync.dma_start(out=nr_w[:], in_=nr_words[0].rearrange("p n i -> p (n i)").bitcast(I32))
         nc.sync.dma_start(out=ni_w[:].bitcast(I32), in_=ni_words[0].bitcast(I32))
         load_plane(nr_s, nr_scales[0])
         load_plane(ni_s, ni_scales[0])
 
-        nc.vector.tensor_copy(e_scales[:], t1_scales[:].indirect(list1[:]))
-        cast_w("er")
-        cast_w("ei")
-        nc.vector.tensor_copy(r_scales0[:], t2_scales[:].indirect(list2[:]))
-        nc.scalar.dma_start(out=r_scales1[0:100, :].bitcast(I32), in_=r_scales0[28:128, :].bitcast(I32))
-        quant_w("er")
-        quant_w("ei")
-        for s in range(J // SLICE):
+        r16 = r_words[:].bitcast(U16)
+
+        def gather1(s):
             cols = slice(s * SLICE, (s + 1) * SLICE)
             nc.vector.tensor_copy(
                 e_words[:, cols], t1_words[:].bitcast(U32).indirect(list1[:, s * SLICE // 16 : (s + 1) * SLICE // 16]))
-        cast_w("rr0")
-        quant_w("rr0")
-        r16 = r_words[:].bitcast(U16)
 
         def gather2(s):
-            cols = slice(s * SLICE, (s + 1) * SLICE)
             nc.vector.tensor_copy(
-                r_pairs[:, cols], t2_words[:].bitcast(U32).indirect(list2[:, s * SLICE // 16 : (s + 1) * SLICE // 16]))
+                r_pairs[s][:], t2_words[:].bitcast(U32).indirect(list2[:, s * SLICE // 16 : (s + 1) * SLICE // 16]))
 
         def part2(s):
             cols = slice(s * SLICE, (s + 1) * SLICE)
-            nc.vector.tensor_copy(r16[:, :, cols], r_pairs[:, cols].bitcast(U16).rearrange("p (n d) -> p d n", d=2))
+            nc.vector.tensor_copy(r16[:, :, cols], r_pairs[s][:].bitcast(U16).rearrange("p (n d) -> p d n", d=2))
 
+        nc.vector.tensor_copy(e_scales[:], t1_scales[:].indirect(list1[:]))
+        cast_w("rr0")
+        cast_w("rr1")
+        nc.vector.tensor_copy(r_scales0[:], t2_scales[:].indirect(list2[:]))
+        nc.gpsimd.dma_start(out=r_scales1[0:100, :].bitcast(I32), in_=r_scales0[28:128, :].bitcast(I32))
+        quant_w("rr0")
+        quant_w("rr1")
         gather2(0)
         gather2(1)
         part2(0)
-        cast_w("rr1")
-        quant_w("rr1")
+        cast_w("ri0")
         gather2(2)
         part2(1)
-        cast_w("ri0")
-        gather2(3)
-        part2(2)
         quant_w("ri0")
         cast_w("ri1")
-        part2(3)
+        gather2(3)
+        part2(2)
         quant_w("ri1")
+        part2(3)
+        cast_w("er")
+        quant_w("er")
+        cast_w("ei")
+        quant_w("ei")
+        e_words = keep.tile([P, J], U32, name="e_words", tag="wb_ei", align_bytes=64)
+        gather1(0)
 
         out_v = out.rearrange("(t p) j -> p t j", p=P)
         h_tiles = {}
@@ -168,22 +179,25 @@ def tile_list_ckg_none_kernel(
             return bank[:].rearrange("p (t n) -> p n t", t=PACK)
 
         def products(k):
-            a_ps = psum1.tile([P, PACK * BLK], F32, name="a_ps")
-            b_ps = psum1.tile([P, PACK * BLK], F32, name="b_ps")
-            c_ps = psum2.tile([P, PACK * BLK], F32, name="c_ps")
-            d_ps = psum2.tile([P, PACK * BLK], F32, name="d_ps")
-            ab = work3.tile([P, 2, BLK, PACK], F32, name="ab")
-            project_e(a_ps, "er", k)
-            nc.scalar.copy(out=ab[:, 0], in_=inter(a_ps))
-            project_e(b_ps, "ei", k)
-            nc.scalar.copy(out=ab[:, 1], in_=inter(b_ps))
+            a_ps = psum2.tile([P, PACK * BLK], F32, name="a_ps")
+            b_ps = psum2.tile([P, PACK * BLK], F32, name="b_ps")
+            c_ps = psum1.tile([P, PACK * BLK], F32, name="c_ps")
+            d_ps = psum1.tile([P, PACK * BLK], F32, name="d_ps")
+            base = (k + 5) % 6 * 8192
+            c_sb = stage.tile([P, BLK, PACK], F32, name="c_sb%d" % k, align_bytes=64, offset=base)
+            d_sb = stage.tile([P, BLK, PACK], F32, name="d_sb%d" % k, align_bytes=64, offset=base + 2048)
             project_r(c_ps, "rr", k)
+            nc.scalar.copy(out=c_sb[:], in_=inter(c_ps))
             project_r(d_ps, "ri", k)
+            nc.scalar.copy(out=d_sb[:], in_=inter(d_ps))
+            project_e(a_ps, "er", k)
+            project_e(b_ps, "ei", k)
             pc = work.tile([P, 2, BLK, PACK], F32, name="pc")
             pd = work.tile([P, 2, BLK, PACK], F32, name="pd")
-            nc.vector.tensor_tensor(pc[:], inter(c_ps).unsqueeze(1).to_broadcast([P, 2, BLK, PACK]), ab[:], MULT)
-            nc.vector.scalar_tensor_tensor(pd[:, 0], inter(d_ps), -1.0, ab[:, 1], MULT, MULT)
-            nc.vector.tensor_tensor(pd[:, 1], inter(d_ps), ab[:, 0], MULT)
+            nc.vector.tensor_tensor(pc[:, 1], inter(a_ps), d_sb[:], MULT)
+            nc.vector.scalar_tensor_tensor(pd[:, 0], inter(b_ps), -1.0, d_sb[:], MULT, MULT)
+            nc.vector.tensor_tensor(pc[:, 0], inter(a_ps), c_sb[:], MULT)
+            nc.vector.tensor_tensor(pd[:, 1], inter(b_ps), c_sb[:], MULT)
             h = work3.tile([P, 2 * BLK * PACK], BF16, name="h", align_bytes=64)
             eng = nc.vector if k == NBLK - 1 else nc.gpsimd
             return (eng, h, pc, pd)
@@ -193,7 +207,9 @@ def tile_list_ckg_none_kernel(
             h_tiles[k] = h
 
         def score(k):
-            hq = work.tile([P, 2 * BLK], U32, name="hq", align_bytes=64)
+            after = NBLK - 1 if k == NBLK - 2 else k + LAG
+            part = 0 if k == NBLK - 2 else 2048
+            hq = stage.tile([P, 2 * BLK], U32, name="hq%d" % k, align_bytes=64, offset=(after + 5) % 6 * 8192 + part)
             hs = work.tile([P, 2 * BLK], U8, name="hs", align_bytes=64)
             nc.vector.quantize_mx(out=hq[:].bitcast(FP8X4), scales=hs[:], in_=h_tiles[k][:])
             y_ps = psum2.tile([P, PACK * BLK], F32, name="y_ps")
@@ -217,5 +233,7 @@ def tile_list_ckg_none_kernel(
                 score(k - LAG)
             if k == NBLK - 1:
                 combine(k, *st)
+            if k % 4 == 1 and k // 4 + 1 < J // SLICE:
+                gather1(k // 4 + 1)
         for k in range(NBLK - LAG, NBLK):
             score(k)

@@ -1,6 +1,7 @@
 from contextlib import ExitStack
 
 import concourse.mybir as mybir
+from concourse.masks import make_identity
 
 K, L, R, N, T, J = 512, 1024, 512, 512, 4096, 2048
 FLOPS = 2 * J * R * (2 * K + 2 * L + 2 * N)
@@ -21,7 +22,9 @@ PACK = 4
 BLK = 128
 NBLK = J // BLK
 SLICE = 512
-LAG = 2
+LEAD = 3
+GROUP = 4
+MODES = "TGGGTGGGTGGGTGTV"
 
 
 def tile_list_ckg_none_kernel(
@@ -32,43 +35,53 @@ def tile_list_ckg_none_kernel(
     with ExitStack() as ctx:
         keep = ctx.enter_context(tc.tile_pool(name="keep", bufs=1))
         stage = ctx.enter_context(tc.tile_pool(name="stage", bufs=1))
-        work = ctx.enter_context(tc.tile_pool(name="work", bufs=2))
         work3 = ctx.enter_context(tc.tile_pool(name="work3", bufs=3))
+        work4 = ctx.enter_context(tc.tile_pool(name="work4", bufs=4))
         psum1 = ctx.enter_context(tc.psum_pool(name="psum1", bufs=1))
-        psum2 = ctx.enter_context(tc.psum_pool(name="psum2", bufs=2))
+        psum3 = ctx.enter_context(tc.psum_pool(name="psum3", bufs=3))
 
         list1 = keep.tile([P, J // 16], U16, name="list1")
         list2 = keep.tile([P, J // 16], U16, name="list2")
-        t1_words = keep.tile([P, T], I32, name="t1_words", align_bytes=64)
+        ident = keep.tile([P, P], F32, name="ident", align_bytes=64)
         t2_words = keep.tile([P, T], I32, name="t2_words", align_bytes=64)
         t1_scales = keep.tile([P, T], U8, name="t1_scales", align_bytes=64)
-        t2_scales = keep.tile([P, T], U8, name="t2_scales", align_bytes=64)
         e_scales = keep.tile([P, J], U8, name="e_scales", align_bytes=64)
         r_words = keep.tile([P, 2, 2 * J], U8, name="r_words", align_bytes=64)
         r_scales0 = keep.tile([P, J], U8, name="r_scales0", align_bytes=64)
         r_scales1 = keep.tile([P, J], U8, name="r_scales1", align_bytes=64)
         r_scales = [r_scales0, r_scales1]
-        nr_w = keep.tile([P, N], I32, name="nr_w", align_bytes=64)
-        nr_s = keep.tile([P, N], U8, name="nr_s", align_bytes=64)
-        ni_w = keep.tile([P, 2 * N], U8, name="ni_w", align_bytes=64)
-        ni_s = keep.tile([P, N], U8, name="ni_s", align_bytes=64)
 
-        names = ["rr0", "rr1", "ri0", "ri1", "er", "ei"]
-        names2 = ["ri0", "ri1", "er", "ei"]
+        names = ["ri1", "ri0", "rr1", "rr0", "er", "ei"]
         src = {"er": wer, "ei": wei, "rr0": wrr[0:512, :], "rr1": wrr[512:1024, :],
                "ri0": wri[0:512, :], "ri1": wri[512:1024, :]}
-        raw = {n: stage.tile([P, PACK, R], F32, name="raw_" + n, align_bytes=64, offset=i * 8192) for i, n in enumerate(names)}
-        wb = {n: keep.tile([P, PACK * R], BF16, name="wb_" + n, tag="wb_" + n, align_bytes=64) for n in names}
-        r_pairs = [keep.tile([P, SLICE], U32, name="pairs%d" % s, tag="slot%d" % s, align_bytes=64) for s in range(4)]
-        wq = {n: keep.tile([P, R], U32, name="wq_" + n, align_bytes=64) for n in names[:2]}
-        ws = {n: keep.tile([P, R], U8, name="ws_" + n, align_bytes=64) for n in names}
+        RAW = 4 * PACK * R
+        raw = {n: stage.tile([P, PACK, R], F32, name="raw_" + n, align_bytes=64, offset=i * RAW)[:] for i, n in enumerate(names[:4])}
+        raw["ei"] = stage.tile([P, PACK, R], F32, name="raw_ei", align_bytes=64, offset=4 * RAW)[:]
+        raw["er"] = stage.tile([P, PACK, R], F32, name="raw_er", align_bytes=64, offset=5 * RAW)[:]
+        t2_scales = stage.tile([P, T], U8, name="t2_scales", align_bytes=64, offset=6 * RAW - 768)
+        t1_words = stage.tile([P, T], I32, name="t1_words", align_bytes=64, offset=6 * RAW + 5 * R)
+        late = 6 * RAW + 5 * R + 4 * T
+        wb = {n: keep.tile([P, PACK * R], BF16, name="wb_" + n, align_bytes=64) for n in ("er", "ei")}
+        wb["rr0"] = stage.tile([P, PACK * R], BF16, name="wb_rr0", align_bytes=64, offset=4 * RAW)
+        wb["ri0"] = stage.tile([P, PACK * R], BF16, name="wb_ri0", align_bytes=64, offset=late + 8 * N + 4 * J)
+        wb["ri1"] = stage.tile([P, PACK * R], BF16, name="wb_ri1", align_bytes=64, offset=late + 8 * N + 4 * J + 8 * R)
+        e_words = stage.tile([P, J], U32, name="e_words", align_bytes=64, offset=late + 8 * N)
+        wb["rr1"] = stage.tile([P, PACK * R], BF16, name="wb_rr1", align_bytes=64, offset=late)
+        nr_w = stage.tile([P, N], I32, name="nr_w", align_bytes=64, offset=late)
+        ni_w = stage.tile([P, 2 * N], U8, name="ni_w", align_bytes=64, offset=late + 4 * N)
+        nr_s = stage.tile([P, N], U8, name="nr_s", align_bytes=64, offset=late + 6 * N)
+        ni_s = stage.tile([P, N], U8, name="ni_s", align_bytes=64, offset=late + 7 * N)
+        r_pairs = [keep.tile([P, SLICE], U32, name="pairs%d" % s, align_bytes=64) for s in range(2)]
+        r_pairs = r_pairs + [stage.tile([P, SLICE], U32, name="pairs%d" % s, align_bytes=64, offset=late + 8 * N + 4 * J + 8 * R * (s - 2))
+                             for s in (2, 3)]
+        wq = {n: keep.tile([P, R], U32, name="wq_" + n, align_bytes=64) for n in names if n != "rr0"}
+        wq["rr0"] = stage.tile([P, R], U32, name="wq_rr0", align_bytes=64, offset=6 * RAW)
+        ws = {n: keep.tile([P, R], U8, name="ws_" + n, align_bytes=64) for n in names if n != "rr1"}
+        ws["rr1"] = stage.tile([P, R], U8, name="ws_rr1", align_bytes=64, offset=6 * RAW + 4 * R)
 
         def load_plane(plane, rows):
             for q in range(4):
-                nc.sync.dma_start(
-                    out=plane[32 * q : 32 * q + 32, :].bitcast(I32),
-                    in_=rows[4 * q : 4 * q + 4, :].bitcast(I32).partition_broadcast(8),
-                )
+                nc.sync.dma_start(out=plane[32 * q : 32 * q + 4, :].bitcast(I32), in_=rows[4 * q : 4 * q + 4, :].bitcast(I32))
 
         def load_words(tile, words):
             rows = words[0].rearrange("p t i -> p (t i)").bitcast(I32)
@@ -77,40 +90,36 @@ def tile_list_ckg_none_kernel(
                 nc.sync.dma_start(out=tile[:, cols], in_=rows[:, cols])
 
         def load_w(n):
-            nc.sync.dma_start(out=raw[n][:], in_=src[n].rearrange("(p j) r -> p j r", j=PACK))
+            nc.sync.dma_start(out=raw[n], in_=src[n].rearrange("(p j) r -> p j r", j=PACK))
 
         def cast_w(n):
             nc.scalar.copy(
                 out=wb[n][:].rearrange("p (t m j) -> p m j t", t=PACK, j=PACK),
-                in_=raw[n][:].rearrange("p j (m t) -> p m j t", t=PACK),
+                in_=raw[n].rearrange("p j (m t) -> p m j t", t=PACK),
             )
 
         def quant_w(n):
-            if n not in wq:
-                wq[n] = keep.tile([P, R], U32, name="wq_" + n, tag="slot%d" % (names2.index(n)), align_bytes=64)
             nc.vector.quantize_mx(out=wq[n][:].bitcast(FP8X4), scales=ws[n][:], in_=wb[n][:])
 
-        nc.vector.memset(r_scales1[:].bitcast(I32), 0)
+        for plane in (t2_scales, r_scales1):
+            nc.vector.memset(plane[:].bitcast(I32), 0)
+        make_identity(nc, ident[:])
 
         nc.sync.dma_start(list1[:], offs)
-        load_plane(t1_scales, tab_scales[0])
+        for q in range(4):
+            nc.sync.dma_start(
+                out=t1_scales[32 * q : 32 * q + 32, :].bitcast(I32),
+                in_=tab_scales[0][4 * q : 4 * q + 4, :].bitcast(I32).partition_broadcast(8),
+            )
         load_w("rr0")
         nc.sync.dma_start(list2[:], offs2)
         load_w("rr1")
-        rows2 = tab2_scales.rearrange("a q t -> (a q) t").bitcast(I32)
         for q in range(4):
-            nc.sync.dma_start(out=t2_scales[32 * q : 32 * q + 16, :].bitcast(I32), in_=rows2[4 * q : 4 * q + 16, :])
-            nc.sync.dma_start(out=t2_scales[32 * q + 16 : 32 * q + 32, :].bitcast(I32), in_=rows2[4 * q + 4 : 4 * q + 20, :])
+            nc.sync.dma_start(out=t2_scales[32 * q : 32 * q + 8, :].bitcast(I32),
+                              in_=tab2_scales[:, 4 * q : 4 * q + 4, :].bitcast(I32))
         load_words(t2_words, tab2_words)
         load_w("ri0")
         load_w("ri1")
-        load_w("er")
-        load_w("ei")
-        load_words(t1_words, tab_words)
-        nc.sync.dma_start(out=nr_w[:], in_=nr_words[0].rearrange("p n i -> p (n i)").bitcast(I32))
-        nc.sync.dma_start(out=ni_w[:].bitcast(I32), in_=ni_words[0].bitcast(I32))
-        load_plane(nr_s, nr_scales[0])
-        load_plane(ni_s, ni_scales[0])
 
         r16 = r_words[:].bitcast(U16)
 
@@ -131,109 +140,185 @@ def tile_list_ckg_none_kernel(
         cast_w("rr0")
         cast_w("rr1")
         nc.vector.tensor_copy(r_scales0[:], t2_scales[:].indirect(list2[:]))
-        nc.gpsimd.dma_start(out=r_scales1[0:100, :].bitcast(I32), in_=r_scales0[28:128, :].bitcast(I32))
+        nc.sync.dma_start(out=r_scales1[0:100, :].bitcast(I32), in_=r_scales0[4:104, :].bitcast(I32))
+        load_w("er")
+        load_words(t1_words, tab_words)
         quant_w("rr0")
+        load_w("ei")
         quant_w("rr1")
+        for plane in (nr_s, ni_s):
+            nc.gpsimd.memset(plane[:].bitcast(I32), 0)
+        nc.sync.dma_start(out=nr_w[:], in_=nr_words[0].rearrange("p n i -> p (n i)").bitcast(I32))
+        nc.sync.dma_start(out=ni_w[:].bitcast(I32), in_=ni_words[0].bitcast(I32))
+        load_plane(nr_s, nr_scales[0])
+        load_plane(ni_s, ni_scales[0])
         gather2(0)
         gather2(1)
         part2(0)
         cast_w("ri0")
-        gather2(2)
-        part2(1)
         quant_w("ri0")
+        part2(1)
         cast_w("ri1")
+        quant_w("ri1")
+        gather2(2)
         gather2(3)
         part2(2)
-        quant_w("ri1")
-        part2(3)
         cast_w("er")
         quant_w("er")
+        part2(3)
+        for s in range(J // SLICE):
+            gather1(s)
         cast_w("ei")
         quant_w("ei")
-        e_words = keep.tile([P, J], U32, name="e_words", tag="wb_ei", align_bytes=64)
-        gather1(0)
 
         out_v = out.rearrange("(t p) j -> p t j", p=P)
-        h_tiles = {}
+        cd, ab, prods = {}, {}, {}
+        h_both = keep.tile([P, 2 * (GROUP + 1) * R], BF16, name="h_both", align_bytes=64)
 
-        def project_e(bank, n, k):
-            tok = slice(k * BLK, (k + 1) * BLK)
-            for t in range(PACK):
-                m = slice(t * P, (t + 1) * P)
-                nc.tensor.matmul_mx(
-                    out=bank[:, t * BLK : (t + 1) * BLK], lhsT=wq[n][:, m].bitcast(FP8X4), lhsT_scale=ws[n][:, m],
-                    rhs=e_words[:, tok].bitcast(FP8X4), rhs_scale=e_scales[:, tok], start=True, stop=True)
+        def h_slot(k):
+            g, i = divmod(k, GROUP)
+            return i if i > 0 else GROUP * (g % 2)
 
-        def project_r(bank, n, k):
-            tok = slice(k * BLK, (k + 1) * BLK)
-            for t in range(PACK):
-                m = slice(t * P, (t + 1) * P)
-                for a in range(2):
-                    w = n + str(a)
-                    nc.tensor.matmul_mx(
-                        out=bank[:, t * BLK : (t + 1) * BLK], lhsT=wq[w][:, m].bitcast(FP8X4), lhsT_scale=ws[w][:, m],
-                        rhs=r_words[:, a, 2 * k * BLK : 2 * (k + 1) * BLK].bitcast(FP4X4),
-                        rhs_scale=r_scales[a][:, tok], start=(a == 0), stop=(a == 1))
+        def tokens(k):
+            g = k // GROUP
+            return (g * GROUP + h_slot(k) - g % 2) * BLK
+
+        def h_part(c, first, count):
+            at = (c * (GROUP + 1) + first) * R
+            return h_both[:, at : at + count * R]
+
+        def project(bank, passes, k):
+            last = len(passes) - 1
+            if MODES[k] == "T":
+                for a, (w, codes, scales) in enumerate(passes):
+                    nc.tensor.matmul_mx(out=bank[:], lhsT=codes, lhsT_scale=scales, rhs=wq[w][:].bitcast(FP8X4),
+                                        rhs_scale=ws[w][:], start=(a == 0), stop=(a == last))
+            else:
+                for t in range(PACK):
+                    m = slice(t * P, (t + 1) * P)
+                    for a, (w, codes, scales) in enumerate(passes):
+                        nc.tensor.matmul_mx(out=bank[:, t * BLK : (t + 1) * BLK], lhsT=wq[w][:, m].bitcast(FP8X4),
+                                            lhsT_scale=ws[w][:, m], rhs=codes, rhs_scale=scales,
+                                            start=(a == 0), stop=(a == last))
+
+        def e_passes(n, k):
+            tok = slice(tokens(k), tokens(k) + BLK)
+            return [(n, e_words[:, tok].bitcast(FP8X4), e_scales[:, tok])]
+
+        def r_passes(n, k):
+            tok = slice(tokens(k), tokens(k) + BLK)
+            return [(n + str(a), r_words[:, a, 2 * tokens(k) : 2 * (tokens(k) + BLK)].bitcast(FP4X4), r_scales[a][:, tok])
+                    for a in range(2)]
 
         def inter(bank):
             return bank[:].rearrange("p (t n) -> p n t", t=PACK)
 
+        def view(bank, k):
+            return bank[:].rearrange("p (n t) -> p n t", t=PACK) if MODES[k] == "T" else inter(bank)
+
+        def relation(k):
+            c_at = (0, 1, 2, 10, 11, 8, 9, 3, 6, 7)[k % 10] * 4096
+            d_at = c_at + 2048
+            c_ps = psum1.tile([P, R], F32, name="c_ps")
+            d_ps = psum1.tile([P, R], F32, name="d_ps")
+            c_sb = stage.tile([P, BLK, PACK], F32, name="c_sb%d" % k, align_bytes=64, offset=c_at)
+            d_sb = stage.tile([P, BLK, PACK], F32, name="d_sb%d" % k, align_bytes=64, offset=d_at)
+            project(c_ps, r_passes("rr", k), k)
+            nc.scalar.copy(out=c_sb[:], in_=view(c_ps, k))
+            project(d_ps, r_passes("ri", k), k)
+            nc.scalar.copy(out=d_sb[:], in_=view(d_ps, k))
+            cd[k] = (c_sb, d_sb)
+
+        def entity(k):
+            a_ps = psum3.tile([P, R], F32, name="a_ps", tag="ab")
+            project(a_ps, e_passes("er", k), k)
+            b_ps = psum3.tile([P, R], F32, name="b_ps", tag="ab")
+            project(b_ps, e_passes("ei", k), k)
+            ab[k] = (a_ps, b_ps)
+
         def products(k):
-            a_ps = psum2.tile([P, PACK * BLK], F32, name="a_ps")
-            b_ps = psum2.tile([P, PACK * BLK], F32, name="b_ps")
-            c_ps = psum1.tile([P, PACK * BLK], F32, name="c_ps")
-            d_ps = psum1.tile([P, PACK * BLK], F32, name="d_ps")
-            base = (k + 5) % 6 * 8192
-            c_sb = stage.tile([P, BLK, PACK], F32, name="c_sb%d" % k, align_bytes=64, offset=base)
-            d_sb = stage.tile([P, BLK, PACK], F32, name="d_sb%d" % k, align_bytes=64, offset=base + 2048)
-            project_r(c_ps, "rr", k)
-            nc.scalar.copy(out=c_sb[:], in_=inter(c_ps))
-            project_r(d_ps, "ri", k)
-            nc.scalar.copy(out=d_sb[:], in_=inter(d_ps))
-            project_e(a_ps, "er", k)
-            project_e(b_ps, "ei", k)
-            pc = work.tile([P, 2, BLK, PACK], F32, name="pc")
-            pd = work.tile([P, 2, BLK, PACK], F32, name="pd")
-            nc.vector.tensor_tensor(pc[:, 1], inter(a_ps), d_sb[:], MULT)
-            nc.vector.scalar_tensor_tensor(pd[:, 0], inter(b_ps), -1.0, d_sb[:], MULT, MULT)
-            nc.vector.tensor_tensor(pc[:, 0], inter(a_ps), c_sb[:], MULT)
-            nc.vector.tensor_tensor(pd[:, 1], inter(b_ps), c_sb[:], MULT)
-            h = work3.tile([P, 2 * BLK * PACK], BF16, name="h", align_bytes=64)
-            eng = nc.vector if k == NBLK - 1 else nc.gpsimd
-            return (eng, h, pc, pd)
+            a_ps, b_ps = ab[k]
+            c_sb, d_sb = cd[k]
+            pa = work3.tile([P, 2, BLK, PACK], F32, name="pa", align_bytes=64)
+            pb = work3.tile([P, 2, BLK, PACK], F32, name="pb", align_bytes=64)
+            nc.vector.tensor_tensor(pa[:, 0], view(a_ps, k), c_sb[:], MULT)
+            nc.vector.tensor_tensor(pa[:, 1], view(a_ps, k), d_sb[:], MULT)
+            nc.vector.scalar_tensor_tensor(pb[:, 0], view(b_ps, k), -1.0, d_sb[:], MULT, MULT)
+            nc.vector.tensor_tensor(pb[:, 1], view(b_ps, k), c_sb[:], MULT)
+            prods[k] = (pa, pb)
 
-        def combine(k, eng, h, pc, pd):
-            eng.tensor_tensor(h[:], pc[:].rearrange("p c n t -> p (c n t)"), pd[:].rearrange("p c n t -> p (c n t)"), ADD)
-            h_tiles[k] = h
+        def combine(k):
+            pa, pb = prods[k]
+            fa = pa[:].rearrange("p c n t -> p (c n t)")
+            fb = pb[:].rearrange("p c n t -> p (c n t)")
+            if MODES[k] == "T":
+                for c in (1, 0):
+                    h_ps = psum3.tile([P, R], F32, name="h_ps", tag="hy")
+                    for t in range(PACK):
+                        cols = slice(c * R + t * P, c * R + (t + 1) * P)
+                        o = h_ps[:, t * BLK : (t + 1) * BLK]
+                        nc.tensor.matmul(o, lhsT=fa[:, cols], rhs=ident[:], is_transpose=True, start=True, stop=False)
+                        nc.tensor.matmul(o, lhsT=fb[:, cols], rhs=ident[:], is_transpose=True, start=False, stop=True)
+                    nc.scalar.copy(out=h_part(c, h_slot(k), 1).rearrange("p (n t) -> p n t", t=PACK), in_=inter(h_ps))
+            else:
+                eng = nc.vector if MODES[k] == "V" else nc.gpsimd
+                h = h_both[:].rearrange("p (c s r) -> p c s r", c=2, r=R)[:, :, h_slot(k), :]
+                eng.tensor_tensor(h, fa.rearrange("p (c r) -> p c r", c=2), fb.rearrange("p (c r) -> p c r", c=2), ADD)
 
-        def score(k):
-            after = NBLK - 1 if k == NBLK - 2 else k + LAG
-            part = 0 if k == NBLK - 2 else 2048
-            hq = stage.tile([P, 2 * BLK], U32, name="hq%d" % k, align_bytes=64, offset=(after + 5) % 6 * 8192 + part)
-            hs = work.tile([P, 2 * BLK], U8, name="hs", align_bytes=64)
-            nc.vector.quantize_mx(out=hq[:].bitcast(FP8X4), scales=hs[:], in_=h_tiles[k][:])
-            y_ps = psum2.tile([P, PACK * BLK], F32, name="y_ps")
+        def quantise(first, count):
+            width = count * BLK
+            hq = work3.tile([P, 2 * width], U32, name="hq", align_bytes=64)
+            hs = work3.tile([P, 2 * width], U8, name="hs", align_bytes=64)
+            for c in range(2):
+                cols = slice(c * width, (c + 1) * width)
+                nc.vector.quantize_mx(out=hq[:, cols].bitcast(FP8X4), scales=hs[:, cols], in_=h_part(c, first, count))
+            return hq, hs
+
+        def score_passes(o, t, hq, hs, width):
+            m = slice(t * P, (t + 1) * P)
+            nc.tensor.matmul_mx(out=o, lhsT=nr_w[:, m].bitcast(FP8X4), lhsT_scale=nr_s[:, m],
+                                rhs=hq[:, 0:width].bitcast(FP8X4), rhs_scale=hs[:, 0:width], start=True, stop=False)
+            nc.tensor.matmul_mx(out=o, lhsT=ni_w[:, 2 * t * P : 2 * (t + 1) * P].bitcast(FP4X4), lhsT_scale=ni_s[:, m],
+                                rhs=hq[:, width : 2 * width].bitcast(FP8X4), rhs_scale=hs[:, width : 2 * width],
+                                start=False, stop=True)
+
+        def score_group(g):
+            width = GROUP * BLK
+            hq, hs = quantise(g % 2, GROUP)
             for t in range(N // P):
-                m = slice(t * P, (t + 1) * P)
-                o = y_ps[:, t * BLK : (t + 1) * BLK]
-                nc.tensor.matmul_mx(out=o, lhsT=nr_w[:, m].bitcast(FP8X4), lhsT_scale=nr_s[:, m],
-                                    rhs=hq[:, 0:BLK].bitcast(FP8X4), rhs_scale=hs[:, 0:BLK], start=True, stop=False)
-                nc.tensor.matmul_mx(out=o, lhsT=ni_w[:, 2 * t * P : 2 * (t + 1) * P].bitcast(FP4X4), lhsT_scale=ni_s[:, m],
-                                    rhs=hq[:, BLK : 2 * BLK].bitcast(FP8X4), rhs_scale=hs[:, BLK : 2 * BLK],
-                                    start=False, stop=True)
-            y = work3.tile([P, N // P, BLK], F32, name="y")
-            nc.scalar.copy(out=y[:].rearrange("p t n -> p (t n)"), in_=y_ps[:])
-            nc.sync.dma_start(out=out_v[:, :, k * BLK : (k + 1) * BLK], in_=y[:])
+                y_ps = psum3.tile([P, width], F32, name="y_ps", tag="hy")
+                score_passes(y_ps[:], t, hq, hs, width)
+                y = work4.tile([P, width], F32, name="y")
+                nc.scalar.copy(out=y[:], in_=y_ps[:])
+                nc.sync.dma_start(out=out[t * P : (t + 1) * P, g * width : (g + 1) * width], in_=y[:])
 
+        def score_block(k):
+            hq, hs = quantise(h_slot(k), 1)
+            y_ps = psum3.tile([P, PACK * BLK], F32, name="y_ps", tag="hy")
+            for t in range(N // P):
+                score_passes(y_ps[:, t * BLK : (t + 1) * BLK], t, hq, hs, BLK)
+            y = work4.tile([P, N // P * BLK], F32, name="y")
+            nc.scalar.copy(out=y[:], in_=y_ps[:])
+            nc.sync.dma_start(out=out_v[:, :, tokens(k) : tokens(k) + BLK], in_=y[:].rearrange("p (t n) -> p t n", n=BLK))
+
+        for k in range(LEAD):
+            relation(k)
+        entity(0)
         for k in range(NBLK):
-            st = products(k)
-            if k < NBLK - 1:
-                combine(k, *st)
-            if k >= LAG:
-                score(k - LAG)
-            if k == NBLK - 1:
-                combine(k, *st)
-            if k % 4 == 1 and k // 4 + 1 < J // SLICE:
-                gather1(k // 4 + 1)
-        for k in range(NBLK - LAG, NBLK):
-            score(k)
+            if k + 1 < NBLK:
+                entity(k + 1)
+            products(k)
+            if k % GROUP == 1 and k > GROUP:
+                score_group(k // GROUP - 1)
+            if k == NBLK - 2:
+                combine(k)
+                score_block(k - 2)
+            elif k == NBLK - 1:
+                score_block(k - 2)
+                combine(k)
+            else:
+                combine(k)
+            if k + LEAD < NBLK:
+                relation(k + LEAD)
+        for k in range(NBLK - 2, NBLK):
+            score_block(k)

@@ -114,9 +114,9 @@ def tile_list_ckg_none_kernel(
         load_w("rr0")
         nc.sync.dma_start(list2[:], offs2)
         load_w("rr1")
-        for q in range(4):
-            nc.sync.dma_start(out=t2_scales[32 * q : 32 * q + 8, :].bitcast(I32),
-                              in_=tab2_scales[:, 4 * q : 4 * q + 4, :].bitcast(I32))
+        rows2 = tab2_scales.rearrange("a (q r) t -> r q a t", r=4)
+        for r in range(4):
+            nc.sync.dma_start(out=t2_scales[r : P : 16, :].bitcast(I32), in_=rows2[r].bitcast(I32))
         load_words(t2_words, tab2_words)
         load_w("ri0")
         load_w("ri1")
@@ -140,7 +140,7 @@ def tile_list_ckg_none_kernel(
         cast_w("rr0")
         cast_w("rr1")
         nc.vector.tensor_copy(r_scales0[:], t2_scales[:].indirect(list2[:]))
-        nc.sync.dma_start(out=r_scales1[0:100, :].bitcast(I32), in_=r_scales0[4:104, :].bitcast(I32))
+        nc.sync.dma_start(out=r_scales1[0:112, :].bitcast(I32), in_=r_scales0[16:128, :].bitcast(I32))
         load_w("er")
         load_words(t1_words, tab_words)
         quant_w("rr0")
@@ -217,7 +217,7 @@ def tile_list_ckg_none_kernel(
             return bank[:].rearrange("p (n t) -> p n t", t=PACK) if MODES[k] == "T" else inter(bank)
 
         def relation(k):
-            c_at = (0, 1, 2, 10, 11, 8, 9, 3, 6, 7)[k % 10] * 4096
+            c_at = (10, 11, 8, 9, 0, 1, 2, 3, 6, 7)[k % 10] * 4096
             d_at = c_at + 2048
             c_ps = psum1.tile([P, R], F32, name="c_ps")
             d_ps = psum1.tile([P, R], F32, name="d_ps")

@@ -24,7 +24,7 @@ NBLK = J // BLK
 SLICE = 512
 LEAD = 3
 GROUP = 4
-MODES = "TGGGTGGGTGGGTGTV"
+MODES = "VGGGVGGGVGGGVGTV"
 
 
 def tile_list_ckg_none_kernel(
@@ -308,6 +308,8 @@ def tile_list_ckg_none_kernel(
             if k + 1 < NBLK:
                 entity(k + 1)
             products(k)
+            if k % GROUP == 1:
+                combine(k - 1)
             if k % GROUP == 1 and k > GROUP:
                 score_group(k // GROUP - 1)
             if k == NBLK - 2:
@@ -316,7 +318,7 @@ def tile_list_ckg_none_kernel(
             elif k == NBLK - 1:
                 score_block(k - 2)
                 combine(k)
-            else:
+            elif k % GROUP != 0:
                 combine(k)
             if k + LEAD < NBLK:
                 relation(k + LEAD)

@@ -16,6 +16,7 @@ FP8X4 = mybir.dt.float8_e4m3fn_x4
 FP4X4 = mybir.dt.float4_e2m1fn_x4
 MULT = mybir.AluOpType.mult
 ADD = mybir.AluOpType.add
+SUB = mybir.AluOpType.subtract
 
 P = 128
 PACK = 4
@@ -216,18 +217,19 @@ def tile_list_ckg_none_kernel(
         def view(bank, k):
             return bank[:].rearrange("p (n t) -> p n t", t=PACK) if MODES[k] == "T" else inter(bank)
 
+        def twice(ap):
+            return ap.unsqueeze(1).to_broadcast([P, 2, BLK, PACK])
+
         def relation(k):
             c_at = (10, 11, 8, 9, 0, 1, 2, 3, 6, 7)[k % 10] * 4096
-            d_at = c_at + 2048
             c_ps = psum1.tile([P, R], F32, name="c_ps")
             d_ps = psum1.tile([P, R], F32, name="d_ps")
-            c_sb = stage.tile([P, BLK, PACK], F32, name="c_sb%d" % k, align_bytes=64, offset=c_at)
-            d_sb = stage.tile([P, BLK, PACK], F32, name="d_sb%d" % k, align_bytes=64, offset=d_at)
+            cd_sb = stage.tile([P, 2, BLK, PACK], F32, name="cd_sb%d" % k, align_bytes=64, offset=c_at)
             project(c_ps, r_passes("rr", k), k)
-            nc.scalar.copy(out=c_sb[:], in_=view(c_ps, k))
+            nc.scalar.copy(out=cd_sb[:, 0], in_=view(c_ps, k))
             project(d_ps, r_passes("ri", k), k)
-            nc.scalar.copy(out=d_sb[:], in_=view(d_ps, k))
-            cd[k] = (c_sb, d_sb)
+            nc.scalar.copy(out=cd_sb[:, 1], in_=view(d_ps, k))
+            cd[k] = cd_sb
 
         def entity(k):
             a_ps = psum3.tile([P, R], F32, name="a_ps", tag="ab")
@@ -238,13 +240,15 @@ def tile_list_ckg_none_kernel(
 
         def products(k):
             a_ps, b_ps = ab[k]
-            c_sb, d_sb = cd[k]
+            cd_sb = cd[k]
             pa = work3.tile([P, 2, BLK, PACK], F32, name="pa", align_bytes=64)
             pb = work3.tile([P, 2, BLK, PACK], F32, name="pb", align_bytes=64)
-            nc.vector.tensor_tensor(pa[:, 0], view(a_ps, k), c_sb[:], MULT)
-            nc.vector.tensor_tensor(pa[:, 1], view(a_ps, k), d_sb[:], MULT)
-            nc.vector.scalar_tensor_tensor(pb[:, 0], view(b_ps, k), -1.0, d_sb[:], MULT, MULT)
-            nc.vector.tensor_tensor(pb[:, 1], view(b_ps, k), c_sb[:], MULT)
+            nc.vector.tensor_tensor(pa[:], cd_sb[:], twice(view(a_ps, k)), MULT)
+            if MODES[k] == "G":
+                nc.vector.tensor_tensor(pb[:], cd_sb[:], twice(view(b_ps, k)), MULT)
+            else:
+                nc.vector.scalar_tensor_tensor(pb[:, 0], cd_sb[:, 1], -1.0, view(b_ps, k), MULT, MULT)
+                nc.vector.tensor_tensor(pb[:, 1], cd_sb[:, 0], view(b_ps, k), MULT)
             prods[k] = (pa, pb)
 
         def combine(k):
@@ -260,10 +264,12 @@ def tile_list_ckg_none_kernel(
                         nc.tensor.matmul(o, lhsT=fa[:, cols], rhs=ident[:], is_transpose=True, start=True, stop=False)
                         nc.tensor.matmul(o, lhsT=fb[:, cols], rhs=ident[:], is_transpose=True, start=False, stop=True)
                     nc.scalar.copy(out=h_part(c, h_slot(k), 1).rearrange("p (n t) -> p n t", t=PACK), in_=inter(h_ps))
+            elif MODES[k] == "G":
+                nc.gpsimd.tensor_tensor(h_part(0, h_slot(k), 1), fa[:, 0:R], fb[:, R : 2 * R], SUB)
+                nc.gpsimd.tensor_tensor(h_part(1, h_slot(k), 1), fa[:, R : 2 * R], fb[:, 0:R], ADD)
             else:
-                eng = nc.vector if MODES[k] == "V" else nc.gpsimd
                 h = h_both[:].rearrange("p (c s r) -> p c s r", c=2, r=R)[:, :, h_slot(k), :]
-                eng.tensor_tensor(h, fa.rearrange("p (c r) -> p c r", c=2), fb.rearrange("p (c r) -> p c r", c=2), ADD)
+                nc.vector.tensor_tensor(h, fa.rearrange("p (c r) -> p c r", c=2), fb.rearrange("p (c r) -> p c r", c=2), ADD)
 
         def quantise(first, count):
             width = count * BLK

@@ -16,7 +16,6 @@ FP8X4 = mybir.dt.float8_e4m3fn_x4
 FP4X4 = mybir.dt.float4_e2m1fn_x4
 MULT = mybir.AluOpType.mult
 ADD = mybir.AluOpType.add
-SUB = mybir.AluOpType.subtract
 
 P = 128
 PACK = 4
@@ -25,7 +24,7 @@ NBLK = J // BLK
 SLICE = 512
 LEAD = 3
 GROUP = 4
-MODES = "VGGGVGGGVGGGVGTV"
+MODES = "GGGGGGGGGGGGGGTV"
 
 
 def tile_list_ckg_none_kernel(
@@ -46,6 +45,7 @@ def tile_list_ckg_none_kernel(
         ident = keep.tile([P, P], F32, name="ident", align_bytes=64)
         t2_words = keep.tile([P, T], I32, name="t2_words", align_bytes=64)
         t1_scales = keep.tile([P, T], U8, name="t1_scales", align_bytes=64)
+        e_picked = keep.tile([P, J], U8, name="e_picked", align_bytes=64)
         e_scales = keep.tile([P, J], U8, name="e_scales", align_bytes=64)
         r_words = keep.tile([P, 2, 2 * J], U8, name="r_words", align_bytes=64)
         r_scales0 = keep.tile([P, J], U8, name="r_scales0", align_bytes=64)
@@ -93,6 +93,11 @@ def tile_list_ckg_none_kernel(
         def load_w(n):
             nc.sync.dma_start(out=raw[n], in_=src[n].rearrange("(p j) r -> p j r", j=PACK))
 
+        def load_rows(n, cuts):
+            rows = src[n].rearrange("(p j) r -> p j r", j=PACK)
+            for j0, j1 in zip(cuts, cuts[1:]):
+                nc.sync.dma_start(out=raw[n][:, j0:j1, :], in_=rows[:, j0:j1, :])
+
         def cast_w(n):
             nc.scalar.copy(
                 out=wb[n][:].rearrange("p (t m j) -> p m j t", t=PACK, j=PACK),
@@ -102,19 +107,16 @@ def tile_list_ckg_none_kernel(
         def quant_w(n):
             nc.vector.quantize_mx(out=wq[n][:].bitcast(FP8X4), scales=ws[n][:], in_=wb[n][:])
 
-        for plane in (t2_scales, r_scales1):
+        for plane in (t2_scales, r_scales1, e_scales):
             nc.vector.memset(plane[:].bitcast(I32), 0)
         make_identity(nc, ident[:])
 
         nc.sync.dma_start(list1[:], offs)
-        for q in range(4):
-            nc.sync.dma_start(
-                out=t1_scales[32 * q : 32 * q + 32, :].bitcast(I32),
-                in_=tab_scales[0][4 * q : 4 * q + 4, :].bitcast(I32).partition_broadcast(8),
-            )
-        load_w("rr0")
+        nc.sync.dma_start(out=t1_scales[:].bitcast(I32),
+                          in_=tab_scales[0].bitcast(I32).unsqueeze(1).to_broadcast([16, 8, T // 4]))
+        load_rows("rr0", (0, 2, 4))
         nc.sync.dma_start(list2[:], offs2)
-        load_w("rr1")
+        load_rows("rr1", (0, 2, 3, 4))
         rows2 = tab2_scales.rearrange("a (q r) t -> r q a t", r=4)
         for r in range(4):
             nc.sync.dma_start(out=t2_scales[r : P : 16, :].bitcast(I32), in_=rows2[r].bitcast(I32))
@@ -137,7 +139,9 @@ def tile_list_ckg_none_kernel(
             cols = slice(s * SLICE, (s + 1) * SLICE)
             nc.vector.tensor_copy(r16[:, :, cols], r_pairs[s][:].bitcast(U16).rearrange("p (n d) -> p d n", d=2))
 
-        nc.vector.tensor_copy(e_scales[:], t1_scales[:].indirect(list1[:]))
+        nc.vector.tensor_copy(e_picked[:], t1_scales[:].indirect(list1[:]))
+        for q in range(4):
+            nc.gpsimd.dma_start(out=e_scales[32 * q : 32 * q + 4, :].bitcast(I32), in_=e_picked[32 * q : 32 * q + 32 : 8, :].bitcast(I32))
         cast_w("rr0")
         cast_w("rr1")
         nc.vector.tensor_copy(r_scales0[:], t2_scales[:].indirect(list2[:]))
@@ -145,7 +149,9 @@ def tile_list_ckg_none_kernel(
         load_w("er")
         load_words(t1_words, tab_words)
         quant_w("rr0")
-        load_w("ei")
+        for half in range(2):
+            cols = slice(half * R // 2, (half + 1) * R // 2)
+            nc.sync.dma_start(out=raw["ei"][:, :, cols], in_=src["ei"].rearrange("(p j) r -> p j r", j=PACK)[:, :, cols])
         quant_w("rr1")
         for plane in (nr_s, ni_s):
             nc.gpsimd.memset(plane[:].bitcast(I32), 0)
@@ -169,7 +175,12 @@ def tile_list_ckg_none_kernel(
         part2(3)
         for s in range(J // SLICE):
             gather1(s)
-        cast_w("ei")
+        for half in range(2):
+            ms = slice(half * P // 2, (half + 1) * P // 2)
+            nc.scalar.copy(
+                out=wb["ei"][:].rearrange("p (t m j) -> p m j t", t=PACK, j=PACK)[:, ms],
+                in_=raw["ei"].rearrange("p j (m t) -> p m j t", t=PACK)[:, ms],
+            )
         quant_w("ei")
 
         out_v = out.rearrange("(t p) j -> p t j", p=P)
@@ -244,11 +255,8 @@ def tile_list_ckg_none_kernel(
             pa = work3.tile([P, 2, BLK, PACK], F32, name="pa", align_bytes=64)
             pb = work3.tile([P, 2, BLK, PACK], F32, name="pb", align_bytes=64)
             nc.vector.tensor_tensor(pa[:], cd_sb[:], twice(view(a_ps, k)), MULT)
-            if MODES[k] == "G":
-                nc.vector.tensor_tensor(pb[:], cd_sb[:], twice(view(b_ps, k)), MULT)
-            else:
-                nc.vector.scalar_tensor_tensor(pb[:, 0], cd_sb[:, 1], -1.0, view(b_ps, k), MULT, MULT)
-                nc.vector.tensor_tensor(pb[:, 1], cd_sb[:, 0], view(b_ps, k), MULT)
+            nc.vector.scalar_tensor_tensor(pb[:, 0], cd_sb[:, 1], -1.0, view(b_ps, k), MULT, MULT)
+            nc.vector.tensor_tensor(pb[:, 1], cd_sb[:, 0], view(b_ps, k), MULT)
             prods[k] = (pa, pb)
 
         def combine(k):
@@ -264,12 +272,10 @@ def tile_list_ckg_none_kernel(
                         nc.tensor.matmul(o, lhsT=fa[:, cols], rhs=ident[:], is_transpose=True, start=True, stop=False)
                         nc.tensor.matmul(o, lhsT=fb[:, cols], rhs=ident[:], is_transpose=True, start=False, stop=True)
                     nc.scalar.copy(out=h_part(c, h_slot(k), 1).rearrange("p (n t) -> p n t", t=PACK), in_=inter(h_ps))
-            elif MODES[k] == "G":
-                nc.gpsimd.tensor_tensor(h_part(0, h_slot(k), 1), fa[:, 0:R], fb[:, R : 2 * R], SUB)
-                nc.gpsimd.tensor_tensor(h_part(1, h_slot(k), 1), fa[:, R : 2 * R], fb[:, 0:R], ADD)
             else:
+                eng = nc.vector if MODES[k] == "V" else nc.gpsimd
                 h = h_both[:].rearrange("p (c s r) -> p c s r", c=2, r=R)[:, :, h_slot(k), :]
-                nc.vector.tensor_tensor(h, fa.rearrange("p (c r) -> p c r", c=2), fb.rearrange("p (c r) -> p c r", c=2), ADD)
+                eng.tensor_tensor(h, fa.rearrange("p (c r) -> p c r", c=2), fb.rearrange("p (c r) -> p c r", c=2), ADD)
 
         def quantise(first, count):
             width = count * BLK
@@ -307,6 +313,17 @@ def tile_list_ckg_none_kernel(
             nc.scalar.copy(out=y[:], in_=y_ps[:])
             nc.sync.dma_start(out=out_v[:, :, tokens(k) : tokens(k) + BLK], in_=y[:].rearrange("p (t n) -> p t n", n=BLK))
 
+        def score_last(k):
+            hq, hs = quantise(h_slot(k), 1)
+            for half, copy in enumerate((nc.scalar.copy, nc.vector.tensor_copy)):
+                y_ps = psum3.tile([P, 2 * BLK], F32, name="y_ps", tag="hy")
+                for t in range(2):
+                    score_passes(y_ps[:, t * BLK : (t + 1) * BLK], 2 * half + t, hq, hs, BLK)
+                y = work4.tile([P, 2 * BLK], F32, name="y")
+                copy(y[:], y_ps[:])
+                nc.sync.dma_start(out=out_v[:, 2 * half : 2 * half + 2, tokens(k) : tokens(k) + BLK],
+                                  in_=y[:].rearrange("p (t n) -> p t n", n=BLK))
+
         for k in range(LEAD):
             relation(k)
         entity(0)
@@ -314,19 +331,16 @@ def tile_list_ckg_none_kernel(
             if k + 1 < NBLK:
                 entity(k + 1)
             products(k)
-            if k % GROUP == 1:
+            if k % GROUP == 1 and MODES[k - 1] == "V":
                 combine(k - 1)
             if k % GROUP == 1 and k > GROUP:
                 score_group(k // GROUP - 1)
+            if k % GROUP != 0 or MODES[k] != "V":
+                combine(k)
             if k == NBLK - 2:
-                combine(k)
                 score_block(k - 2)
-            elif k == NBLK - 1:
-                score_block(k - 2)
-                combine(k)
-            elif k % GROUP != 0:
-                combine(k)
+                score_block(k - 1)
             if k + LEAD < NBLK:
                 relation(k + LEAD)
-        for k in range(NBLK - 2, NBLK):
-            score_block(k)
+        score_block(NBLK - 2)
+        score_last(NBLK - 1)

@@ -24,7 +24,7 @@ NBLK = J // BLK
 SLICE = 512
 LEAD = 3
 GROUP = 4
-MODES = "GGGGGGGGGGGGGGTV"
+MODES = "GGGGHGGGHGGGHGTV"
 
 
 def tile_list_ckg_none_kernel(
@@ -137,7 +137,8 @@ def tile_list_ckg_none_kernel(
 
         def part2(s):
             cols = slice(s * SLICE, (s + 1) * SLICE)
-            nc.vector.tensor_copy(r16[:, :, cols], r_pairs[s][:].bitcast(U16).rearrange("p (n d) -> p d n", d=2))
+            nc.vector.tensor_copy(r16[:, :, cols].rearrange("p d (c i) -> p c d i", i=8),
+                                  r_pairs[s][:].bitcast(U16).rearrange("p (c i d) -> p c d i", i=8, d=2))
 
         nc.vector.tensor_copy(e_picked[:], t1_scales[:].indirect(list1[:]))
         for q in range(4):
@@ -145,7 +146,8 @@ def tile_list_ckg_none_kernel(
         cast_w("rr0")
         cast_w("rr1")
         nc.vector.tensor_copy(r_scales0[:], t2_scales[:].indirect(list2[:]))
-        nc.sync.dma_start(out=r_scales1[0:112, :].bitcast(I32), in_=r_scales0[16:128, :].bitcast(I32))
+        for q in range(4):
+            nc.sync.dma_start(out=r_scales1[32 * q : 32 * q + 4, :].bitcast(I32), in_=r_scales0[32 * q + 16 : 32 * q + 20, :].bitcast(I32))
         load_w("er")
         load_words(t1_words, tab_words)
         quant_w("rr0")
@@ -277,6 +279,10 @@ def tile_list_ckg_none_kernel(
                 h = h_both[:].rearrange("p (c s r) -> p c s r", c=2, r=R)[:, :, h_slot(k), :]
                 eng.tensor_tensor(h, fa.rearrange("p (c r) -> p c r", c=2), fb.rearrange("p (c r) -> p c r", c=2), ADD)
 
+        def add_half(eng, c, k):
+            pa, pb = prods[k]
+            eng.tensor_tensor(h_part(c, h_slot(k), 1), pa[:, c].rearrange("p n t -> p (n t)"), pb[:, c].rearrange("p n t -> p (n t)"), ADD)
+
         def quantise(first, count):
             width = count * BLK
             hq = work3.tile([P, 2 * width], U32, name="hq", align_bytes=64)
@@ -331,11 +337,13 @@ def tile_list_ckg_none_kernel(
             if k + 1 < NBLK:
                 entity(k + 1)
             products(k)
-            if k % GROUP == 1 and MODES[k - 1] == "V":
-                combine(k - 1)
+            if k > 0 and MODES[k - 1] == "H":
+                add_half(nc.vector, 0, k - 1)
             if k % GROUP == 1 and k > GROUP:
                 score_group(k // GROUP - 1)
-            if k % GROUP != 0 or MODES[k] != "V":
+            if MODES[k] == "H":
+                add_half(nc.gpsimd, 1, k)
+            else:
                 combine(k)
             if k == NBLK - 2:
                 score_block(k - 2)

@@ -107,19 +107,19 @@ def tile_list_ckg_none_kernel(
         def quant_w(n):
             nc.vector.quantize_mx(out=wq[n][:].bitcast(FP8X4), scales=ws[n][:], in_=wb[n][:])
 
-        for plane in (t2_scales, r_scales1, e_scales):
+        for plane in (t2_scales, t1_scales, r_scales1, e_scales):
             nc.vector.memset(plane[:].bitcast(I32), 0)
         make_identity(nc, ident[:])
 
-        nc.sync.dma_start(list1[:], offs)
-        nc.sync.dma_start(out=t1_scales[:].bitcast(I32),
-                          in_=tab_scales[0].bitcast(I32).unsqueeze(1).to_broadcast([16, 8, T // 4]))
-        load_rows("rr0", (0, 2, 4))
         nc.sync.dma_start(list2[:], offs2)
-        load_rows("rr1", (0, 2, 3, 4))
+        nc.sync.dma_start(list1[:], offs)
+        load_rows("rr0", (0, 1, 2, 3, 4))
+        load_rows("rr1", (0, 1, 2))
         rows2 = tab2_scales.rearrange("a (q r) t -> r q a t", r=4)
         for r in range(4):
             nc.sync.dma_start(out=t2_scales[r : P : 16, :].bitcast(I32), in_=rows2[r].bitcast(I32))
+        nc.sync.dma_start(out=t1_scales[0:P:8, :].bitcast(I32), in_=tab_scales[0].bitcast(I32))
+        load_rows("rr1", (2, 4))
         load_words(t2_words, tab2_words)
         load_w("ri0")
         load_w("ri1")
@@ -140,20 +140,18 @@ def tile_list_ckg_none_kernel(
             nc.vector.tensor_copy(r16[:, :, cols].rearrange("p d (c i) -> p c d i", i=8),
                                   r_pairs[s][:].bitcast(U16).rearrange("p (c i d) -> p c d i", i=8, d=2))
 
-        nc.vector.tensor_copy(e_picked[:], t1_scales[:].indirect(list1[:]))
-        for q in range(4):
-            nc.gpsimd.dma_start(out=e_scales[32 * q : 32 * q + 4, :].bitcast(I32), in_=e_picked[32 * q : 32 * q + 32 : 8, :].bitcast(I32))
         cast_w("rr0")
         cast_w("rr1")
         nc.vector.tensor_copy(r_scales0[:], t2_scales[:].indirect(list2[:]))
         for q in range(4):
             nc.sync.dma_start(out=r_scales1[32 * q : 32 * q + 4, :].bitcast(I32), in_=r_scales0[32 * q + 16 : 32 * q + 20, :].bitcast(I32))
+        nc.vector.tensor_copy(e_picked[:], t1_scales[:].indirect(list1[:]))
+        for q in range(4):
+            nc.gpsimd.dma_start(out=e_scales[32 * q : 32 * q + 4, :].bitcast(I32), in_=e_picked[32 * q : 32 * q + 32 : 8, :].bitcast(I32))
         load_w("er")
         load_words(t1_words, tab_words)
         quant_w("rr0")
-        for half in range(2):
-            cols = slice(half * R // 2, (half + 1) * R // 2)
-            nc.sync.dma_start(out=raw["ei"][:, :, cols], in_=src["ei"].rearrange("(p j) r -> p j r", j=PACK)[:, :, cols])
+        load_w("ei")
         quant_w("rr1")
         for plane in (nr_s, ni_s):
             nc.gpsimd.memset(plane[:].bitcast(I32), 0)
@@ -177,12 +175,7 @@ def tile_list_ckg_none_kernel(
         part2(3)
         for s in range(J // SLICE):
             gather1(s)
-        for half in range(2):
-            ms = slice(half * P // 2, (half + 1) * P // 2)
-            nc.scalar.copy(
-                out=wb["ei"][:].rearrange("p (t m j) -> p m j t", t=PACK, j=PACK)[:, ms],
-                in_=raw["ei"].rearrange("p j (m t) -> p m j t", t=PACK)[:, ms],
-            )
+        cast_w("ei")
         quant_w("ei")
 
         out_v = out.rearrange("(t p) j -> p t j", p=P)

@@ -22,7 +22,7 @@ PACK = 4
 BLK = 128
 NBLK = J // BLK
 SLICE = 512
-LEAD = 3
+LEAD = 6
 GROUP = 4
 MODES = "GGGGHGGGHGGGHGTV"
 
@@ -48,9 +48,8 @@ def tile_list_ckg_none_kernel(
         e_picked = keep.tile([P, J], U8, name="e_picked", align_bytes=64)
         e_scales = keep.tile([P, J], U8, name="e_scales", align_bytes=64)
         r_words = keep.tile([P, 2, 2 * J], U8, name="r_words", align_bytes=64)
-        r_scales0 = keep.tile([P, J], U8, name="r_scales0", align_bytes=64)
-        r_scales1 = keep.tile([P, J], U8, name="r_scales1", align_bytes=64)
-        r_scales = [r_scales0, r_scales1]
+        r_picked = keep.tile([P, J], U8, name="r_picked", align_bytes=64)
+        r_planes = keep.tile([P, 2 * J], U8, name="r_planes", align_bytes=64)
 
         names = ["ri1", "ri0", "rr1", "rr0", "er", "ei"]
         src = {"er": wer, "ei": wei, "rr0": wrr[0:512, :], "rr1": wrr[512:1024, :],
@@ -84,11 +83,10 @@ def tile_list_ckg_none_kernel(
             for q in range(4):
                 nc.sync.dma_start(out=plane[32 * q : 32 * q + 4, :].bitcast(I32), in_=rows[4 * q : 4 * q + 4, :].bitcast(I32))
 
-        def load_words(tile, words):
+        def load_words(tile, words, cuts):
             rows = words[0].rearrange("p t i -> p (t i)").bitcast(I32)
-            for half in range(2):
-                cols = slice(half * T // 2, (half + 1) * T // 2)
-                nc.sync.dma_start(out=tile[:, cols], in_=rows[:, cols])
+            for c0, c1 in zip(cuts, cuts[1:]):
+                nc.sync.dma_start(out=tile[:, c0:c1], in_=rows[:, c0:c1])
 
         def load_w(n):
             nc.sync.dma_start(out=raw[n], in_=src[n].rearrange("(p j) r -> p j r", j=PACK))
@@ -107,22 +105,20 @@ def tile_list_ckg_none_kernel(
         def quant_w(n):
             nc.vector.quantize_mx(out=wq[n][:].bitcast(FP8X4), scales=ws[n][:], in_=wb[n][:])
 
-        for plane in (t2_scales, t1_scales, r_scales1, e_scales):
-            nc.vector.memset(plane[:].bitcast(I32), 0)
-        make_identity(nc, ident[:])
-
+        nc.vector.memset(t1_scales[:].bitcast(I32), 0)
         nc.sync.dma_start(list2[:], offs2)
+        nc.sync.dma_start(out=t2_scales[96:P, :].bitcast(I32), in_=tab2_scales.rearrange("a q t -> (a q) t").bitcast(I32))
+        nc.vector.memset(t2_scales[0:96, :].bitcast(I32), 0)
+        for plane in (r_planes, e_scales):
+            nc.gpsimd.memset(plane[:].bitcast(I32), 0)
+        make_identity(nc, ident[:])
         nc.sync.dma_start(list1[:], offs)
-        load_rows("rr0", (0, 1, 2, 3, 4))
-        load_rows("rr1", (0, 1, 2))
-        rows2 = tab2_scales.rearrange("a (q r) t -> r q a t", r=4)
-        for r in range(4):
-            nc.sync.dma_start(out=t2_scales[r : P : 16, :].bitcast(I32), in_=rows2[r].bitcast(I32))
+        load_rows("rr0", (0, 2, 4))
+        load_rows("rr1", (0, 2, 4))
+        load_words(t2_words, tab2_words, (0, T // 4))
         nc.sync.dma_start(out=t1_scales[0:P:8, :].bitcast(I32), in_=tab_scales[0].bitcast(I32))
-        load_rows("rr1", (2, 4))
-        load_words(t2_words, tab2_words)
+        load_words(t2_words, tab2_words, (T // 4, T // 2, T))
         load_w("ri0")
-        load_w("ri1")
 
         r16 = r_words[:].bitcast(U16)
 
@@ -142,14 +138,22 @@ def tile_list_ckg_none_kernel(
 
         cast_w("rr0")
         cast_w("rr1")
-        nc.vector.tensor_copy(r_scales0[:], t2_scales[:].indirect(list2[:]))
-        for q in range(4):
-            nc.sync.dma_start(out=r_scales1[32 * q : 32 * q + 4, :].bitcast(I32), in_=r_scales0[32 * q + 16 : 32 * q + 20, :].bitcast(I32))
+        nc.vector.tensor_copy(r_picked[:], t2_scales[:].indirect(list2[:]))
+
+        def move_plane(a):
+            for q in range(4):
+                row = 96 + 16 * a + 4 * q
+                nc.sync.dma_start(out=r_planes[32 * q : 32 * q + 4, a * J : (a + 1) * J].bitcast(I32),
+                                  in_=r_picked[row : row + 4, :].bitcast(I32))
+
+        move_plane(0)
+        load_w("ri1")
+        load_w("er")
+        move_plane(1)
         nc.vector.tensor_copy(e_picked[:], t1_scales[:].indirect(list1[:]))
         for q in range(4):
             nc.gpsimd.dma_start(out=e_scales[32 * q : 32 * q + 4, :].bitcast(I32), in_=e_picked[32 * q : 32 * q + 32 : 8, :].bitcast(I32))
-        load_w("er")
-        load_words(t1_words, tab_words)
+        load_words(t1_words, tab_words, (0, T // 2, T))
         quant_w("rr0")
         load_w("ei")
         quant_w("rr1")
@@ -213,8 +217,7 @@ def tile_list_ckg_none_kernel(
             return [(n, e_words[:, tok].bitcast(FP8X4), e_scales[:, tok])]
 
         def r_passes(n, k):
-            tok = slice(tokens(k), tokens(k) + BLK)
-            return [(n + str(a), r_words[:, a, 2 * tokens(k) : 2 * (tokens(k) + BLK)].bitcast(FP4X4), r_scales[a][:, tok])
+            return [(n + str(a), r_words[:, a, 2 * tokens(k) : 2 * (tokens(k) + BLK)].bitcast(FP4X4), r_planes[:, a * J + tokens(k) : a * J + tokens(k) + BLK])
                     for a in range(2)]
 
         def inter(bank):
@@ -227,7 +230,7 @@ def tile_list_ckg_none_kernel(
             return ap.unsqueeze(1).to_broadcast([P, 2, BLK, PACK])
 
         def relation(k):
-            c_at = (10, 11, 8, 9, 0, 1, 2, 3, 6, 7)[k % 10] * 4096
+            c_at = (10, 11, 8, 9, 0, 1, 2, 3, 4, 5, 6, 7)[k % 12] * 4096
             c_ps = psum1.tile([P, R], F32, name="c_ps")
             d_ps = psum1.tile([P, R], F32, name="d_ps")
             cd_sb = stage.tile([P, 2, BLK, PACK], F32, name="cd_sb%d" % k, align_bytes=64, offset=c_at)
@@ -323,12 +326,12 @@ def tile_list_ckg_none_kernel(
                 nc.sync.dma_start(out=out_v[:, 2 * half : 2 * half + 2, tokens(k) : tokens(k) + BLK],
                                   in_=y[:].rearrange("p (t n) -> p t n", n=BLK))
 
+        for k in range(NBLK):
+            entity(k)
         for k in range(LEAD):
             relation(k)
-        entity(0)
+        steps = [k for k in range(NBLK) if k % GROUP != 1][: NBLK - LEAD]
         for k in range(NBLK):
-            if k + 1 < NBLK:
-                entity(k + 1)
             products(k)
             if k > 0 and MODES[k - 1] == "H":
                 add_half(nc.vector, 0, k - 1)
@@ -341,7 +344,7 @@ def tile_list_ckg_none_kernel(
             if k == NBLK - 2:
                 score_block(k - 2)
                 score_block(k - 1)
-            if k + LEAD < NBLK:
-                relation(k + LEAD)
+            if k in steps:
+                relation(LEAD + steps.index(k))
         score_block(NBLK - 2)
         score_last(NBLK - 1)

@@ -37,32 +37,31 @@ def tile_list_ckg_none_kernel(
         stage = ctx.enter_context(tc.tile_pool(name="stage", bufs=1))
         work3 = ctx.enter_context(tc.tile_pool(name="work3", bufs=3))
         work4 = ctx.enter_context(tc.tile_pool(name="work4", bufs=4))
-        psum1 = ctx.enter_context(tc.psum_pool(name="psum1", bufs=1))
-        psum3 = ctx.enter_context(tc.psum_pool(name="psum3", bufs=3))
+        psum4 = ctx.enter_context(tc.psum_pool(name="psum4", bufs=4))
 
         list1 = keep.tile([P, J // 16], U16, name="list1")
         list2 = keep.tile([P, J // 16], U16, name="list2")
         ident = keep.tile([P, P], F32, name="ident", align_bytes=64)
         t2_words = keep.tile([P, T], I32, name="t2_words", align_bytes=64)
-        t1_scales = keep.tile([P, T], U8, name="t1_scales", align_bytes=64)
         e_picked = keep.tile([P, J], U8, name="e_picked", align_bytes=64)
         e_scales = keep.tile([P, J], U8, name="e_scales", align_bytes=64)
-        r_words = keep.tile([P, 2, 2 * J], U8, name="r_words", align_bytes=64)
         r_picked = keep.tile([P, J], U8, name="r_picked", align_bytes=64)
         r_planes = keep.tile([P, 2 * J], U8, name="r_planes", align_bytes=64)
 
-        names = ["ri1", "ri0", "rr1", "rr0", "er", "ei"]
+        names = ["ri0", "rr1", "rr0", "ei", "er", "ri1"]
         src = {"er": wer, "ei": wei, "rr0": wrr[0:512, :], "rr1": wrr[512:1024, :],
                "ri0": wri[0:512, :], "ri1": wri[512:1024, :]}
         RAW = 4 * PACK * R
-        raw = {n: stage.tile([P, PACK, R], F32, name="raw_" + n, align_bytes=64, offset=i * RAW)[:] for i, n in enumerate(names[:4])}
-        raw["ei"] = stage.tile([P, PACK, R], F32, name="raw_ei", align_bytes=64, offset=4 * RAW)[:]
-        raw["er"] = stage.tile([P, PACK, R], F32, name="raw_er", align_bytes=64, offset=5 * RAW)[:]
-        t2_scales = stage.tile([P, T], U8, name="t2_scales", align_bytes=64, offset=6 * RAW - 768)
-        t1_words = stage.tile([P, T], I32, name="t1_words", align_bytes=64, offset=6 * RAW + 5 * R)
-        late = 6 * RAW + 5 * R + 4 * T
-        wb = {n: keep.tile([P, PACK * R], BF16, name="wb_" + n, align_bytes=64) for n in ("er", "ei")}
-        wb["rr0"] = stage.tile([P, PACK * R], BF16, name="wb_rr0", align_bytes=64, offset=4 * RAW)
+        raw = {n: stage.tile([P, PACK, R], F32, name="raw_" + n, align_bytes=64, offset=i * RAW)[:] for i, n in enumerate(names)}
+        t2_scales = stage.tile([P, T], U8, name="t2_scales", align_bytes=64, offset=6 * RAW - T // 2)
+        t1_scales = stage.tile([P, T], U8, name="t1_scales", align_bytes=64, offset=4 * RAW)
+        t1_words = stage.tile([P, T], I32, name="t1_words", align_bytes=64, offset=6 * RAW)
+        late = 6 * RAW + 4 * T
+        last = late + 8 * N + 4 * J + 16 * R
+        wb = {n: stage.tile([P, PACK * R], BF16, name="wb_" + n, align_bytes=64, offset=last + i * 8 * R) for i, n in enumerate(("er", "ei"))}
+        r_words = [keep.tile([P, 2, 2 * SLICE], U8, name="r_words%d" % s, align_bytes=64) for s in range(3)]
+        r_words = r_words + [stage.tile([P, 2, 2 * SLICE], U8, name="r_words3", align_bytes=64, offset=last)]
+        wb["rr0"] = stage.tile([P, PACK * R], BF16, name="wb_rr0", align_bytes=64, offset=3 * RAW)
         wb["ri0"] = stage.tile([P, PACK * R], BF16, name="wb_ri0", align_bytes=64, offset=late + 8 * N + 4 * J)
         wb["ri1"] = stage.tile([P, PACK * R], BF16, name="wb_ri1", align_bytes=64, offset=late + 8 * N + 4 * J + 8 * R)
         e_words = stage.tile([P, J], U32, name="e_words", align_bytes=64, offset=late + 8 * N)
@@ -74,10 +73,8 @@ def tile_list_ckg_none_kernel(
         r_pairs = [keep.tile([P, SLICE], U32, name="pairs%d" % s, align_bytes=64) for s in range(2)]
         r_pairs = r_pairs + [stage.tile([P, SLICE], U32, name="pairs%d" % s, align_bytes=64, offset=late + 8 * N + 4 * J + 8 * R * (s - 2))
                              for s in (2, 3)]
-        wq = {n: keep.tile([P, R], U32, name="wq_" + n, align_bytes=64) for n in names if n != "rr0"}
-        wq["rr0"] = stage.tile([P, R], U32, name="wq_rr0", align_bytes=64, offset=6 * RAW)
-        ws = {n: keep.tile([P, R], U8, name="ws_" + n, align_bytes=64) for n in names if n != "rr1"}
-        ws["rr1"] = stage.tile([P, R], U8, name="ws_rr1", align_bytes=64, offset=6 * RAW + 4 * R)
+        wq = {n: keep.tile([P, R], U32, name="wq_" + n, align_bytes=64) for n in names}
+        ws = {n: keep.tile([P, R], U8, name="ws_" + n, align_bytes=64) for n in names}
 
         def load_plane(plane, rows):
             for q in range(4):
@@ -91,11 +88,6 @@ def tile_list_ckg_none_kernel(
         def load_w(n):
             nc.sync.dma_start(out=raw[n], in_=src[n].rearrange("(p j) r -> p j r", j=PACK))
 
-        def load_rows(n, cuts):
-            rows = src[n].rearrange("(p j) r -> p j r", j=PACK)
-            for j0, j1 in zip(cuts, cuts[1:]):
-                nc.sync.dma_start(out=raw[n][:, j0:j1, :], in_=rows[:, j0:j1, :])
-
         def cast_w(n):
             nc.scalar.copy(
                 out=wb[n][:].rearrange("p (t m j) -> p m j t", t=PACK, j=PACK),
@@ -105,22 +97,20 @@ def tile_list_ckg_none_kernel(
         def quant_w(n):
             nc.vector.quantize_mx(out=wq[n][:].bitcast(FP8X4), scales=ws[n][:], in_=wb[n][:])
 
-        nc.vector.memset(t1_scales[:].bitcast(I32), 0)
         nc.sync.dma_start(list2[:], offs2)
         nc.sync.dma_start(out=t2_scales[96:P, :].bitcast(I32), in_=tab2_scales.rearrange("a q t -> (a q) t").bitcast(I32))
+        nc.sync.dma_start(list1[:], offs)
+        nc.sync.dma_start(out=t1_scales[112:P, :].bitcast(I32), in_=tab_scales[0].bitcast(I32))
         nc.vector.memset(t2_scales[0:96, :].bitcast(I32), 0)
+        nc.vector.memset(t1_scales[0:96, :].bitcast(I32), 0)
+        nc.vector.memset(t1_scales[96:112, :].bitcast(I32), 0)
         for plane in (r_planes, e_scales):
             nc.gpsimd.memset(plane[:].bitcast(I32), 0)
         make_identity(nc, ident[:])
-        nc.sync.dma_start(list1[:], offs)
-        load_rows("rr0", (0, 2, 4))
-        load_rows("rr1", (0, 2, 4))
-        load_words(t2_words, tab2_words, (0, T // 4))
-        nc.sync.dma_start(out=t1_scales[0:P:8, :].bitcast(I32), in_=tab_scales[0].bitcast(I32))
-        load_words(t2_words, tab2_words, (T // 4, T // 2, T))
+        load_w("rr0")
+        load_w("rr1")
+        load_words(t2_words, tab2_words, (0, T // 2, T))
         load_w("ri0")
-
-        r16 = r_words[:].bitcast(U16)
 
         def gather1(s):
             cols = slice(s * SLICE, (s + 1) * SLICE)
@@ -132,8 +122,7 @@ def tile_list_ckg_none_kernel(
                 r_pairs[s][:], t2_words[:].bitcast(U32).indirect(list2[:, s * SLICE // 16 : (s + 1) * SLICE // 16]))
 
         def part2(s):
-            cols = slice(s * SLICE, (s + 1) * SLICE)
-            nc.vector.tensor_copy(r16[:, :, cols].rearrange("p d (c i) -> p c d i", i=8),
+            nc.vector.tensor_copy(r_words[s][:].bitcast(U16).rearrange("p d (c i) -> p c d i", i=8),
                                   r_pairs[s][:].bitcast(U16).rearrange("p (c i d) -> p c d i", i=8, d=2))
 
         cast_w("rr0")
@@ -148,12 +137,13 @@ def tile_list_ckg_none_kernel(
 
         move_plane(0)
         load_w("ri1")
-        load_w("er")
+        load_words(t1_words, tab_words, (0, T // 2))
         move_plane(1)
+        load_words(t1_words, tab_words, (T // 2, T))
         nc.vector.tensor_copy(e_picked[:], t1_scales[:].indirect(list1[:]))
         for q in range(4):
-            nc.gpsimd.dma_start(out=e_scales[32 * q : 32 * q + 4, :].bitcast(I32), in_=e_picked[32 * q : 32 * q + 32 : 8, :].bitcast(I32))
-        load_words(t1_words, tab_words, (0, T // 2, T))
+            nc.gpsimd.dma_start(out=e_scales[32 * q : 32 * q + 4, :].bitcast(I32), in_=e_picked[112 + 4 * q : 116 + 4 * q, :].bitcast(I32))
+        load_w("er")
         quant_w("rr0")
         load_w("ei")
         quant_w("rr1")
@@ -174,11 +164,11 @@ def tile_list_ckg_none_kernel(
         gather2(2)
         gather2(3)
         part2(2)
+        for s in range(J // SLICE):
+            gather1(s)
         cast_w("er")
         quant_w("er")
         part2(3)
-        for s in range(J // SLICE):
-            gather1(s)
         cast_w("ei")
         quant_w("ei")
 
@@ -187,12 +177,12 @@ def tile_list_ckg_none_kernel(
         h_both = keep.tile([P, 2 * (GROUP + 1) * R], BF16, name="h_both", align_bytes=64)
 
         def h_slot(k):
-            g, i = divmod(k, GROUP)
+            g, i = divmod(min(k, NBLK - 2), GROUP)
             return i if i > 0 else GROUP * (g % 2)
 
         def tokens(k):
-            g = k // GROUP
-            return (g * GROUP + h_slot(k) - g % 2) * BLK
+            g, i = divmod(k, GROUP)
+            return (g * GROUP + (i - g % 2) % GROUP) * BLK
 
         def h_part(c, first, count):
             at = (c * (GROUP + 1) + first) * R
@@ -217,7 +207,7 @@ def tile_list_ckg_none_kernel(
             return [(n, e_words[:, tok].bitcast(FP8X4), e_scales[:, tok])]
 
         def r_passes(n, k):
-            return [(n + str(a), r_words[:, a, 2 * tokens(k) : 2 * (tokens(k) + BLK)].bitcast(FP4X4), r_planes[:, a * J + tokens(k) : a * J + tokens(k) + BLK])
+            return [(n + str(a), r_words[k // GROUP][:, a, 2 * (tokens(k) % SLICE) : 2 * (tokens(k) % SLICE + BLK)].bitcast(FP4X4), r_planes[:, a * J + tokens(k) : a * J + tokens(k) + BLK])
                     for a in range(2)]
 
         def inter(bank):
@@ -230,9 +220,9 @@ def tile_list_ckg_none_kernel(
             return ap.unsqueeze(1).to_broadcast([P, 2, BLK, PACK])
 
         def relation(k):
-            c_at = (10, 11, 8, 9, 0, 1, 2, 3, 4, 5, 6, 7)[k % 12] * 4096
-            c_ps = psum1.tile([P, R], F32, name="c_ps")
-            d_ps = psum1.tile([P, R], F32, name="d_ps")
+            c_at = (10, 11, 6, 7, 8, 9, 0, 1, 2, 3, 4, 5)[k % 12] * 4096
+            c_ps = psum4.tile([P, R], F32, name="c_ps", tag="out")
+            d_ps = psum4.tile([P, R], F32, name="d_ps", tag="out")
             cd_sb = stage.tile([P, 2, BLK, PACK], F32, name="cd_sb%d" % k, align_bytes=64, offset=c_at)
             project(c_ps, r_passes("rr", k), k)
             nc.scalar.copy(out=cd_sb[:, 0], in_=view(c_ps, k))
@@ -241,16 +231,19 @@ def tile_list_ckg_none_kernel(
             cd[k] = cd_sb
 
         def entity(k):
-            a_ps = psum3.tile([P, R], F32, name="a_ps", tag="ab")
+            a_ps = psum4.tile([P, R], F32, name="a_ps", tag="ab")
             project(a_ps, e_passes("er", k), k)
-            b_ps = psum3.tile([P, R], F32, name="b_ps", tag="ab")
+            b_ps = psum4.tile([P, R], F32, name="b_ps", tag="ab")
             project(b_ps, e_passes("ei", k), k)
             ab[k] = (a_ps, b_ps)
 
         def products(k):
             a_ps, b_ps = ab[k]
             cd_sb = cd[k]
-            pa = work3.tile([P, 2, BLK, PACK], F32, name="pa", align_bytes=64)
+            if k == 1:
+                pa = stage.tile([P, 2, BLK, PACK], F32, name="pa1", align_bytes=64, offset=last + 8 * R)
+            else:
+                pa = work3.tile([P, 2, BLK, PACK], F32, name="pa", align_bytes=64)
             pb = work3.tile([P, 2, BLK, PACK], F32, name="pb", align_bytes=64)
             nc.vector.tensor_tensor(pa[:], cd_sb[:], twice(view(a_ps, k)), MULT)
             nc.vector.scalar_tensor_tensor(pb[:, 0], cd_sb[:, 1], -1.0, view(b_ps, k), MULT, MULT)
@@ -263,7 +256,7 @@ def tile_list_ckg_none_kernel(
             fb = pb[:].rearrange("p c n t -> p (c n t)")
             if MODES[k] == "T":
                 for c in (1, 0):
-                    h_ps = psum3.tile([P, R], F32, name="h_ps", tag="hy")
+                    h_ps = psum4.tile([P, R], F32, name="h_ps", tag="out")
                     for t in range(PACK):
                         cols = slice(c * R + t * P, c * R + (t + 1) * P)
                         o = h_ps[:, t * BLK : (t + 1) * BLK]
@@ -271,9 +264,8 @@ def tile_list_ckg_none_kernel(
                         nc.tensor.matmul(o, lhsT=fb[:, cols], rhs=ident[:], is_transpose=True, start=False, stop=True)
                     nc.scalar.copy(out=h_part(c, h_slot(k), 1).rearrange("p (n t) -> p n t", t=PACK), in_=inter(h_ps))
             else:
-                eng = nc.vector if MODES[k] == "V" else nc.gpsimd
                 h = h_both[:].rearrange("p (c s r) -> p c s r", c=2, r=R)[:, :, h_slot(k), :]
-                eng.tensor_tensor(h, fa.rearrange("p (c r) -> p c r", c=2), fb.rearrange("p (c r) -> p c r", c=2), ADD)
+                nc.gpsimd.tensor_tensor(h, fa.rearrange("p (c r) -> p c r", c=2), fb.rearrange("p (c r) -> p c r", c=2), ADD)
 
         def add_half(eng, c, k):
             pa, pb = prods[k]
@@ -300,7 +292,7 @@ def tile_list_ckg_none_kernel(
             width = GROUP * BLK
             hq, hs = quantise(g % 2, GROUP)
             for t in range(N // P):
-                y_ps = psum3.tile([P, width], F32, name="y_ps", tag="hy")
+                y_ps = psum4.tile([P, width], F32, name="y_ps", tag="out")
                 score_passes(y_ps[:], t, hq, hs, width)
                 y = work4.tile([P, width], F32, name="y")
                 nc.scalar.copy(out=y[:], in_=y_ps[:])
@@ -308,7 +300,7 @@ def tile_list_ckg_none_kernel(
 
         def score_block(k):
             hq, hs = quantise(h_slot(k), 1)
-            y_ps = psum3.tile([P, PACK * BLK], F32, name="y_ps", tag="hy")
+            y_ps = psum4.tile([P, PACK * BLK], F32, name="y_ps", tag="out")
             for t in range(N // P):
                 score_passes(y_ps[:, t * BLK : (t + 1) * BLK], t, hq, hs, BLK)
             y = work4.tile([P, N // P * BLK], F32, name="y")
@@ -318,7 +310,7 @@ def tile_list_ckg_none_kernel(
         def score_last(k):
             hq, hs = quantise(h_slot(k), 1)
             for half, copy in enumerate((nc.scalar.copy, nc.vector.tensor_copy)):
-                y_ps = psum3.tile([P, 2 * BLK], F32, name="y_ps", tag="hy")
+                y_ps = psum4.tile([P, 2 * BLK], F32, name="y_ps", tag="out")
                 for t in range(2):
                     score_passes(y_ps[:, t * BLK : (t + 1) * BLK], 2 * half + t, hq, hs, BLK)
                 y = work4.tile([P, 2 * BLK], F32, name="y")
@@ -339,6 +331,10 @@ def tile_list_ckg_none_kernel(
                 score_group(k // GROUP - 1)
             if MODES[k] == "H":
                 add_half(nc.gpsimd, 1, k)
+            elif MODES[k] == "V":
+                score_block(k - 1)
+                add_half(nc.vector, 0, k)
+                add_half(nc.vector, 1, k)
             else:
                 combine(k)
             if k == NBLK - 2:
@@ -346,5 +342,4 @@ def tile_list_ckg_none_kernel(
                 score_block(k - 1)
             if k in steps:
                 relation(LEAD + steps.index(k))
-        score_block(NBLK - 2)
         score_last(NBLK - 1)

@@ -24,7 +24,7 @@ NBLK = J // BLK
 SLICE = 512
 LEAD = 6
 GROUP = 4
-MODES = "GGGGHGGGHGGGHGTV"
+MODES = "WGGGTGGGTGGGTGTV"
 
 
 def tile_list_ckg_none_kernel(
@@ -219,16 +219,15 @@ def tile_list_ckg_none_kernel(
         def twice(ap):
             return ap.unsqueeze(1).to_broadcast([P, 2, BLK, PACK])
 
-        def relation(k):
-            c_at = (10, 11, 6, 7, 8, 9, 0, 1, 2, 3, 4, 5)[k % 12] * 4096
-            c_ps = psum4.tile([P, R], F32, name="c_ps", tag="out")
-            d_ps = psum4.tile([P, R], F32, name="d_ps", tag="out")
-            cd_sb = stage.tile([P, 2, BLK, PACK], F32, name="cd_sb%d" % k, align_bytes=64, offset=c_at)
-            project(c_ps, r_passes("rr", k), k)
-            nc.scalar.copy(out=cd_sb[:, 0], in_=view(c_ps, k))
-            project(d_ps, r_passes("ri", k), k)
-            nc.scalar.copy(out=cd_sb[:, 1], in_=view(d_ps, k))
-            cd[k] = cd_sb
+        def relation(blocks):
+            for k in blocks:
+                c_at = (10, 11, 0, 1, 6, 7, 8, 9, 2, 3, 4, 5)[k % 12] * 4096
+                cd[k] = stage.tile([P, 2, BLK, PACK], F32, name="cd_sb%d" % k, align_bytes=64, offset=c_at)
+            for c, n in enumerate(("rr", "ri")):
+                for k in blocks:
+                    bank = psum4.tile([P, R], F32, name="cd_ps", tag="out")
+                    project(bank, r_passes(n, k), k)
+                    nc.scalar.copy(out=cd[k][:, c], in_=view(bank, k))
 
         def entity(k):
             a_ps = psum4.tile([P, R], F32, name="a_ps", tag="ab")
@@ -265,7 +264,8 @@ def tile_list_ckg_none_kernel(
                     nc.scalar.copy(out=h_part(c, h_slot(k), 1).rearrange("p (n t) -> p n t", t=PACK), in_=inter(h_ps))
             else:
                 h = h_both[:].rearrange("p (c s r) -> p c s r", c=2, r=R)[:, :, h_slot(k), :]
-                nc.gpsimd.tensor_tensor(h, fa.rearrange("p (c r) -> p c r", c=2), fb.rearrange("p (c r) -> p c r", c=2), ADD)
+                eng = nc.vector if MODES[k] == "W" else nc.gpsimd
+                eng.tensor_tensor(h, fa.rearrange("p (c r) -> p c r", c=2), fb.rearrange("p (c r) -> p c r", c=2), ADD)
 
         def add_half(eng, c, k):
             pa, pb = prods[k]
@@ -320,18 +320,17 @@ def tile_list_ckg_none_kernel(
 
         for k in range(NBLK):
             entity(k)
-        for k in range(LEAD):
-            relation(k)
-        steps = [k for k in range(NBLK) if k % GROUP != 1][: NBLK - LEAD]
+        relation(range(GROUP))
+        for k in range(GROUP, LEAD + 1):
+            relation([k])
+        steps = [k for k in range(NBLK) if k < GROUP or k % GROUP > 1 or k == NBLK - GROUP][: NBLK - LEAD - 1]
         for k in range(NBLK):
             products(k)
-            if k > 0 and MODES[k - 1] == "H":
-                add_half(nc.vector, 0, k - 1)
             if k % GROUP == 1 and k > GROUP:
                 score_group(k // GROUP - 1)
-            if MODES[k] == "H":
-                add_half(nc.gpsimd, 1, k)
-            elif MODES[k] == "V":
+            if k in steps:
+                relation([LEAD + 1 + steps.index(k)])
+            if MODES[k] == "V":
                 score_block(k - 1)
                 add_half(nc.vector, 0, k)
                 add_half(nc.vector, 1, k)
@@ -340,6 +339,4 @@ def tile_list_ckg_none_kernel(
             if k == NBLK - 2:
                 score_block(k - 2)
                 score_block(k - 1)
-            if k in steps:
-                relation(LEAD + steps.index(k))
         score_last(NBLK - 1)

@@ -22,9 +22,10 @@ PACK = 4
 BLK = 128
 NBLK = J // BLK
 SLICE = 512
-LEAD = 6
+LEAD = 8
+FIRST = 5
 GROUP = 4
-MODES = "WGGGTGGGTGGGTGTV"
+MODES = "GGGGTGGGTGGGTGTV"
 
 
 def tile_list_ckg_none_kernel(
@@ -48,20 +49,19 @@ def tile_list_ckg_none_kernel(
         r_picked = keep.tile([P, J], U8, name="r_picked", align_bytes=64)
         r_planes = keep.tile([P, 2 * J], U8, name="r_planes", align_bytes=64)
 
-        names = ["ri0", "rr1", "rr0", "ei", "er", "ri1"]
+        names = ["ri0", "rr1", "rr0", "ei", "ri1", "er"]
         src = {"er": wer, "ei": wei, "rr0": wrr[0:512, :], "rr1": wrr[512:1024, :],
                "ri0": wri[0:512, :], "ri1": wri[512:1024, :]}
         RAW = 4 * PACK * R
         raw = {n: stage.tile([P, PACK, R], F32, name="raw_" + n, align_bytes=64, offset=i * RAW)[:] for i, n in enumerate(names)}
-        t2_scales = stage.tile([P, T], U8, name="t2_scales", align_bytes=64, offset=6 * RAW - T // 2)
-        t1_scales = stage.tile([P, T], U8, name="t1_scales", align_bytes=64, offset=4 * RAW)
+        t2_scales = stage.tile([P, T], U8, name="t2_scales", align_bytes=64, offset=5 * RAW - T // 2)
+        t1_scales = stage.tile([P, T], U8, name="t1_scales", align_bytes=64, offset=3 * RAW)
         t1_words = stage.tile([P, T], I32, name="t1_words", align_bytes=64, offset=6 * RAW)
         late = 6 * RAW + 4 * T
         last = late + 8 * N + 4 * J + 16 * R
         wb = {n: stage.tile([P, PACK * R], BF16, name="wb_" + n, align_bytes=64, offset=last + i * 8 * R) for i, n in enumerate(("er", "ei"))}
-        r_words = [keep.tile([P, 2, 2 * SLICE], U8, name="r_words%d" % s, align_bytes=64) for s in range(3)]
-        r_words = r_words + [stage.tile([P, 2, 2 * SLICE], U8, name="r_words3", align_bytes=64, offset=last)]
-        wb["rr0"] = stage.tile([P, PACK * R], BF16, name="wb_rr0", align_bytes=64, offset=3 * RAW)
+        r_words = [keep.tile([P, 2, 2 * SLICE], U8, name="r_words%d" % s, align_bytes=64) for s in range(J // SLICE)]
+        wb["rr0"] = stage.tile([P, PACK * R], BF16, name="wb_rr0", align_bytes=64, offset=6 * RAW)
         wb["ri0"] = stage.tile([P, PACK * R], BF16, name="wb_ri0", align_bytes=64, offset=late + 8 * N + 4 * J)
         wb["ri1"] = stage.tile([P, PACK * R], BF16, name="wb_ri1", align_bytes=64, offset=late + 8 * N + 4 * J + 8 * R)
         e_words = stage.tile([P, J], U32, name="e_words", align_bytes=64, offset=late + 8 * N)
@@ -137,15 +137,14 @@ def tile_list_ckg_none_kernel(
 
         move_plane(0)
         load_w("ri1")
-        load_words(t1_words, tab_words, (0, T // 2))
+        load_w("er")
         move_plane(1)
-        load_words(t1_words, tab_words, (T // 2, T))
         nc.vector.tensor_copy(e_picked[:], t1_scales[:].indirect(list1[:]))
         for q in range(4):
             nc.gpsimd.dma_start(out=e_scales[32 * q : 32 * q + 4, :].bitcast(I32), in_=e_picked[112 + 4 * q : 116 + 4 * q, :].bitcast(I32))
-        load_w("er")
-        quant_w("rr0")
         load_w("ei")
+        quant_w("rr0")
+        load_words(t1_words, tab_words, (0, T // 2, T))
         quant_w("rr1")
         for plane in (nr_s, ni_s):
             nc.gpsimd.memset(plane[:].bitcast(I32), 0)
@@ -164,13 +163,13 @@ def tile_list_ckg_none_kernel(
         gather2(2)
         gather2(3)
         part2(2)
-        for s in range(J // SLICE):
-            gather1(s)
         cast_w("er")
         quant_w("er")
         part2(3)
         cast_w("ei")
         quant_w("ei")
+        for s in range(J // SLICE):
+            gather1(s)
 
         out_v = out.rearrange("(t p) j -> p t j", p=P)
         cd, ab, prods = {}, {}, {}
@@ -219,9 +218,11 @@ def tile_list_ckg_none_kernel(
         def twice(ap):
             return ap.unsqueeze(1).to_broadcast([P, 2, BLK, PACK])
 
+        order = list(range(1, FIRST)) + [0] + list(range(FIRST, NBLK))
+
         def relation(blocks):
             for k in blocks:
-                c_at = (10, 11, 0, 1, 6, 7, 8, 9, 2, 3, 4, 5)[k % 12] * 4096
+                c_at = ((order.index(k) + 6) % 12) * 4096
                 cd[k] = stage.tile([P, 2, BLK, PACK], F32, name="cd_sb%d" % k, align_bytes=64, offset=c_at)
             for c, n in enumerate(("rr", "ri")):
                 for k in blocks:
@@ -239,10 +240,7 @@ def tile_list_ckg_none_kernel(
         def products(k):
             a_ps, b_ps = ab[k]
             cd_sb = cd[k]
-            if k == 1:
-                pa = stage.tile([P, 2, BLK, PACK], F32, name="pa1", align_bytes=64, offset=last + 8 * R)
-            else:
-                pa = work3.tile([P, 2, BLK, PACK], F32, name="pa", align_bytes=64)
+            pa = work3.tile([P, 2, BLK, PACK], F32, name="pa", align_bytes=64)
             pb = work3.tile([P, 2, BLK, PACK], F32, name="pb", align_bytes=64)
             nc.vector.tensor_tensor(pa[:], cd_sb[:], twice(view(a_ps, k)), MULT)
             nc.vector.scalar_tensor_tensor(pb[:, 0], cd_sb[:, 1], -1.0, view(b_ps, k), MULT, MULT)
@@ -264,8 +262,7 @@ def tile_list_ckg_none_kernel(
                     nc.scalar.copy(out=h_part(c, h_slot(k), 1).rearrange("p (n t) -> p n t", t=PACK), in_=inter(h_ps))
             else:
                 h = h_both[:].rearrange("p (c s r) -> p c s r", c=2, r=R)[:, :, h_slot(k), :]
-                eng = nc.vector if MODES[k] == "W" else nc.gpsimd
-                eng.tensor_tensor(h, fa.rearrange("p (c r) -> p c r", c=2), fb.rearrange("p (c r) -> p c r", c=2), ADD)
+                nc.gpsimd.tensor_tensor(h, fa.rearrange("p (c r) -> p c r", c=2), fb.rearrange("p (c r) -> p c r", c=2), ADD)
 
         def add_half(eng, c, k):
             pa, pb = prods[k]
@@ -320,16 +317,15 @@ def tile_list_ckg_none_kernel(
 
         for k in range(NBLK):
             entity(k)
-        relation(range(GROUP))
-        for k in range(GROUP, LEAD + 1):
+        for k in order[:LEAD]:
             relation([k])
-        steps = [k for k in range(NBLK) if k < GROUP or k % GROUP > 1 or k == NBLK - GROUP][: NBLK - LEAD - 1]
+        steps = [k for k in range(NBLK) if k < GROUP or k % GROUP > 1][: NBLK - LEAD]
         for k in range(NBLK):
             products(k)
             if k % GROUP == 1 and k > GROUP:
                 score_group(k // GROUP - 1)
             if k in steps:
-                relation([LEAD + 1 + steps.index(k)])
+                relation([LEAD + steps.index(k)])
             if MODES[k] == "V":
                 score_block(k - 1)
                 add_half(nc.vector, 0, k)

@@ -16,6 +16,7 @@ FP8X4 = mybir.dt.float8_e4m3fn_x4
 FP4X4 = mybir.dt.float4_e2m1fn_x4
 MULT = mybir.AluOpType.mult
 ADD = mybir.AluOpType.add
+SUB = mybir.AluOpType.subtract
 
 P = 128
 PACK = 4
@@ -23,7 +24,7 @@ BLK = 128
 NBLK = J // BLK
 SLICE = 512
 LEAD = 8
-FIRST = 5
+FIRST = 3
 GROUP = 4
 MODES = "GGGGTGGGTGGGTGTV"
 
@@ -53,23 +54,25 @@ def tile_list_ckg_none_kernel(
         src = {"er": wer, "ei": wei, "rr0": wrr[0:512, :], "rr1": wrr[512:1024, :],
                "ri0": wri[0:512, :], "ri1": wri[512:1024, :]}
         RAW = 4 * PACK * R
-        raw = {n: stage.tile([P, PACK, R], F32, name="raw_" + n, align_bytes=64, offset=i * RAW)[:] for i, n in enumerate(names)}
+        raw = {n: stage.tile([P, PACK, R], F32, name="raw_" + n, align_bytes=64, offset=i * RAW)[:] for i, n in enumerate(names) if n != "ei"}
+        raw_ei = [stage.tile([P, PACK, R // 2], F32, name="raw_ei%d" % h, align_bytes=64, offset=3 * RAW + h * RAW // 2) for h in range(2)]
         t2_scales = stage.tile([P, T], U8, name="t2_scales", align_bytes=64, offset=5 * RAW - T // 2)
-        t1_scales = stage.tile([P, T], U8, name="t1_scales", align_bytes=64, offset=3 * RAW)
+        t1_scales = stage.tile([P, T], U8, name="t1_scales", align_bytes=64, offset=6 * RAW)
         t1_words = stage.tile([P, T], I32, name="t1_words", align_bytes=64, offset=6 * RAW)
         late = 6 * RAW + 4 * T
+        cand = late + 8 * N + 4 * J
         last = late + 8 * N + 4 * J + 16 * R
         wb = {n: stage.tile([P, PACK * R], BF16, name="wb_" + n, align_bytes=64, offset=last + i * 8 * R) for i, n in enumerate(("er", "ei"))}
         r_words = [keep.tile([P, 2, 2 * SLICE], U8, name="r_words%d" % s, align_bytes=64) for s in range(J // SLICE)]
-        wb["rr0"] = stage.tile([P, PACK * R], BF16, name="wb_rr0", align_bytes=64, offset=6 * RAW)
+        wb["rr0"] = stage.tile([P, PACK * R], BF16, name="wb_rr0", align_bytes=64, offset=late)
         wb["ri0"] = stage.tile([P, PACK * R], BF16, name="wb_ri0", align_bytes=64, offset=late + 8 * N + 4 * J)
         wb["ri1"] = stage.tile([P, PACK * R], BF16, name="wb_ri1", align_bytes=64, offset=late + 8 * N + 4 * J + 8 * R)
         e_words = stage.tile([P, J], U32, name="e_words", align_bytes=64, offset=late + 8 * N)
-        wb["rr1"] = stage.tile([P, PACK * R], BF16, name="wb_rr1", align_bytes=64, offset=late)
-        nr_w = stage.tile([P, N], I32, name="nr_w", align_bytes=64, offset=late)
-        ni_w = stage.tile([P, 2 * N], U8, name="ni_w", align_bytes=64, offset=late + 4 * N)
-        nr_s = stage.tile([P, N], U8, name="nr_s", align_bytes=64, offset=late + 6 * N)
-        ni_s = stage.tile([P, N], U8, name="ni_s", align_bytes=64, offset=late + 7 * N)
+        wb["rr1"] = stage.tile([P, PACK * R], BF16, name="wb_rr1", align_bytes=64, offset=3 * RAW + RAW // 4)
+        nr_w = stage.tile([P, N], I32, name="nr_w", align_bytes=64, offset=cand)
+        ni_w = stage.tile([P, 2 * N], U8, name="ni_w", align_bytes=64, offset=cand + 4 * N)
+        nr_s = stage.tile([P, N], U8, name="nr_s", align_bytes=64, offset=cand + 6 * N)
+        ni_s = stage.tile([P, N], U8, name="ni_s", align_bytes=64, offset=cand + 7 * N)
         r_pairs = [keep.tile([P, SLICE], U32, name="pairs%d" % s, align_bytes=64) for s in range(2)]
         r_pairs = r_pairs + [stage.tile([P, SLICE], U32, name="pairs%d" % s, align_bytes=64, offset=late + 8 * N + 4 * J + 8 * R * (s - 2))
                              for s in (2, 3)]
@@ -103,7 +106,7 @@ def tile_list_ckg_none_kernel(
         nc.sync.dma_start(out=t1_scales[112:P, :].bitcast(I32), in_=tab_scales[0].bitcast(I32))
         nc.vector.memset(t2_scales[0:96, :].bitcast(I32), 0)
         nc.vector.memset(t1_scales[0:96, :].bitcast(I32), 0)
-        nc.vector.memset(t1_scales[96:112, :].bitcast(I32), 0)
+        nc.gpsimd.memset(t1_scales[96:112, :].bitcast(I32), 0)
         for plane in (r_planes, e_scales):
             nc.gpsimd.memset(plane[:].bitcast(I32), 0)
         make_identity(nc, ident[:])
@@ -142,16 +145,11 @@ def tile_list_ckg_none_kernel(
         nc.vector.tensor_copy(e_picked[:], t1_scales[:].indirect(list1[:]))
         for q in range(4):
             nc.gpsimd.dma_start(out=e_scales[32 * q : 32 * q + 4, :].bitcast(I32), in_=e_picked[112 + 4 * q : 116 + 4 * q, :].bitcast(I32))
-        load_w("ei")
-        quant_w("rr0")
         load_words(t1_words, tab_words, (0, T // 2, T))
+        quant_w("rr0")
         quant_w("rr1")
-        for plane in (nr_s, ni_s):
-            nc.gpsimd.memset(plane[:].bitcast(I32), 0)
-        nc.sync.dma_start(out=nr_w[:], in_=nr_words[0].rearrange("p n i -> p (n i)").bitcast(I32))
-        nc.sync.dma_start(out=ni_w[:].bitcast(I32), in_=ni_words[0].bitcast(I32))
-        load_plane(nr_s, nr_scales[0])
-        load_plane(ni_s, ni_scales[0])
+        for h in range(2):
+            nc.sync.dma_start(out=raw_ei[h][:], in_=wei.rearrange("(p j) r -> p j r", j=PACK)[:, :, h * R // 2 : (h + 1) * R // 2])
         gather2(0)
         gather2(1)
         part2(0)
@@ -163,13 +161,23 @@ def tile_list_ckg_none_kernel(
         gather2(2)
         gather2(3)
         part2(2)
+        for plane in (nr_s, ni_s):
+            nc.gpsimd.memset(plane[:].bitcast(I32), 0)
+        nc.sync.dma_start(out=nr_w[:], in_=nr_words[0].rearrange("p n i -> p (n i)").bitcast(I32))
+        nc.sync.dma_start(out=ni_w[:].bitcast(I32), in_=ni_words[0].bitcast(I32))
+        load_plane(nr_s, nr_scales[0])
+        load_plane(ni_s, ni_scales[0])
         cast_w("er")
         quant_w("er")
         part2(3)
-        cast_w("ei")
-        quant_w("ei")
         for s in range(J // SLICE):
             gather1(s)
+        for h in range(2):
+            nc.scalar.copy(
+                out=wb["ei"][:].rearrange("p (t m j) -> p m j t", t=PACK, j=PACK)[:, h * P // 2 : (h + 1) * P // 2],
+                in_=raw_ei[h][:].rearrange("p j (m t) -> p m j t", t=PACK),
+            )
+        quant_w("ei")
 
         out_v = out.rearrange("(t p) j -> p t j", p=P)
         cd, ab, prods = {}, {}, {}
@@ -222,7 +230,7 @@ def tile_list_ckg_none_kernel(
 
         def relation(blocks):
             for k in blocks:
-                c_at = ((order.index(k) + 6) % 12) * 4096
+                c_at = (10, 11, 0, 6, 7, 1, 2, 3, 4, 5, 8, 9)[order.index(k) % 12] * 4096
                 cd[k] = stage.tile([P, 2, BLK, PACK], F32, name="cd_sb%d" % k, align_bytes=64, offset=c_at)
             for c, n in enumerate(("rr", "ri")):
                 for k in blocks:
@@ -240,11 +248,17 @@ def tile_list_ckg_none_kernel(
         def products(k):
             a_ps, b_ps = ab[k]
             cd_sb = cd[k]
-            pa = work3.tile([P, 2, BLK, PACK], F32, name="pa", align_bytes=64)
+            if k == 0:
+                pa = stage.tile([P, 2, BLK, PACK], F32, name="pa0", align_bytes=64, offset=last + 8 * R)
+            else:
+                pa = work3.tile([P, 2, BLK, PACK], F32, name="pa", align_bytes=64)
             pb = work3.tile([P, 2, BLK, PACK], F32, name="pb", align_bytes=64)
             nc.vector.tensor_tensor(pa[:], cd_sb[:], twice(view(a_ps, k)), MULT)
-            nc.vector.scalar_tensor_tensor(pb[:, 0], cd_sb[:, 1], -1.0, view(b_ps, k), MULT, MULT)
-            nc.vector.tensor_tensor(pb[:, 1], cd_sb[:, 0], view(b_ps, k), MULT)
+            if MODES[k] == "T":
+                nc.vector.tensor_tensor(pb[:, 0], cd_sb[:, 0], view(b_ps, k), MULT)
+                nc.vector.scalar_tensor_tensor(pb[:, 1], cd_sb[:, 1], -1.0, view(b_ps, k), MULT, MULT)
+            else:
+                nc.vector.tensor_tensor(pb[:], cd_sb[:], twice(view(b_ps, k)), MULT)
             prods[k] = (pa, pb)
 
         def combine(k):
@@ -256,17 +270,18 @@ def tile_list_ckg_none_kernel(
                     h_ps = psum4.tile([P, R], F32, name="h_ps", tag="out")
                     for t in range(PACK):
                         cols = slice(c * R + t * P, c * R + (t + 1) * P)
+                        other = slice((1 - c) * R + t * P, (1 - c) * R + (t + 1) * P)
                         o = h_ps[:, t * BLK : (t + 1) * BLK]
                         nc.tensor.matmul(o, lhsT=fa[:, cols], rhs=ident[:], is_transpose=True, start=True, stop=False)
-                        nc.tensor.matmul(o, lhsT=fb[:, cols], rhs=ident[:], is_transpose=True, start=False, stop=True)
+                        nc.tensor.matmul(o, lhsT=fb[:, other], rhs=ident[:], is_transpose=True, start=False, stop=True)
                     nc.scalar.copy(out=h_part(c, h_slot(k), 1).rearrange("p (n t) -> p n t", t=PACK), in_=inter(h_ps))
             else:
-                h = h_both[:].rearrange("p (c s r) -> p c s r", c=2, r=R)[:, :, h_slot(k), :]
-                nc.gpsimd.tensor_tensor(h, fa.rearrange("p (c r) -> p c r", c=2), fb.rearrange("p (c r) -> p c r", c=2), ADD)
+                add_half(nc.gpsimd, 0, k)
+                add_half(nc.gpsimd, 1, k)
 
         def add_half(eng, c, k):
             pa, pb = prods[k]
-            eng.tensor_tensor(h_part(c, h_slot(k), 1), pa[:, c].rearrange("p n t -> p (n t)"), pb[:, c].rearrange("p n t -> p (n t)"), ADD)
+            eng.tensor_tensor(h_part(c, h_slot(k), 1), pa[:, c].rearrange("p n t -> p (n t)"), pb[:, 1 - c].rearrange("p n t -> p (n t)"), (SUB, ADD)[c])
 
         def quantise(first, count):
             width = count * BLK
@@ -319,7 +334,7 @@ def tile_list_ckg_none_kernel(
             entity(k)
         for k in order[:LEAD]:
             relation([k])
-        steps = [k for k in range(NBLK) if k < GROUP or k % GROUP > 1][: NBLK - LEAD]
+        steps = [k for k in range(NBLK) if k < GROUP - 1 or (k > GROUP and k % GROUP > 1) or k == NBLK - GROUP][: NBLK - LEAD]
         for k in range(NBLK):
             products(k)
             if k % GROUP == 1 and k > GROUP:

@@ -184,11 +184,15 @@ def tile_list_ckg_none_kernel(
         h_both = keep.tile([P, 2 * (GROUP + 1) * R], BF16, name="h_both", align_bytes=64)
 
         def h_slot(k):
-            g, i = divmod(min(k, NBLK - 2), GROUP)
+            g, i = divmod(k, GROUP)
+            if g == NBLK // GROUP - 1:
+                return max(GROUP - i, 2)
             return i if i > 0 else GROUP * (g % 2)
 
         def tokens(k):
             g, i = divmod(k, GROUP)
+            if g == NBLK // GROUP - 1:
+                return (g * GROUP + (1 - i if i < 2 else i)) * BLK
             return (g * GROUP + (i - g % 2) % GROUP) * BLK
 
         def h_part(c, first, count):
@@ -228,22 +232,26 @@ def tile_list_ckg_none_kernel(
 
         order = list(range(1, FIRST)) + [0] + list(range(FIRST, NBLK))
 
-        def relation(blocks):
-            for k in blocks:
-                c_at = (10, 11, 0, 6, 7, 1, 2, 3, 4, 5, 8, 9)[order.index(k) % 12] * 4096
-                cd[k] = stage.tile([P, 2, BLK, PACK], F32, name="cd_sb%d" % k, align_bytes=64, offset=c_at)
+        parked = {}
+
+        def banked(passes, k, tag):
+            bank = psum4.tile([P, R], F32, name="bank", tag=tag)
+            project(bank, passes, k)
+            return bank
+
+        def relation(k):
+            c_at = (10, 11, 0, 7, 6, 1, 2, 3, 4, 5, 8, 9)[order.index(k) % 12] * 4096
+            cd[k] = stage.tile([P, 2, BLK, PACK], F32, name="cd_sb%d" % k, align_bytes=64, offset=c_at)
             for c, n in enumerate(("rr", "ri")):
-                for k in blocks:
-                    bank = psum4.tile([P, R], F32, name="cd_ps", tag="out")
-                    project(bank, r_passes(n, k), k)
-                    nc.scalar.copy(out=cd[k][:, c], in_=view(bank, k))
+                bank = parked[n] if k == FIRST else banked(r_passes(n, k), k, "out")
+                nc.scalar.copy(out=cd[k][:, c], in_=view(bank, k))
 
         def entity(k):
-            a_ps = psum4.tile([P, R], F32, name="a_ps", tag="ab")
-            project(a_ps, e_passes("er", k), k)
-            b_ps = psum4.tile([P, R], F32, name="b_ps", tag="ab")
-            project(b_ps, e_passes("ei", k), k)
-            ab[k] = (a_ps, b_ps)
+            a_ps = banked(e_passes("er", k), k, "ab")
+            if k == 0:
+                for n in ("rr", "ri"):
+                    parked[n] = banked(r_passes(n, FIRST), FIRST, "ab")
+            ab[k] = (a_ps, banked(e_passes("ei", k), k, "ab"))
 
         def products(k):
             a_ps, b_ps = ab[k]
@@ -292,12 +300,14 @@ def tile_list_ckg_none_kernel(
                 nc.vector.quantize_mx(out=hq[:, cols].bitcast(FP8X4), scales=hs[:, cols], in_=h_part(c, first, count))
             return hq, hs
 
-        def score_passes(o, t, hq, hs, width):
+        def score_passes(o, t, hq, hs, width, at, n):
             m = slice(t * P, (t + 1) * P)
+            re = slice(at, at + n)
+            im = slice(width + at, width + at + n)
             nc.tensor.matmul_mx(out=o, lhsT=nr_w[:, m].bitcast(FP8X4), lhsT_scale=nr_s[:, m],
-                                rhs=hq[:, 0:width].bitcast(FP8X4), rhs_scale=hs[:, 0:width], start=True, stop=False)
+                                rhs=hq[:, re].bitcast(FP8X4), rhs_scale=hs[:, re], start=True, stop=False)
             nc.tensor.matmul_mx(out=o, lhsT=ni_w[:, 2 * t * P : 2 * (t + 1) * P].bitcast(FP4X4), lhsT_scale=ni_s[:, m],
-                                rhs=hq[:, width : 2 * width].bitcast(FP8X4), rhs_scale=hs[:, width : 2 * width],
+                                rhs=hq[:, im].bitcast(FP8X4), rhs_scale=hs[:, im],
                                 start=False, stop=True)
 
         def score_group(g):
@@ -305,7 +315,7 @@ def tile_list_ckg_none_kernel(
             hq, hs = quantise(g % 2, GROUP)
             for t in range(N // P):
                 y_ps = psum4.tile([P, width], F32, name="y_ps", tag="out")
-                score_passes(y_ps[:], t, hq, hs, width)
+                score_passes(y_ps[:], t, hq, hs, width, 0, width)
                 y = work4.tile([P, width], F32, name="y")
                 nc.scalar.copy(out=y[:], in_=y_ps[:])
                 nc.sync.dma_start(out=out[t * P : (t + 1) * P, g * width : (g + 1) * width], in_=y[:])
@@ -314,17 +324,28 @@ def tile_list_ckg_none_kernel(
             hq, hs = quantise(h_slot(k), 1)
             y_ps = psum4.tile([P, PACK * BLK], F32, name="y_ps", tag="out")
             for t in range(N // P):
-                score_passes(y_ps[:, t * BLK : (t + 1) * BLK], t, hq, hs, BLK)
+                score_passes(y_ps[:, t * BLK : (t + 1) * BLK], t, hq, hs, BLK, 0, BLK)
             y = work4.tile([P, N // P * BLK], F32, name="y")
             nc.scalar.copy(out=y[:], in_=y_ps[:])
             nc.sync.dma_start(out=out_v[:, :, tokens(k) : tokens(k) + BLK], in_=y[:].rearrange("p (t n) -> p t n", n=BLK))
+
+        def score_pair(k):
+            hq, hs = quantise(h_slot(k), 2)
+            for half in range(2):
+                y_ps = psum4.tile([P, PACK * BLK], F32, name="y_ps", tag="out")
+                for i in range(PACK):
+                    score_passes(y_ps[:, i * BLK : (i + 1) * BLK], 2 * half + i // 2, hq, hs, 2 * BLK, i % 2 * BLK, BLK)
+                y = work4.tile([P, PACK * BLK], F32, name="y")
+                nc.scalar.copy(out=y[:], in_=y_ps[:])
+                nc.sync.dma_start(out=out_v[:, 2 * half : 2 * half + 2, tokens(k) : tokens(k) + 2 * BLK],
+                                  in_=y[:].rearrange("p (t n) -> p t n", t=2))
 
         def score_last(k):
             hq, hs = quantise(h_slot(k), 1)
             for half, copy in enumerate((nc.scalar.copy, nc.vector.tensor_copy)):
                 y_ps = psum4.tile([P, 2 * BLK], F32, name="y_ps", tag="out")
                 for t in range(2):
-                    score_passes(y_ps[:, t * BLK : (t + 1) * BLK], 2 * half + t, hq, hs, BLK)
+                    score_passes(y_ps[:, t * BLK : (t + 1) * BLK], 2 * half + t, hq, hs, BLK, 0, BLK)
                 y = work4.tile([P, 2 * BLK], F32, name="y")
                 copy(y[:], y_ps[:])
                 nc.sync.dma_start(out=out_v[:, 2 * half : 2 * half + 2, tokens(k) : tokens(k) + BLK],
@@ -333,14 +354,14 @@ def tile_list_ckg_none_kernel(
         for k in range(NBLK):
             entity(k)
         for k in order[:LEAD]:
-            relation([k])
-        steps = [k for k in range(NBLK) if k < GROUP - 1 or (k > GROUP and k % GROUP > 1) or k == NBLK - GROUP][: NBLK - LEAD]
+            relation(k)
+        steps = [k for k in range(NBLK) if k < GROUP or k % GROUP > 1][: NBLK - LEAD]
         for k in range(NBLK):
             products(k)
             if k % GROUP == 1 and k > GROUP:
                 score_group(k // GROUP - 1)
             if k in steps:
-                relation([LEAD + steps.index(k)])
+                relation(LEAD + steps.index(k))
             if MODES[k] == "V":
                 score_block(k - 1)
                 add_half(nc.vector, 0, k)
@@ -348,6 +369,5 @@ def tile_list_ckg_none_kernel(
             else:
                 combine(k)
             if k == NBLK - 2:
-                score_block(k - 2)
-                score_block(k - 1)
+                score_pair(k - 1)
         score_last(NBLK - 1)

@@ -46,7 +46,6 @@ def tile_list_ckg_none_kernel(
         ident = keep.tile([P, P], F32, name="ident", align_bytes=64)
         t2_words = keep.tile([P, T], I32, name="t2_words", align_bytes=64)
         e_picked = keep.tile([P, J], U8, name="e_picked", align_bytes=64)
-        e_scales = keep.tile([P, J], U8, name="e_scales", align_bytes=64)
         r_picked = keep.tile([P, J], U8, name="r_picked", align_bytes=64)
         r_planes = keep.tile([P, 2 * J], U8, name="r_planes", align_bytes=64)
 
@@ -55,7 +54,7 @@ def tile_list_ckg_none_kernel(
                "ri0": wri[0:512, :], "ri1": wri[512:1024, :]}
         RAW = 4 * PACK * R
         raw = {n: stage.tile([P, PACK, R], F32, name="raw_" + n, align_bytes=64, offset=i * RAW)[:] for i, n in enumerate(names) if n != "ei"}
-        raw_ei = [stage.tile([P, PACK, R // 2], F32, name="raw_ei%d" % h, align_bytes=64, offset=3 * RAW + h * RAW // 2) for h in range(2)]
+        raw_ei = stage.tile([P, 2, PACK, R // 2], F32, name="raw_ei", align_bytes=64, offset=3 * RAW)
         t2_scales = stage.tile([P, T], U8, name="t2_scales", align_bytes=64, offset=5 * RAW - T // 2)
         t1_scales = stage.tile([P, T], U8, name="t1_scales", align_bytes=64, offset=6 * RAW)
         t1_words = stage.tile([P, T], I32, name="t1_words", align_bytes=64, offset=6 * RAW)
@@ -68,7 +67,8 @@ def tile_list_ckg_none_kernel(
         wb["ri0"] = stage.tile([P, PACK * R], BF16, name="wb_ri0", align_bytes=64, offset=late + 8 * N + 4 * J)
         wb["ri1"] = stage.tile([P, PACK * R], BF16, name="wb_ri1", align_bytes=64, offset=late + 8 * N + 4 * J + 8 * R)
         e_words = stage.tile([P, J], U32, name="e_words", align_bytes=64, offset=late + 8 * N)
-        wb["rr1"] = stage.tile([P, PACK * R], BF16, name="wb_rr1", align_bytes=64, offset=3 * RAW + RAW // 4)
+        wb["rr1"] = stage.tile([P, PACK * R], BF16, name="wb_rr1", align_bytes=64, offset=3 * RAW)
+        e_scales = stage.tile([P, J], U8, name="e_scales", align_bytes=64, offset=late)
         nr_w = stage.tile([P, N], I32, name="nr_w", align_bytes=64, offset=cand)
         ni_w = stage.tile([P, 2 * N], U8, name="ni_w", align_bytes=64, offset=cand + 4 * N)
         nr_s = stage.tile([P, N], U8, name="nr_s", align_bytes=64, offset=cand + 6 * N)
@@ -106,9 +106,8 @@ def tile_list_ckg_none_kernel(
         nc.sync.dma_start(out=t1_scales[112:P, :].bitcast(I32), in_=tab_scales[0].bitcast(I32))
         nc.vector.memset(t2_scales[0:96, :].bitcast(I32), 0)
         nc.vector.memset(t1_scales[0:96, :].bitcast(I32), 0)
-        nc.gpsimd.memset(t1_scales[96:112, :].bitcast(I32), 0)
-        for plane in (r_planes, e_scales):
-            nc.gpsimd.memset(plane[:].bitcast(I32), 0)
+        nc.vector.memset(t1_scales[96:112, :].bitcast(I32), 0)
+        nc.vector.memset(r_planes[:].bitcast(I32), 0)
         make_identity(nc, ident[:])
         load_w("rr0")
         load_w("rr1")
@@ -143,13 +142,14 @@ def tile_list_ckg_none_kernel(
         load_w("er")
         move_plane(1)
         nc.vector.tensor_copy(e_picked[:], t1_scales[:].indirect(list1[:]))
-        for q in range(4):
-            nc.gpsimd.dma_start(out=e_scales[32 * q : 32 * q + 4, :].bitcast(I32), in_=e_picked[112 + 4 * q : 116 + 4 * q, :].bitcast(I32))
         load_words(t1_words, tab_words, (0, T // 2, T))
         quant_w("rr0")
+        nc.vector.memset(e_scales[:].bitcast(I32), 0)
+        for q in range(4):
+            nc.sync.dma_start(out=e_scales[32 * q : 32 * q + 4, :].bitcast(I32), in_=e_picked[112 + 4 * q : 116 + 4 * q, :].bitcast(I32))
         quant_w("rr1")
         for h in range(2):
-            nc.sync.dma_start(out=raw_ei[h][:], in_=wei.rearrange("(p j) r -> p j r", j=PACK)[:, :, h * R // 2 : (h + 1) * R // 2])
+            nc.sync.dma_start(out=raw_ei[:, h], in_=wei.rearrange("(p j) r -> p j r", j=PACK)[:, :, h * R // 2 : (h + 1) * R // 2])
         gather2(0)
         gather2(1)
         part2(0)
@@ -162,7 +162,7 @@ def tile_list_ckg_none_kernel(
         gather2(3)
         part2(2)
         for plane in (nr_s, ni_s):
-            nc.gpsimd.memset(plane[:].bitcast(I32), 0)
+            nc.vector.memset(plane[:].bitcast(I32), 0)
         nc.sync.dma_start(out=nr_w[:], in_=nr_words[0].rearrange("p n i -> p (n i)").bitcast(I32))
         nc.sync.dma_start(out=ni_w[:].bitcast(I32), in_=ni_words[0].bitcast(I32))
         load_plane(nr_s, nr_scales[0])
@@ -175,7 +175,7 @@ def tile_list_ckg_none_kernel(
         for h in range(2):
             nc.scalar.copy(
                 out=wb["ei"][:].rearrange("p (t m j) -> p m j t", t=PACK, j=PACK)[:, h * P // 2 : (h + 1) * P // 2],
-                in_=raw_ei[h][:].rearrange("p j (m t) -> p m j t", t=PACK),
+                in_=raw_ei[:, h].rearrange("p j (m t) -> p m j t", t=PACK),
             )
         quant_w("ei")
 
@@ -240,7 +240,7 @@ def tile_list_ckg_none_kernel(
             return bank
 
         def relation(k):
-            c_at = (10, 11, 0, 7, 6, 1, 2, 3, 4, 5, 8, 9)[order.index(k) % 12] * 4096
+            c_at = (20, 22, 0, 11, 13, 15, 2, 4, 6, 8, 18)[order.index(k) % 11] * 2048
             cd[k] = stage.tile([P, 2, BLK, PACK], F32, name="cd_sb%d" % k, align_bytes=64, offset=c_at)
             for c, n in enumerate(("rr", "ri")):
                 bank = parked[n] if k == FIRST else banked(r_passes(n, k), k, "out")
@@ -351,9 +351,11 @@ def tile_list_ckg_none_kernel(
                 nc.sync.dma_start(out=out_v[:, 2 * half : 2 * half + 2, tokens(k) : tokens(k) + BLK],
                                   in_=y[:].rearrange("p (t n) -> p t n", n=BLK))
 
+        for k in order[:FIRST]:
+            relation(k)
         for k in range(NBLK):
             entity(k)
-        for k in order[:LEAD]:
+        for k in order[FIRST:LEAD]:
             relation(k)
         steps = [k for k in range(NBLK) if k < GROUP or k % GROUP > 1][: NBLK - LEAD]
         for k in range(NBLK):

@@ -80,8 +80,8 @@ def tile_list_ckg_none_kernel(
         ws = {n: keep.tile([P, R], U8, name="ws_" + n, align_bytes=64) for n in names}
 
         def load_plane(plane, rows):
-            for q in range(4):
-                nc.sync.dma_start(out=plane[32 * q : 32 * q + 4, :].bitcast(I32), in_=rows[4 * q : 4 * q + 4, :].bitcast(I32))
+            for r in range(4):
+                nc.sync.dma_start(out=plane[r:P:32, :].bitcast(I32), in_=rows[r:16:4, :].bitcast(I32))
 
         def load_words(tile, words, cuts):
             rows = words[0].rearrange("p t i -> p (t i)").bitcast(I32)
@@ -103,10 +103,10 @@ def tile_list_ckg_none_kernel(
         nc.sync.dma_start(list2[:], offs2)
         nc.sync.dma_start(out=t2_scales[96:P, :].bitcast(I32), in_=tab2_scales.rearrange("a q t -> (a q) t").bitcast(I32))
         nc.sync.dma_start(list1[:], offs)
-        nc.sync.dma_start(out=t1_scales[112:P, :].bitcast(I32), in_=tab_scales[0].bitcast(I32))
+        nc.sync.dma_start(out=t1_scales[48:64, :].bitcast(I32), in_=tab_scales[0].bitcast(I32))
         nc.vector.memset(t2_scales[0:96, :].bitcast(I32), 0)
-        nc.vector.memset(t1_scales[0:96, :].bitcast(I32), 0)
-        nc.vector.memset(t1_scales[96:112, :].bitcast(I32), 0)
+        nc.vector.memset(t1_scales[0:48, :].bitcast(I32), 0)
+        nc.vector.memset(t1_scales[64:P, :].bitcast(I32), 0)
         nc.vector.memset(r_planes[:].bitcast(I32), 0)
         make_identity(nc, ident[:])
         load_w("rr0")
@@ -132,10 +132,10 @@ def tile_list_ckg_none_kernel(
         nc.vector.tensor_copy(r_picked[:], t2_scales[:].indirect(list2[:]))
 
         def move_plane(a):
-            for q in range(4):
-                row = 96 + 16 * a + 4 * q
-                nc.sync.dma_start(out=r_planes[32 * q : 32 * q + 4, a * J : (a + 1) * J].bitcast(I32),
-                                  in_=r_picked[row : row + 4, :].bitcast(I32))
+            for r in range(4):
+                row = 96 + 16 * a
+                nc.sync.dma_start(out=r_planes[r:P:32, a * J : (a + 1) * J].bitcast(I32),
+                                  in_=r_picked[row + r : row + 16 : 4, :].bitcast(I32))
 
         move_plane(0)
         load_w("ri1")
@@ -145,8 +145,8 @@ def tile_list_ckg_none_kernel(
         load_words(t1_words, tab_words, (0, T // 2, T))
         quant_w("rr0")
         nc.vector.memset(e_scales[:].bitcast(I32), 0)
-        for q in range(4):
-            nc.sync.dma_start(out=e_scales[32 * q : 32 * q + 4, :].bitcast(I32), in_=e_picked[112 + 4 * q : 116 + 4 * q, :].bitcast(I32))
+        for r in range(4):
+            nc.sync.dma_start(out=e_scales[8 + r : P : 32, :].bitcast(I32), in_=e_picked[48 + r : 64 : 4, :].bitcast(I32))
         quant_w("rr1")
         for h in range(2):
             nc.sync.dma_start(out=raw_ei[:, h], in_=wei.rearrange("(p j) r -> p j r", j=PACK)[:, :, h * R // 2 : (h + 1) * R // 2])
@@ -215,7 +215,7 @@ def tile_list_ckg_none_kernel(
 
         def e_passes(n, k):
             tok = slice(tokens(k), tokens(k) + BLK)
-            return [(n, e_words[:, tok].bitcast(FP8X4), e_scales[:, tok])]
+            return [(n, e_words[:, tok].bitcast(FP8X4), e_scales[8:P, tok])]
 
         def r_passes(n, k):
             return [(n + str(a), r_words[k // GROUP][:, a, 2 * (tokens(k) % SLICE) : 2 * (tokens(k) % SLICE + BLK)].bitcast(FP4X4), r_planes[:, a * J + tokens(k) : a * J + tokens(k) + BLK])

@@ -23,10 +23,10 @@ PACK = 4
 BLK = 128
 NBLK = J // BLK
 SLICE = 512
-LEAD = 8
-FIRST = 3
 GROUP = 4
-MODES = "GGGGTGGGTGGGTGTV"
+KIB = 1024
+TURNED = (2, 3, 12, 13, 14)
+LAST = NBLK - 1
 
 
 def tile_list_ckg_none_kernel(
@@ -36,340 +36,427 @@ def tile_list_ckg_none_kernel(
     nc = tc.nc
     with ExitStack() as ctx:
         keep = ctx.enter_context(tc.tile_pool(name="keep", bufs=1))
-        stage = ctx.enter_context(tc.tile_pool(name="stage", bufs=1))
-        work3 = ctx.enter_context(tc.tile_pool(name="work3", bufs=3))
-        work4 = ctx.enter_context(tc.tile_pool(name="work4", bufs=4))
-        psum4 = ctx.enter_context(tc.psum_pool(name="psum4", bufs=4))
+        arena = ctx.enter_context(tc.tile_pool(name="arena", bufs=1))
+        codes = ctx.enter_context(tc.tile_pool(name="codes", bufs=4))
+        psum = ctx.enter_context(tc.psum_pool(name="psum", bufs=4))
+
+        def at(name, shape, dtype, kib):
+            return arena.tile([P] + shape, dtype, name=name, align_bytes=64, offset=kib * KIB)
+
+        def held(name, shape, dtype):
+            return keep.tile([P] + shape, dtype, name=name, align_bytes=64)
 
         list1 = keep.tile([P, J // 16], U16, name="list1")
         list2 = keep.tile([P, J // 16], U16, name="list2")
-        ident = keep.tile([P, P], F32, name="ident", align_bytes=64)
-        t2_words = keep.tile([P, T], I32, name="t2_words", align_bytes=64)
-        e_picked = keep.tile([P, J], U8, name="e_picked", align_bytes=64)
-        r_picked = keep.tile([P, J], U8, name="r_picked", align_bytes=64)
-        r_planes = keep.tile([P, 2 * J], U8, name="r_planes", align_bytes=64)
+        ident = held("ident", [P], F32)
+        e_words = [held("e_words%d" % s, [SLICE], U32) for s in range(J // SLICE - 1)]
+        e_plane = held("e_plane", [J], U8)
+        r_planes = held("r_planes", [2 * J], U8)
+        r_words = [held("r_words%d" % s, [2, 2 * SLICE], U8) for s in range(J // SLICE)]
+        wq = {n: held("wq_" + n, [w], U32) for n, w in (("rr", 2 * R), ("ri0", R), ("ri1", R), ("er", R), ("ei", R))}
+        ws = {n: held("ws_" + n, [w], U8) for n, w in (("rr", 2 * R), ("ri0", R), ("ri1", R), ("er", R), ("ei", R))}
 
-        names = ["ri0", "rr1", "rr0", "ei", "ri1", "er"]
-        src = {"er": wer, "ei": wei, "rr0": wrr[0:512, :], "rr1": wrr[512:1024, :],
-               "ri0": wri[0:512, :], "ri1": wri[512:1024, :]}
-        RAW = 4 * PACK * R
-        raw = {n: stage.tile([P, PACK, R], F32, name="raw_" + n, align_bytes=64, offset=i * RAW)[:] for i, n in enumerate(names) if n != "ei"}
-        raw_ei = stage.tile([P, 2, PACK, R // 2], F32, name="raw_ei", align_bytes=64, offset=3 * RAW)
-        t2_scales = stage.tile([P, T], U8, name="t2_scales", align_bytes=64, offset=5 * RAW - T // 2)
-        t1_scales = stage.tile([P, T], U8, name="t1_scales", align_bytes=64, offset=6 * RAW)
-        t1_words = stage.tile([P, T], I32, name="t1_words", align_bytes=64, offset=6 * RAW)
-        late = 6 * RAW + 4 * T
-        cand = late + 8 * N + 4 * J
-        last = late + 8 * N + 4 * J + 16 * R
-        wb = {n: stage.tile([P, PACK * R], BF16, name="wb_" + n, align_bytes=64, offset=last + i * 8 * R) for i, n in enumerate(("er", "ei"))}
-        r_words = [keep.tile([P, 2, 2 * SLICE], U8, name="r_words%d" % s, align_bytes=64) for s in range(J // SLICE)]
-        wb["rr0"] = stage.tile([P, PACK * R], BF16, name="wb_rr0", align_bytes=64, offset=late)
-        wb["ri0"] = stage.tile([P, PACK * R], BF16, name="wb_ri0", align_bytes=64, offset=late + 8 * N + 4 * J)
-        wb["ri1"] = stage.tile([P, PACK * R], BF16, name="wb_ri1", align_bytes=64, offset=late + 8 * N + 4 * J + 8 * R)
-        e_words = stage.tile([P, J], U32, name="e_words", align_bytes=64, offset=late + 8 * N)
-        wb["rr1"] = stage.tile([P, PACK * R], BF16, name="wb_rr1", align_bytes=64, offset=3 * RAW)
-        e_scales = stage.tile([P, J], U8, name="e_scales", align_bytes=64, offset=late)
-        nr_w = stage.tile([P, N], I32, name="nr_w", align_bytes=64, offset=cand)
-        ni_w = stage.tile([P, 2 * N], U8, name="ni_w", align_bytes=64, offset=cand + 4 * N)
-        nr_s = stage.tile([P, N], U8, name="nr_s", align_bytes=64, offset=cand + 6 * N)
-        ni_s = stage.tile([P, N], U8, name="ni_s", align_bytes=64, offset=cand + 7 * N)
-        r_pairs = [keep.tile([P, SLICE], U32, name="pairs%d" % s, align_bytes=64) for s in range(2)]
-        r_pairs = r_pairs + [stage.tile([P, SLICE], U32, name="pairs%d" % s, align_bytes=64, offset=late + 8 * N + 4 * J + 8 * R * (s - 2))
-                             for s in (2, 3)]
-        wq = {n: keep.tile([P, R], U32, name="wq_" + n, align_bytes=64) for n in names}
-        ws = {n: keep.tile([P, R], U8, name="ws_" + n, align_bytes=64) for n in names}
+        RAW_A, RAW_B, RAW_C, RAW_D, TAB1, TAB2, CAST_A, CAST_B, SMALL, H_A, H_B, A_COPY, CD = 0, 8, 16, 24, 32, 48, 64, 72, 80, 88, 96, 104, 110
 
-        def load_plane(plane, rows):
+        t2_rows = at("t2_rows", [T], U8, RAW_D)
+        t1_rows = at("t1_rows", [T], U8, TAB1)
+        r_picked = at("r_picked", [J], U8, SMALL)
+        e_picked = at("e_picked", [J], U8, SMALL + 2)
+        t2_words = at("t2_words", [T], I32, TAB2)
+
+        def rows_of(w):
+            return w.rearrange("(p j) r -> p j r", j=PACK)
+
+        def load_raw(name, w, kib):
+            raw = at("raw_" + name, [PACK, R], F32, kib)
+            nc.sync.dma_start(out=raw[:], in_=rows_of(w))
+            return raw
+
+        def cast(dst, raw):
+            nc.scalar.copy(out=dst.rearrange("p (t m j) -> p m j t", t=PACK, j=PACK),
+                           in_=raw.rearrange("p j (m t) -> p m j t", t=PACK))
+
+        def quantise_weight(n, src):
+            nc.vector.quantize_mx(out=wq[n][:].bitcast(FP8X4), scales=ws[n][:], in_=src)
+
+        def move_rows(plane, picked, first):
             for r in range(4):
-                nc.sync.dma_start(out=plane[r:P:32, :].bitcast(I32), in_=rows[r:16:4, :].bitcast(I32))
+                nc.sync.dma_start(out=plane[r:P:32].bitcast(I32), in_=picked[first + r : first + 16 : 4, :].bitcast(I32))
 
-        def load_words(tile, words, cuts):
-            rows = words[0].rearrange("p t i -> p (t i)").bitcast(I32)
-            for c0, c1 in zip(cuts, cuts[1:]):
-                nc.sync.dma_start(out=tile[:, c0:c1], in_=rows[:, c0:c1])
-
-        def load_w(n):
-            nc.sync.dma_start(out=raw[n], in_=src[n].rearrange("(p j) r -> p j r", j=PACK))
-
-        def cast_w(n):
-            nc.scalar.copy(
-                out=wb[n][:].rearrange("p (t m j) -> p m j t", t=PACK, j=PACK),
-                in_=raw[n].rearrange("p j (m t) -> p m j t", t=PACK),
-            )
-
-        def quant_w(n):
-            nc.vector.quantize_mx(out=wq[n][:].bitcast(FP8X4), scales=ws[n][:], in_=wb[n][:])
+        def words_of(words):
+            return words[0].rearrange("p t i -> p (t i)").bitcast(I32)
 
         nc.sync.dma_start(list2[:], offs2)
-        nc.sync.dma_start(out=t2_scales[96:P, :].bitcast(I32), in_=tab2_scales.rearrange("a q t -> (a q) t").bitcast(I32))
+        nc.sync.dma_start(out=t2_rows[96:P, :].bitcast(I32), in_=tab2_scales.rearrange("a q t -> (a q) t").bitcast(I32))
         nc.sync.dma_start(list1[:], offs)
-        nc.sync.dma_start(out=t1_scales[48:64, :].bitcast(I32), in_=tab_scales[0].bitcast(I32))
-        nc.vector.memset(t2_scales[0:96, :].bitcast(I32), 0)
-        nc.vector.memset(t1_scales[0:48, :].bitcast(I32), 0)
-        nc.vector.memset(t1_scales[64:P, :].bitcast(I32), 0)
+        nc.sync.dma_start(out=t1_rows[112:P, :].bitcast(I32), in_=tab_scales[0].bitcast(I32))
+        nc.vector.memset(t2_rows[0:96, :].bitcast(I32), 0)
         nc.vector.memset(r_planes[:].bitcast(I32), 0)
+        nc.vector.memset(t1_rows[0:112, :].bitcast(I32), 0)
+        nc.vector.memset(e_plane[:].bitcast(I32), 0)
         make_identity(nc, ident[:])
-        load_w("rr0")
-        load_w("rr1")
-        load_words(t2_words, tab2_words, (0, T // 2, T))
-        load_w("ri0")
+        raw_rr0 = load_raw("rr0", wrr[0:K, :], RAW_A)
+        raw_rr1 = load_raw("rr1", wrr[K:L, :], RAW_B)
+        nc.sync.dma_start(out=t2_words[:], in_=words_of(tab2_words))
+        raw_ri0 = load_raw("ri0", wri[0:K, :], RAW_C)
 
-        def gather1(s):
-            cols = slice(s * SLICE, (s + 1) * SLICE)
-            nc.vector.tensor_copy(
-                e_words[:, cols], t1_words[:].bitcast(U32).indirect(list1[:, s * SLICE // 16 : (s + 1) * SLICE // 16]))
+        nc.vector.tensor_copy(r_picked[:], t2_rows[:].indirect(list2[:]))
+        nc.vector.tensor_copy(e_picked[:], t1_rows[:].indirect(list1[:]))
+        wb_rr = at("wb_rr", [2 * PACK * R], BF16, CAST_A)
+        cast(wb_rr[:, 0 : PACK * R], raw_rr0[:])
+        cast(wb_rr[:, PACK * R :], raw_rr1[:])
+        quantise_weight("rr", wb_rr[:])
 
-        def gather2(s):
-            nc.vector.tensor_copy(
-                r_pairs[s][:], t2_words[:].bitcast(U32).indirect(list2[:, s * SLICE // 16 : (s + 1) * SLICE // 16]))
+        move_rows(r_planes[:, 0:J], r_picked, 96)
+        raw_ri1 = load_raw("ri1", wri[K:L, :], RAW_D)
+        move_rows(r_planes[:, J:], r_picked, 112)
+        t1_words = at("t1_words", [T], I32, TAB1)
+        nc.sync.dma_start(out=t1_words[:], in_=words_of(tab_words))
+        move_rows(e_plane[:], e_picked, 112)
+        raw_er = load_raw("er", wer, RAW_A)
+        raw_ei = at("raw_ei", [2, PACK, R // 2], F32, RAW_B)
+        for h in range(2):
+            nc.sync.dma_start(out=raw_ei[:, h], in_=rows_of(wei)[:, :, h * R // 2 : (h + 1) * R // 2])
 
-        def part2(s):
+        def offsets(lst, s):
+            return lst[:, s * SLICE // 16 : (s + 1) * SLICE // 16]
+
+        def gather_relation(s, kib):
+            pairs = at("pairs%d" % s, [SLICE], U32, kib)
+            nc.vector.tensor_copy(pairs[:], t2_words[:].bitcast(U32).indirect(offsets(list2, s)))
             nc.vector.tensor_copy(r_words[s][:].bitcast(U16).rearrange("p d (c i) -> p c d i", i=8),
-                                  r_pairs[s][:].bitcast(U16).rearrange("p (c i d) -> p c d i", i=8, d=2))
+                                  pairs[:].bitcast(U16).rearrange("p (c i d) -> p c d i", i=8, d=2))
 
-        cast_w("rr0")
-        cast_w("rr1")
-        nc.vector.tensor_copy(r_picked[:], t2_scales[:].indirect(list2[:]))
+        for s in range(2):
+            gather_relation(s, SMALL + 4 + 2 * s)
+        for i, (n, raw) in enumerate((("ri0", raw_ri0), ("ri1", raw_ri1))):
+            wb = at("wb_" + n, [PACK * R], BF16, CAST_B + 4 * i)
+            cast(wb[:], raw[:])
+            quantise_weight(n, wb[:])
+            gather_relation(2 + i, CAST_B + 4 * i)
 
-        def move_plane(a):
-            for r in range(4):
-                row = 96 + 16 * a
-                nc.sync.dma_start(out=r_planes[r:P:32, a * J : (a + 1) * J].bitcast(I32),
-                                  in_=r_picked[row + r : row + 16 : 4, :].bitcast(I32))
-
-        move_plane(0)
-        load_w("ri1")
-        load_w("er")
-        move_plane(1)
-        nc.vector.tensor_copy(e_picked[:], t1_scales[:].indirect(list1[:]))
-        load_words(t1_words, tab_words, (0, T // 2, T))
-        quant_w("rr0")
-        nc.vector.memset(e_scales[:].bitcast(I32), 0)
-        for r in range(4):
-            nc.sync.dma_start(out=e_scales[8 + r : P : 32, :].bitcast(I32), in_=e_picked[48 + r : 64 : 4, :].bitcast(I32))
-        quant_w("rr1")
-        for h in range(2):
-            nc.sync.dma_start(out=raw_ei[:, h], in_=wei.rearrange("(p j) r -> p j r", j=PACK)[:, :, h * R // 2 : (h + 1) * R // 2])
-        gather2(0)
-        gather2(1)
-        part2(0)
-        cast_w("ri0")
-        quant_w("ri0")
-        part2(1)
-        cast_w("ri1")
-        quant_w("ri1")
-        gather2(2)
-        gather2(3)
-        part2(2)
-        for plane in (nr_s, ni_s):
-            nc.vector.memset(plane[:].bitcast(I32), 0)
-        nc.sync.dma_start(out=nr_w[:], in_=nr_words[0].rearrange("p n i -> p (n i)").bitcast(I32))
+        nr_w = at("nr_w", [N], I32, TAB2)
+        ni_w = at("ni_w", [2 * N], U8, TAB2 + 2)
+        n_planes = at("n_planes", [2 * N], U8, TAB2 + 3)
+        nc.vector.memset(n_planes[:].bitcast(I32), 0)
+        nc.sync.dma_start(out=nr_w[:], in_=words_of(nr_words))
         nc.sync.dma_start(out=ni_w[:].bitcast(I32), in_=ni_words[0].bitcast(I32))
-        load_plane(nr_s, nr_scales[0])
-        load_plane(ni_s, ni_scales[0])
-        cast_w("er")
-        quant_w("er")
-        part2(3)
-        for s in range(J // SLICE):
-            gather1(s)
+        for i, rows in enumerate((nr_scales, ni_scales)):
+            for r in range(4):
+                nc.sync.dma_start(out=n_planes[r:P:32, i * N : (i + 1) * N].bitcast(I32), in_=rows[0][r:16:4, :].bitcast(I32))
+
+        def gather_entity(s):
+            nc.vector.tensor_copy(e_words[s][:], t1_words[:].bitcast(U32).indirect(offsets(list1, s)))
+
+        for s in range(J // SLICE - 1):
+            gather_entity(s)
+        wb_er = at("wb_er", [PACK * R], BF16, CAST_A)
+        wb_ei = at("wb_ei", [PACK * R], BF16, CAST_A + 4)
+        cast(wb_er[:], raw_er[:])
+        quantise_weight("er", wb_er[:])
+        e_words.append(at("e_words3", [SLICE], U32, CAST_A))
+        gather_entity(J // SLICE - 1)
         for h in range(2):
-            nc.scalar.copy(
-                out=wb["ei"][:].rearrange("p (t m j) -> p m j t", t=PACK, j=PACK)[:, h * P // 2 : (h + 1) * P // 2],
-                in_=raw_ei[:, h].rearrange("p j (m t) -> p m j t", t=PACK),
-            )
-        quant_w("ei")
+            nc.scalar.copy(out=wb_ei[:].rearrange("p (t m j) -> p m j t", t=PACK, j=PACK)[:, h * P // 2 : (h + 1) * P // 2],
+                           in_=raw_ei[:, h].rearrange("p j (m t) -> p m j t", t=PACK))
+        quantise_weight("ei", wb_ei[:])
 
-        out_v = out.rearrange("(t p) j -> p t j", p=P)
-        cd, ab, prods = {}, {}, {}
-        h_both = keep.tile([P, 2 * (GROUP + 1) * R], BF16, name="h_both", align_bytes=64)
-
-        def h_slot(k):
-            g, i = divmod(k, GROUP)
-            if g == NBLK // GROUP - 1:
-                return max(GROUP - i, 2)
-            return i if i > 0 else GROUP * (g % 2)
-
-        def tokens(k):
-            g, i = divmod(k, GROUP)
-            if g == NBLK // GROUP - 1:
-                return (g * GROUP + (1 - i if i < 2 else i)) * BLK
-            return (g * GROUP + (i - g % 2) % GROUP) * BLK
-
-        def h_part(c, first, count):
-            at = (c * (GROUP + 1) + first) * R
-            return h_both[:, at : at + count * R]
-
-        def project(bank, passes, k):
+        def project(passes, k, tag):
+            bank = psum.tile([P, R], F32, name="bank", tag=tag)
             last = len(passes) - 1
-            if MODES[k] == "T":
-                for a, (w, codes, scales) in enumerate(passes):
-                    nc.tensor.matmul_mx(out=bank[:], lhsT=codes, lhsT_scale=scales, rhs=wq[w][:].bitcast(FP8X4),
-                                        rhs_scale=ws[w][:], start=(a == 0), stop=(a == last))
+            if k in TURNED:
+                for a, (w_codes, w_scales, tok_codes, tok_scales) in enumerate(passes):
+                    nc.tensor.matmul_mx(out=bank[:], lhsT=tok_codes, lhsT_scale=tok_scales, rhs=w_codes.bitcast(FP8X4),
+                                        rhs_scale=w_scales, start=(a == 0), stop=(a == last))
             else:
                 for t in range(PACK):
                     m = slice(t * P, (t + 1) * P)
-                    for a, (w, codes, scales) in enumerate(passes):
-                        nc.tensor.matmul_mx(out=bank[:, t * BLK : (t + 1) * BLK], lhsT=wq[w][:, m].bitcast(FP8X4),
-                                            lhsT_scale=ws[w][:, m], rhs=codes, rhs_scale=scales,
+                    for a, (w_codes, w_scales, tok_codes, tok_scales) in enumerate(passes):
+                        nc.tensor.matmul_mx(out=bank[:, t * BLK : (t + 1) * BLK], lhsT=w_codes[:, m].bitcast(FP8X4),
+                                            lhsT_scale=w_scales[:, m], rhs=tok_codes, rhs_scale=tok_scales,
                                             start=(a == 0), stop=(a == last))
+            return bank
 
-        def e_passes(n, k):
-            tok = slice(tokens(k), tokens(k) + BLK)
-            return [(n, e_words[:, tok].bitcast(FP8X4), e_scales[8:P, tok])]
+        def entity(n, k):
+            tok = slice(k * BLK, (k + 1) * BLK)
+            return project([(wq[n][:], ws[n][:], e_words[k // GROUP][:, k % GROUP * BLK : (k % GROUP + 1) * BLK].bitcast(FP8X4), e_plane[:, tok])], k, "ab")
 
-        def r_passes(n, k):
-            return [(n + str(a), r_words[k // GROUP][:, a, 2 * (tokens(k) % SLICE) : 2 * (tokens(k) % SLICE + BLK)].bitcast(FP4X4), r_planes[:, a * J + tokens(k) : a * J + tokens(k) + BLK])
-                    for a in range(2)]
+        weights_c = [(wq["rr"][:, a * R : (a + 1) * R], ws["rr"][:, a * R : (a + 1) * R]) for a in range(2)]
+        weights_d = [(wq[n][:], ws[n][:]) for n in ("ri0", "ri1")]
 
-        def inter(bank):
+        def relation(weights, k):
+            s, first = divmod(k * BLK, SLICE)
+            return project([weights[a] + (r_words[s][:, a, 2 * first : 2 * (first + BLK)].bitcast(FP4X4),
+                                          r_planes[:, a * J + k * BLK : a * J + (k + 1) * BLK]) for a in range(2)], k, "out")
+
+        def woven(bank):
             return bank[:].rearrange("p (t n) -> p n t", t=PACK)
 
         def view(bank, k):
-            return bank[:].rearrange("p (n t) -> p n t", t=PACK) if MODES[k] == "T" else inter(bank)
+            return bank[:].rearrange("p (n t) -> p n t", t=PACK) if k in TURNED else woven(bank)
 
         def twice(ap):
             return ap.unsqueeze(1).to_broadcast([P, 2, BLK, PACK])
 
-        order = list(range(1, FIRST)) + [0] + list(range(FIRST, NBLK))
+        def rows_cd(k):
+            return 3 if k in TURNED or k == LAST else 2
 
-        parked = {}
+        cd, cd_at, free = {}, {3: RAW_B - 4, 4: RAW_B + 2}, CD
+        for k in range(NBLK):
+            if k == 3 * GROUP:
+                free = CD
+            if k not in cd_at:
+                cd_at[k] = free
+                free = free + rows_cd(k) * 2
 
-        def banked(passes, k, tag):
-            bank = psum4.tile([P, R], F32, name="bank", tag=tag)
-            project(bank, passes, k)
-            return bank
+        EXTRA = CD + 44
 
-        def relation(k):
-            c_at = (20, 22, 0, 11, 13, 15, 2, 4, 6, 8, 18)[order.index(k) % 11] * 2048
-            cd[k] = stage.tile([P, 2, BLK, PACK], F32, name="cd_sb%d" % k, align_bytes=64, offset=c_at)
-            for c, n in enumerate(("rr", "ri")):
-                bank = parked[n] if k == FIRST else banked(r_passes(n, k), k, "out")
-                nc.scalar.copy(out=cd[k][:, c], in_=view(bank, k))
+        def copy_c(k):
+            cd[k] = at("cd%d" % k, [rows_cd(k), BLK, PACK], F32, cd_at[k])
+            nc.scalar.copy(out=cd[k][:, rows_cd(k) - 2], in_=view(relation(weights_c, k), k))
 
-        def entity(k):
-            a_ps = banked(e_passes("er", k), k, "ab")
-            if k == 0:
-                for n in ("rr", "ri"):
-                    parked[n] = banked(r_passes(n, FIRST), FIRST, "ab")
-            ab[k] = (a_ps, banked(e_passes("ei", k), k, "ab"))
+        def copy_d(k):
+            bank = relation(weights_d, k)
+            nc.scalar.copy(out=cd[k][:, rows_cd(k) - 1], in_=view(bank, k))
+            if rows_cd(k) == 3:
+                nc.scalar.mul(cd[k][:, 0], view(bank, k), -1.0)
 
-        def products(k):
-            a_ps, b_ps = ab[k]
-            cd_sb = cd[k]
-            if k == 0:
-                pa = stage.tile([P, 2, BLK, PACK], F32, name="pa0", align_bytes=64, offset=last + 8 * R)
-            else:
-                pa = work3.tile([P, 2, BLK, PACK], F32, name="pa", align_bytes=64)
-            pb = work3.tile([P, 2, BLK, PACK], F32, name="pb", align_bytes=64)
-            nc.vector.tensor_tensor(pa[:], cd_sb[:], twice(view(a_ps, k)), MULT)
-            if MODES[k] == "T":
-                nc.vector.tensor_tensor(pb[:, 0], cd_sb[:, 0], view(b_ps, k), MULT)
-                nc.vector.scalar_tensor_tensor(pb[:, 1], cd_sb[:, 1], -1.0, view(b_ps, k), MULT, MULT)
-            else:
-                nc.vector.tensor_tensor(pb[:], cd_sb[:], twice(view(b_ps, k)), MULT)
-            prods[k] = (pa, pb)
+        def copy_cd(*blocks):
+            for k in blocks:
+                copy_c(k)
+                copy_d(k)
 
-        def combine(k):
-            pa, pb = prods[k]
-            fa = pa[:].rearrange("p c n t -> p (c n t)")
-            fb = pb[:].rearrange("p c n t -> p (c n t)")
-            if MODES[k] == "T":
-                for c in (1, 0):
-                    h_ps = psum4.tile([P, R], F32, name="h_ps", tag="out")
-                    for t in range(PACK):
-                        cols = slice(c * R + t * P, c * R + (t + 1) * P)
-                        other = slice((1 - c) * R + t * P, (1 - c) * R + (t + 1) * P)
-                        o = h_ps[:, t * BLK : (t + 1) * BLK]
-                        nc.tensor.matmul(o, lhsT=fa[:, cols], rhs=ident[:], is_transpose=True, start=True, stop=False)
-                        nc.tensor.matmul(o, lhsT=fb[:, other], rhs=ident[:], is_transpose=True, start=False, stop=True)
-                    nc.scalar.copy(out=h_part(c, h_slot(k), 1).rearrange("p (n t) -> p n t", t=PACK), in_=inter(h_ps))
-            else:
-                add_half(nc.gpsimd, 0, k)
-                add_half(nc.gpsimd, 1, k)
+        ring = [CAST_A + 4, RAW_C, RAW_D, TAB2 + 4, TAB1, TAB1 + 8, EXTRA, EXTRA + 8, RAW_A, RAW_B]
+        taken = []
 
-        def add_half(eng, c, k):
-            pa, pb = prods[k]
-            eng.tensor_tensor(h_part(c, h_slot(k), 1), pa[:, c].rearrange("p n t -> p (n t)"), pb[:, 1 - c].rearrange("p n t -> p (n t)"), (SUB, ADD)[c])
+        def product_tile(name, kib=None):
+            if kib is None:
+                kib = ring[len(taken) % len(ring)]
+                taken.append(name)
+            return at(name, [2, 2, BLK, PACK], F32, kib)
 
-        def quantise(first, count):
-            width = count * BLK
-            hq = work3.tile([P, 2 * width], U32, name="hq", align_bytes=64)
-            hs = work3.tile([P, 2 * width], U8, name="hs", align_bytes=64)
+        a_bank, b_bank, pa, pb = {}, {}, {}, {}
+
+        def tiles_pair(k, a_at=None, b_at=None):
+            both_a = product_tile("pa%d" % k, a_at)
+            both_b = product_tile("pb%d" % k, b_at)
+            for i in range(2):
+                pa[k + i], pb[k + i] = both_a[:, i], both_b[:, i]
+            pa[k, k + 1], pb[k, k + 1] = both_a, both_b
+
+        def tiles_single(k):
+            both = product_tile("pab%d" % k)
+            pa[k], pb[k] = both[:, 0], both[:, 1]
+
+        def times_a(k):
+            n = rows_cd(k)
+            nc.vector.tensor_tensor(pa[k], cd[k][:, n - 2 : n], twice(view(a_bank[k], k)), MULT)
+
+        def times_b(k):
+            nc.vector.tensor_tensor(pb[k], cd[k][:, 0:2], twice(view(b_bank[k], k)), MULT)
+
+        def times(*blocks):
+            for k in blocks:
+                times_a(k)
+                times_b(k)
+
+        a_sb, a_at = {}, {}
+
+        def copy_a(k):
+            a_at[k] = A_COPY + 2 * len(a_at)
+            a_sb[k] = at("a_sb%d" % k, [BLK, PACK], F32, a_at[k])
+            nc.scalar.copy(out=a_sb[k][:], in_=view(a_bank[k], k))
+
+        def times_a_gpsimd(k):
+            nc.gpsimd.tensor_tensor(pa[k], cd[k][:], twice(a_sb[k][:]), MULT)
+
+        h = {}
+
+        def h_tile(name, first, count, kib):
+            tile = at(name, [2 * count * R], BF16, kib)
+            for i in range(count):
+                h[first + i] = (tile, i, count)
+            return tile
+
+        def h_part(k, c, count=1):
+            tile, i, width = h[k]
+            return tile[:, (c * width + i) * R : (c * width + i + count) * R]
+
+        def sum_pair(k):
+            for c, op in enumerate((SUB, ADD)):
+                nc.gpsimd.tensor_tensor(h_part(k, c, 2).rearrange("p (i x) -> p i x", i=2),
+                                        pa[k, k + 1][:, :, c].rearrange("p i n t -> p i (n t)"),
+                                        pb[k, k + 1][:, :, 1 - c].rearrange("p i n t -> p i (n t)"), op)
+
+        def sum_turned(k):
             for c in range(2):
-                cols = slice(c * width, (c + 1) * width)
-                nc.vector.quantize_mx(out=hq[:, cols].bitcast(FP8X4), scales=hs[:, cols], in_=h_part(c, first, count))
+                bank = psum.tile([P, R], F32, name="bank", tag="out")
+                terms = [p[k][:, c].rearrange("p n t -> p (n t)") for p in (pb, pa)]
+                for t in range(PACK):
+                    for i, term in enumerate(terms):
+                        nc.tensor.matmul(bank[:, t * BLK : (t + 1) * BLK], lhsT=term[:, t * P : (t + 1) * P], rhs=ident[:],
+                                         is_transpose=True, start=(i == 0), stop=(i == 1))
+                nc.scalar.copy(out=h_part(k, c).rearrange("p (n t) -> p n t", t=PACK), in_=woven(bank))
+
+        def quantise(tile, count, scales_at=None):
+            hq = codes.tile([P, 2 * count * BLK], U32, name="hq", align_bytes=64)
+            if scales_at is None:
+                hs = codes.tile([P, 2 * count * BLK], U8, name="hs", align_bytes=64)
+            else:
+                hs = at("hs_held", [2 * count * BLK], U8, scales_at)
+            nc.vector.quantize_mx(out=hq[:].bitcast(FP8X4), scales=hs[:], in_=tile[:])
             return hq, hs
 
-        def score_passes(o, t, hq, hs, width, at, n):
-            m = slice(t * P, (t + 1) * P)
-            re = slice(at, at + n)
-            im = slice(width + at, width + at + n)
-            nc.tensor.matmul_mx(out=o, lhsT=nr_w[:, m].bitcast(FP8X4), lhsT_scale=nr_s[:, m],
-                                rhs=hq[:, re].bitcast(FP8X4), rhs_scale=hs[:, re], start=True, stop=False)
-            nc.tensor.matmul_mx(out=o, lhsT=ni_w[:, 2 * t * P : 2 * (t + 1) * P].bitcast(FP4X4), lhsT_scale=ni_s[:, m],
-                                rhs=hq[:, im].bitcast(FP8X4), rhs_scale=hs[:, im],
-                                start=False, stop=True)
+        out_v = out.rearrange("(t p) j -> p t j", p=P)
+        staged = []
 
-        def score_group(g):
-            width = GROUP * BLK
-            hq, hs = quantise(g % 2, GROUP)
-            for t in range(N // P):
-                y_ps = psum4.tile([P, width], F32, name="y_ps", tag="out")
-                score_passes(y_ps[:], t, hq, hs, width, 0, width)
-                y = work4.tile([P, width], F32, name="y")
-                nc.scalar.copy(out=y[:], in_=y_ps[:])
-                nc.sync.dma_start(out=out[t * P : (t + 1) * P, g * width : (g + 1) * width], in_=y[:])
+        def score(quantised, first, count, per_bank, copies=None):
+            hq, hs = quantised
+            width = count * BLK
+            for b in range(N // P // per_bank):
+                bank = psum.tile([P, per_bank * width], F32, name="bank", tag="out")
+                for i in range(per_bank):
+                    t = b * per_bank + i
+                    o = bank[:, i * width : (i + 1) * width]
+                    nc.tensor.matmul_mx(out=o, lhsT=nr_w[:, t * P : (t + 1) * P].bitcast(FP8X4), lhsT_scale=n_planes[:, t * P : (t + 1) * P],
+                                        rhs=hq[:, 0:width].bitcast(FP8X4), rhs_scale=hs[:, 0:width], start=True, stop=False)
+                    nc.tensor.matmul_mx(out=o, lhsT=ni_w[:, 2 * t * P : 2 * (t + 1) * P].bitcast(FP4X4),
+                                        lhsT_scale=n_planes[:, N + t * P : N + (t + 1) * P],
+                                        rhs=hq[:, width:].bitcast(FP8X4), rhs_scale=hs[:, width:], start=False, stop=True)
+                if copies is None:
+                    y = at("y%d" % len(staged), [per_bank * width], F32, (SMALL, EXTRA + 16)[len(staged) // 4 % 2] + 2 * (len(staged) % 4))
+                    nc.scalar.copy(out=y[:], in_=bank[:])
+                else:
+                    y = at("y%d" % len(staged), [per_bank * width], F32, TAB2 + 12 + b)
+                    copies[b](y[:], bank[:])
+                staged.append(y)
+                nc.sync.dma_start(out=out_v[:, b * per_bank : (b + 1) * per_bank, first * BLK : first * BLK + width],
+                                  in_=y[:].rearrange("p (t n) -> p t n", t=per_bank))
 
-        def score_block(k):
-            hq, hs = quantise(h_slot(k), 1)
-            y_ps = psum4.tile([P, PACK * BLK], F32, name="y_ps", tag="out")
-            for t in range(N // P):
-                score_passes(y_ps[:, t * BLK : (t + 1) * BLK], t, hq, hs, BLK, 0, BLK)
-            y = work4.tile([P, N // P * BLK], F32, name="y")
-            nc.scalar.copy(out=y[:], in_=y_ps[:])
-            nc.sync.dma_start(out=out_v[:, :, tokens(k) : tokens(k) + BLK], in_=y[:].rearrange("p (t n) -> p t n", n=BLK))
+        def pass_a(*blocks):
+            for k in blocks:
+                a_bank[k] = entity("er", k)
 
-        def score_pair(k):
-            hq, hs = quantise(h_slot(k), 2)
-            for half in range(2):
-                y_ps = psum4.tile([P, PACK * BLK], F32, name="y_ps", tag="out")
-                for i in range(PACK):
-                    score_passes(y_ps[:, i * BLK : (i + 1) * BLK], 2 * half + i // 2, hq, hs, 2 * BLK, i % 2 * BLK, BLK)
-                y = work4.tile([P, PACK * BLK], F32, name="y")
-                nc.scalar.copy(out=y[:], in_=y_ps[:])
-                nc.sync.dma_start(out=out_v[:, 2 * half : 2 * half + 2, tokens(k) : tokens(k) + 2 * BLK],
-                                  in_=y[:].rearrange("p (t n) -> p t n", t=2))
+        def pass_b(*blocks):
+            for k in blocks:
+                b_bank[k] = entity("ei", k)
 
-        def score_last(k):
-            hq, hs = quantise(h_slot(k), 1)
-            for half, copy in enumerate((nc.scalar.copy, nc.vector.tensor_copy)):
-                y_ps = psum4.tile([P, 2 * BLK], F32, name="y_ps", tag="out")
-                for t in range(2):
-                    score_passes(y_ps[:, t * BLK : (t + 1) * BLK], 2 * half + t, hq, hs, BLK, 0, BLK)
-                y = work4.tile([P, 2 * BLK], F32, name="y")
-                copy(y[:], y_ps[:])
-                nc.sync.dma_start(out=out_v[:, 2 * half : 2 * half + 2, tokens(k) : tokens(k) + BLK],
-                                  in_=y[:].rearrange("p (t n) -> p t n", n=BLK))
-
-        for k in order[:FIRST]:
-            relation(k)
-        for k in range(NBLK):
-            entity(k)
-        for k in order[FIRST:LEAD]:
-            relation(k)
-        steps = [k for k in range(NBLK) if k < GROUP or k % GROUP > 1][: NBLK - LEAD]
-        for k in range(NBLK):
-            products(k)
-            if k % GROUP == 1 and k > GROUP:
-                score_group(k // GROUP - 1)
-            if k in steps:
-                relation(LEAD + steps.index(k))
-            if MODES[k] == "V":
-                score_block(k - 1)
-                add_half(nc.vector, 0, k)
-                add_half(nc.vector, 1, k)
-            else:
-                combine(k)
-            if k == NBLK - 2:
-                score_pair(k - 1)
-        score_last(NBLK - 1)
+        for k in range(3):
+            copy_c(k)
+        for k in (2, 0, 1):
+            copy_d(k)
+        pass_a(0, 1, 2, 4)
+        h0 = h_tile("h0", 0, GROUP, H_A)
+        tiles_pair(0)
+        tiles_single(2)
+        tiles_single(3)
+        tiles_pair(4)
+        for k in range(2):
+            copy_a(k)
+            times_a_gpsimd(k)
+        pass_b(2)
+        pass_a(3)
+        copy_cd(3)
+        copy_a(4)
+        pass_b(3)
+        copy_cd(4)
+        times_a_gpsimd(4)
+        times_a(2)
+        pass_b(0)
+        times_b(2)
+        pass_b(1)
+        copy_cd(5)
+        sum_turned(2)
+        times_a(3)
+        pass_a(5)
+        times_b(3)
+        pass_b(4)
+        copy_cd(6)
+        sum_turned(3)
+        times_b(0)
+        pass_b(5)
+        times_b(1)
+        pass_a(6)
+        sum_pair(0)
+        copy_cd(7)
+        times_a(5)
+        pass_a(7)
+        times_b(4)
+        pass_b(6)
+        copy_cd(8)
+        times_b(5)
+        pass_b(7)
+        copy_cd(9)
+        tiles_pair(6)
+        times_a(6)
+        pass_a(8)
+        q0 = quantise(h0, GROUP)
+        h1 = h_tile("h1", GROUP, GROUP, H_A)
+        sum_pair(4)
+        copy_cd(10)
+        times_a(7)
+        pass_a(9)
+        times_b(6)
+        pass_b(8)
+        copy_cd(11)
+        times_b(7)
+        pass_b(9)
+        sum_pair(6)
+        score(q0, 0, GROUP, 1)
+        tiles_pair(8)
+        copy_cd(12)
+        times_a(8)
+        pass_a(12)
+        times_a(9)
+        pass_b(12)
+        times_b(8)
+        pass_a(10)
+        times_b(9)
+        pass_b(10)
+        copy_cd(13)
+        h12 = h_tile("h12", 12, 2, H_B)
+        h14 = h_tile("h14", 14, 1, H_B + 4)
+        h15 = h_tile("h15", 15, 1, H_B + 6)
+        tiles_single(12)
+        times_a(12)
+        pass_a(11)
+        q1 = quantise(h1, GROUP)
+        h2 = h_tile("h2", 2 * GROUP, GROUP, H_A)
+        sum_pair(8)
+        times_b(12)
+        pass_b(11)
+        sum_turned(12)
+        copy_cd(14)
+        tiles_pair(10)
+        times_a(10)
+        pass_a(13)
+        times_b(10)
+        pass_b(13)
+        score(q1, GROUP, GROUP, 1)
+        times_a(11)
+        pass_a(14)
+        times_b(11)
+        pass_b(14)
+        sum_pair(10)
+        copy_cd(15)
+        tiles_single(13)
+        times_a(13)
+        pass_a(15)
+        times_b(13)
+        pass_b(15)
+        sum_turned(13)
+        tiles_single(14)
+        times_a(14)
+        q2 = quantise(h2, GROUP)
+        times_b(14)
+        sum_turned(14)
+        q12 = quantise(h12, 2)
+        score(q2, 2 * GROUP, GROUP, 1)
+        score(q12, 12, 2, 2)
+        tiles_single(LAST)
+        times(LAST)
+        nc.vector.tensor_tensor(h15[:], pa[LAST].rearrange("p c n t -> p (c n t)"), pb[LAST].rearrange("p c n t -> p (c n t)"), ADD)
+        q14 = quantise(h14, 1)
+        q15 = quantise(h15, 1)
+        score(q14, 14, 1, 4)
+        score(q15, LAST, 1, 2, (nc.scalar.copy, nc.vector.tensor_copy))

@@ -25,7 +25,7 @@ NBLK = J // BLK
 SLICE = 512
 GROUP = 4
 KIB = 1024
-TURNED = (2, 3, 12, 13, 14)
+TURNED = (2, 3, 10, 11, 14)
 LAST = NBLK - 1
 
 
@@ -97,8 +97,8 @@ def tile_list_ckg_none_kernel(
         make_identity(nc, ident[:])
         raw_rr0 = load_raw("rr0", wrr[0:K, :], RAW_A)
         raw_rr1 = load_raw("rr1", wrr[K:L, :], RAW_B)
-        nc.sync.dma_start(out=t2_words[:], in_=words_of(tab2_words))
         raw_ri0 = load_raw("ri0", wri[0:K, :], RAW_C)
+        nc.sync.dma_start(out=t2_words[:], in_=words_of(tab2_words))
 
         nc.vector.tensor_copy(r_picked[:], t2_rows[:].indirect(list2[:]))
         nc.vector.tensor_copy(e_picked[:], t1_rows[:].indirect(list1[:]))
@@ -127,17 +127,19 @@ def tile_list_ckg_none_kernel(
             nc.vector.tensor_copy(r_words[s][:].bitcast(U16).rearrange("p d (c i) -> p c d i", i=8),
                                   pairs[:].bitcast(U16).rearrange("p (c i d) -> p c d i", i=8, d=2))
 
-        for s in range(2):
-            gather_relation(s, SMALL + 4 + 2 * s)
-        for i, (n, raw) in enumerate((("ri0", raw_ri0), ("ri1", raw_ri1))):
-            wb = at("wb_" + n, [PACK * R], BF16, CAST_B + 4 * i)
-            cast(wb[:], raw[:])
-            quantise_weight(n, wb[:])
-            gather_relation(2 + i, CAST_B + 4 * i)
+        wb_ri0 = at("wb_ri0", [PACK * R], BF16, CAST_B)
+        wb_ri1 = at("wb_ri1", [PACK * R], BF16, CAST_B + 4)
+        cast(wb_ri0[:], raw_ri0[:])
+        quantise_weight("ri0", wb_ri0[:])
+        for s in range(3):
+            gather_relation(s, SMALL + 4 + 2 * (s // 2))
+        cast(wb_ri1[:], raw_ri1[:])
+        quantise_weight("ri1", wb_ri1[:])
+        gather_relation(3, CAST_B + 4)
 
-        nr_w = at("nr_w", [N], I32, TAB2)
-        ni_w = at("ni_w", [2 * N], U8, TAB2 + 2)
-        n_planes = at("n_planes", [2 * N], U8, TAB2 + 3)
+        nr_w = at("nr_w", [N], I32, RAW_D + 3)
+        ni_w = at("ni_w", [2 * N], U8, RAW_D + 5)
+        n_planes = at("n_planes", [2 * N], U8, RAW_D + 6)
         nc.vector.memset(n_planes[:].bitcast(I32), 0)
         nc.sync.dma_start(out=nr_w[:], in_=words_of(nr_words))
         nc.sync.dma_start(out=ni_w[:].bitcast(I32), in_=ni_words[0].bitcast(I32))
@@ -150,11 +152,12 @@ def tile_list_ckg_none_kernel(
 
         for s in range(J // SLICE - 1):
             gather_entity(s)
-        wb_er = at("wb_er", [PACK * R], BF16, CAST_A)
+        wb_er = at("wb_er", [PACK * R], BF16, CAST_B + 4)
         wb_ei = at("wb_ei", [PACK * R], BF16, CAST_A + 4)
-        cast(wb_er[:], raw_er[:])
+        nc.gpsimd.tensor_scalar(wb_er[:].rearrange("p (t m j) -> p t m j", t=PACK, j=PACK),
+                                raw_er[:].rearrange("p j (m t) -> p t m j", t=PACK), 1.0, 0.0, MULT, ADD)
         quantise_weight("er", wb_er[:])
-        e_words.append(at("e_words3", [SLICE], U32, CAST_A))
+        e_words.append(at("e_words3", [SLICE], U32, CAST_B + 4))
         gather_entity(J // SLICE - 1)
         for h in range(2):
             nc.scalar.copy(out=wb_ei[:].rearrange("p (t m j) -> p m j t", t=PACK, j=PACK)[:, h * P // 2 : (h + 1) * P // 2],
@@ -199,9 +202,9 @@ def tile_list_ckg_none_kernel(
             return ap.unsqueeze(1).to_broadcast([P, 2, BLK, PACK])
 
         def rows_cd(k):
-            return 3 if k in TURNED or k == LAST else 2
+            return 3 if k >= GROUP and (k in TURNED or k == LAST) else 2
 
-        cd, cd_at, free = {}, {3: RAW_B - 4, 4: RAW_B + 2}, CD
+        cd, cd_at, free = {}, {6: RAW_B - 3, 7: RAW_B + 7}, CD
         for k in range(NBLK):
             if k == 3 * GROUP:
                 free = CD
@@ -226,13 +229,14 @@ def tile_list_ckg_none_kernel(
                 copy_c(k)
                 copy_d(k)
 
-        ring = [CAST_A + 4, RAW_C, RAW_D, TAB2 + 4, TAB1, TAB1 + 8, EXTRA, EXTRA + 8, RAW_A, RAW_B]
-        taken = []
+        ring = [CAST_A + 4, RAW_C + 3, TAB1, TAB1 + 8, TAB2, TAB2 + 8, EXTRA, EXTRA + 8, RAW_A, RAW_B]
+        taken, placed = [], {}
 
         def product_tile(name, kib=None):
             if kib is None:
                 kib = ring[len(taken) % len(ring)]
                 taken.append(name)
+            placed[name] = kib
             return at(name, [2, 2, BLK, PACK], F32, kib)
 
         a_bank, b_bank, pa, pb = {}, {}, {}, {}
@@ -253,7 +257,12 @@ def tile_list_ckg_none_kernel(
             nc.vector.tensor_tensor(pa[k], cd[k][:, n - 2 : n], twice(view(a_bank[k], k)), MULT)
 
         def times_b(k):
-            nc.vector.tensor_tensor(pb[k], cd[k][:, 0:2], twice(view(b_bank[k], k)), MULT)
+            if k in TURNED and rows_cd(k) == 2:
+                flat = lambda ap: ap.rearrange("p n t -> p (n t)")
+                nc.vector.scalar_tensor_tensor(flat(pb[k][:, 0]), flat(cd[k][:, 1]), -1.0, b_bank[k][:], MULT, MULT)
+                nc.vector.tensor_tensor(flat(pb[k][:, 1]), flat(cd[k][:, 0]), b_bank[k][:], MULT)
+            else:
+                nc.vector.tensor_tensor(pb[k], cd[k][:, 0:2], twice(view(b_bank[k], k)), MULT)
 
         def times(*blocks):
             for k in blocks:
@@ -263,7 +272,7 @@ def tile_list_ckg_none_kernel(
         a_sb, a_at = {}, {}
 
         def copy_a(k):
-            a_at[k] = A_COPY + 2 * len(a_at)
+            a_at[k] = RAW_B + 1 + 2 * len(a_at)
             a_sb[k] = at("a_sb%d" % k, [BLK, PACK], F32, a_at[k])
             nc.scalar.copy(out=a_sb[k][:], in_=view(a_bank[k], k))
 
@@ -327,7 +336,7 @@ def tile_list_ckg_none_kernel(
                     y = at("y%d" % len(staged), [per_bank * width], F32, (SMALL, EXTRA + 16)[len(staged) // 4 % 2] + 2 * (len(staged) % 4))
                     nc.scalar.copy(out=y[:], in_=bank[:])
                 else:
-                    y = at("y%d" % len(staged), [per_bank * width], F32, TAB2 + 12 + b)
+                    y = at("y%d" % len(staged), [per_bank * width], F32, CAST_B + 6 + b)
                     copies[b](y[:], bank[:])
                 staged.append(y)
                 nc.sync.dma_start(out=out_v[:, b * per_bank : (b + 1) * per_bank, first * BLK : first * BLK + width],
@@ -341,122 +350,118 @@ def tile_list_ckg_none_kernel(
             for k in blocks:
                 b_bank[k] = entity("ei", k)
 
-        for k in range(3):
+        for k in range(GROUP):
             copy_c(k)
-        for k in (2, 0, 1):
+        for k in (2, 0, 1, 3):
             copy_d(k)
+        copy_cd(4, 5)
         pass_a(0, 1, 2, 4)
         h0 = h_tile("h0", 0, GROUP, H_A)
         tiles_pair(0)
         tiles_single(2)
         tiles_single(3)
         tiles_pair(4)
-        for k in range(2):
+        for k in (0, 1):
             copy_a(k)
             times_a_gpsimd(k)
-        pass_b(2)
-        pass_a(3)
-        copy_cd(3)
         copy_a(4)
-        pass_b(3)
-        copy_cd(4)
-        times_a_gpsimd(4)
+        nc.gpsimd.tensor_tensor(pa[4][:, 0], cd[4][:, 0], a_sb[4][:], MULT)
+        pass_b(2, 0, 1)
+        pass_a(3)
+        copy_cd(6, 7)
         times_a(2)
-        pass_b(0)
+        nc.vector.tensor_tensor(pa[4][:, 1], cd[4][:, 1], view(a_bank[4], 4), MULT)
         times_b(2)
-        pass_b(1)
-        copy_cd(5)
+        pass_b(3)
+        copy_cd(8)
         sum_turned(2)
-        times_a(3)
-        pass_a(5)
-        times_b(3)
-        pass_b(4)
-        copy_cd(6)
-        sum_turned(3)
         times_b(0)
-        pass_b(5)
+        pass_a(5)
         times_b(1)
-        pass_a(6)
+        pass_b(4)
         sum_pair(0)
-        copy_cd(7)
+        times_a(3)
+        pass_b(5)
+        copy_cd(9)
+        times_b(3)
+        pass_a(6)
+        sum_turned(3)
         times_a(5)
         pass_a(7)
         times_b(4)
         pass_b(6)
-        copy_cd(8)
         times_b(5)
         pass_b(7)
-        copy_cd(9)
+        copy_cd(10)
         tiles_pair(6)
         times_a(6)
         pass_a(8)
         q0 = quantise(h0, GROUP)
         h1 = h_tile("h1", GROUP, GROUP, H_A)
         sum_pair(4)
-        copy_cd(10)
+        copy_cd(11)
         times_a(7)
         pass_a(9)
         times_b(6)
         pass_b(8)
-        copy_cd(11)
+        copy_cd(12)
         times_b(7)
         pass_b(9)
         sum_pair(6)
-        score(q0, 0, GROUP, 1)
-        tiles_pair(8)
-        copy_cd(12)
-        times_a(8)
-        pass_a(12)
-        times_a(9)
-        pass_b(12)
-        times_b(8)
-        pass_a(10)
-        times_b(9)
-        pass_b(10)
         copy_cd(13)
-        h12 = h_tile("h12", 12, 2, H_B)
-        h14 = h_tile("h14", 14, 1, H_B + 4)
-        h15 = h_tile("h15", 15, 1, H_B + 6)
-        tiles_single(12)
-        times_a(12)
-        pass_a(11)
+        tiles_pair(8)
+        times_a(8)
+        pass_a(10)
+        times_a(9)
+        pass_b(10)
+        times_b(8)
+        pass_a(12)
+        times_b(9)
+        pass_a(13)
+        score(q0, 0, GROUP, 1)
+        copy_cd(14)
+        tiles_single(10)
+        times_a(10)
+        pass_b(12)
+        times_b(10)
+        pass_b(13)
         q1 = quantise(h1, GROUP)
         h2 = h_tile("h2", 2 * GROUP, GROUP, H_A)
         sum_pair(8)
-        times_b(12)
-        pass_b(11)
-        sum_turned(12)
-        copy_cd(14)
-        tiles_pair(10)
-        times_a(10)
-        pass_a(13)
-        times_b(10)
-        pass_b(13)
-        score(q1, GROUP, GROUP, 1)
-        times_a(11)
-        pass_a(14)
-        times_b(11)
-        pass_b(14)
-        sum_pair(10)
+        sum_turned(10)
         copy_cd(15)
-        tiles_single(13)
+        h12 = h_tile("h12", 12, 2, H_B)
+        h14 = h_tile("h14", 14, 1, H_B + 4)
+        h15 = h_tile("h15", 15, 1, H_B + 6)
+        tiles_pair(12)
+        times_a(12)
+        pass_a(11)
         times_a(13)
-        pass_a(15)
+        pass_b(11)
+        score(q1, GROUP, GROUP, 1)
+        times_b(12)
+        pass_a(14)
         times_b(13)
+        pass_b(14)
+        sum_pair(12)
+        tiles_single(11)
+        times_a(11)
+        pass_a(15)
+        times_b(11)
         pass_b(15)
-        sum_turned(13)
+        sum_turned(11)
         tiles_single(14)
-        times_a(14)
-        q2 = quantise(h2, GROUP)
-        times_b(14)
+        times(14)
         sum_turned(14)
+        tiles_single(LAST)
+        times_a(LAST)
+        q2 = quantise(h2, GROUP, placed["pb12"])
         q12 = quantise(h12, 2)
         score(q2, 2 * GROUP, GROUP, 1)
         score(q12, 12, 2, 2)
-        tiles_single(LAST)
-        times(LAST)
-        nc.vector.tensor_tensor(h15[:], pa[LAST].rearrange("p c n t -> p (c n t)"), pb[LAST].rearrange("p c n t -> p (c n t)"), ADD)
+        times_b(LAST)
         q14 = quantise(h14, 1)
-        q15 = quantise(h15, 1)
         score(q14, 14, 1, 4)
+        nc.vector.tensor_tensor(h15[:], pa[LAST].rearrange("p c n t -> p (c n t)"), pb[LAST].rearrange("p c n t -> p (c n t)"), ADD)
+        q15 = quantise(h15, 1)
         score(q15, LAST, 1, 2, (nc.scalar.copy, nc.vector.tensor_copy))

@@ -25,7 +25,8 @@ NBLK = J // BLK
 SLICE = 512
 GROUP = 4
 KIB = 1024
-TURNED = (2, 3, 10, 11, 14)
+TURNED = (2, 3, 10, 11)
+WIDE = (4, 6, 8, 12, 14)
 LAST = NBLK - 1
 
 
@@ -37,7 +38,7 @@ def tile_list_ckg_none_kernel(
     with ExitStack() as ctx:
         keep = ctx.enter_context(tc.tile_pool(name="keep", bufs=1))
         arena = ctx.enter_context(tc.tile_pool(name="arena", bufs=1))
-        codes = ctx.enter_context(tc.tile_pool(name="codes", bufs=4))
+        codes = ctx.enter_context(tc.tile_pool(name="codes", bufs=3))
         psum = ctx.enter_context(tc.psum_pool(name="psum", bufs=4))
 
         def at(name, shape, dtype, kib):
@@ -49,20 +50,20 @@ def tile_list_ckg_none_kernel(
         list1 = keep.tile([P, J // 16], U16, name="list1")
         list2 = keep.tile([P, J // 16], U16, name="list2")
         ident = held("ident", [P], F32)
-        e_words = [held("e_words%d" % s, [SLICE], U32) for s in range(J // SLICE - 1)]
+        e_words = [held("e_words%d" % s, [SLICE], U32) for s in range(J // SLICE)]
         e_plane = held("e_plane", [J], U8)
         r_planes = held("r_planes", [2 * J], U8)
         r_words = [held("r_words%d" % s, [2, 2 * SLICE], U8) for s in range(J // SLICE)]
         wq = {n: held("wq_" + n, [w], U32) for n, w in (("rr", 2 * R), ("ri0", R), ("ri1", R), ("er", R), ("ei", R))}
         ws = {n: held("ws_" + n, [w], U8) for n, w in (("rr", 2 * R), ("ri0", R), ("ri1", R), ("er", R), ("ei", R))}
 
-        RAW_A, RAW_B, RAW_C, RAW_D, TAB1, TAB2, CAST_A, CAST_B, SMALL, H_A, H_B, A_COPY, CD = 0, 8, 16, 24, 32, 48, 64, 72, 80, 88, 96, 104, 110
+        RAW_A, RAW_B, RAW_C, RAW_D, TAB2, TAB1, CAST_A, CAST_B, SMALL, H_A, H_B, H_C, CD = 0, 8, 16, 24, 32, 48, 64, 72, 80, 88, 96, 104, 112
 
         t2_rows = at("t2_rows", [T], U8, RAW_D)
+        t2_words = at("t2_words", [T], I32, TAB2)
         t1_rows = at("t1_rows", [T], U8, TAB1)
         r_picked = at("r_picked", [J], U8, SMALL)
         e_picked = at("e_picked", [J], U8, SMALL + 2)
-        t2_words = at("t2_words", [T], I32, TAB2)
 
         def rows_of(w):
             return w.rearrange("(p j) r -> p j r", j=PACK)
@@ -110,10 +111,10 @@ def tile_list_ckg_none_kernel(
         move_rows(r_planes[:, 0:J], r_picked, 96)
         raw_ri1 = load_raw("ri1", wri[K:L, :], RAW_D)
         move_rows(r_planes[:, J:], r_picked, 112)
+        raw_er = load_raw("er", wer, RAW_A)
         t1_words = at("t1_words", [T], I32, TAB1)
         nc.sync.dma_start(out=t1_words[:], in_=words_of(tab_words))
         move_rows(e_plane[:], e_picked, 112)
-        raw_er = load_raw("er", wer, RAW_A)
         raw_ei = at("raw_ei", [2, PACK, R // 2], F32, RAW_B)
         for h in range(2):
             nc.sync.dma_start(out=raw_ei[:, h], in_=rows_of(wei)[:, :, h * R // 2 : (h + 1) * R // 2])
@@ -131,11 +132,11 @@ def tile_list_ckg_none_kernel(
         wb_ri1 = at("wb_ri1", [PACK * R], BF16, CAST_B + 4)
         cast(wb_ri0[:], raw_ri0[:])
         quantise_weight("ri0", wb_ri0[:])
-        for s in range(3):
-            gather_relation(s, SMALL + 4 + 2 * (s // 2))
+        for s, kib in ((0, SMALL + 4), (2, SMALL + 6), (3, CAST_B)):
+            gather_relation(s, kib)
         cast(wb_ri1[:], raw_ri1[:])
         quantise_weight("ri1", wb_ri1[:])
-        gather_relation(3, CAST_B + 4)
+        gather_relation(1, CAST_B + 4)
 
         nr_w = at("nr_w", [N], I32, RAW_D + 3)
         ni_w = at("ni_w", [2 * N], U8, RAW_D + 5)
@@ -150,15 +151,12 @@ def tile_list_ckg_none_kernel(
         def gather_entity(s):
             nc.vector.tensor_copy(e_words[s][:], t1_words[:].bitcast(U32).indirect(offsets(list1, s)))
 
-        for s in range(J // SLICE - 1):
-            gather_entity(s)
-        wb_er = at("wb_er", [PACK * R], BF16, CAST_B + 4)
-        wb_ei = at("wb_ei", [PACK * R], BF16, CAST_A + 4)
-        nc.gpsimd.tensor_scalar(wb_er[:].rearrange("p (t m j) -> p t m j", t=PACK, j=PACK),
-                                raw_er[:].rearrange("p j (m t) -> p t m j", t=PACK), 1.0, 0.0, MULT, ADD)
+        wb_er = at("wb_er", [PACK * R], BF16, CAST_A)
+        wb_ei = at("wb_ei", [PACK * R], BF16, CAST_B)
+        cast(wb_er[:], raw_er[:])
         quantise_weight("er", wb_er[:])
-        e_words.append(at("e_words3", [SLICE], U32, CAST_B + 4))
-        gather_entity(J // SLICE - 1)
+        for s in range(J // SLICE):
+            gather_entity(s)
         for h in range(2):
             nc.scalar.copy(out=wb_ei[:].rearrange("p (t m j) -> p m j t", t=PACK, j=PACK)[:, h * P // 2 : (h + 1) * P // 2],
                            in_=raw_ei[:, h].rearrange("p j (m t) -> p m j t", t=PACK))
@@ -202,67 +200,88 @@ def tile_list_ckg_none_kernel(
             return ap.unsqueeze(1).to_broadcast([P, 2, BLK, PACK])
 
         def rows_cd(k):
-            return 3 if k >= GROUP and (k in TURNED or k == LAST) else 2
+            return 3 if k >= NBLK - 2 else 2
 
-        cd, cd_at, free = {}, {6: RAW_B - 3, 7: RAW_B + 7}, CD
+        cd, cd_pair, cd_at, free = {}, {}, {2: RAW_A, 0: RAW_A + 4, 4: RAW_B + 7}, CD
         for k in range(NBLK):
             if k == 3 * GROUP:
-                free = CD
-            if k not in cd_at:
+                free = CD + 4
+            if k not in cd_at and k - 1 not in WIDE:
                 cd_at[k] = free
-                free = free + rows_cd(k) * 2
+                free = free + rows_cd(k) * (4 if k in WIDE else 2)
+        EXTRA = CD + 32
 
-        EXTRA = CD + 44
+        def split(ap):
+            return ap.rearrange("p c n (u v) -> p c n u v", v=2)
 
         def copy_c(k):
-            cd[k] = at("cd%d" % k, [rows_cd(k), BLK, PACK], F32, cd_at[k])
-            nc.scalar.copy(out=cd[k][:, rows_cd(k) - 2], in_=view(relation(weights_c, k), k))
+            tile = at("cd%d" % k, [rows_cd(k), BLK, PACK], F32, cd_at[k])
+            cd[k] = split(tile[:])
+            nc.scalar.copy(out=tile[:, rows_cd(k) - 2], in_=view(relation(weights_c, k), k))
+            cd_pair[k] = tile
 
         def copy_d(k):
             bank = relation(weights_d, k)
-            nc.scalar.copy(out=cd[k][:, rows_cd(k) - 1], in_=view(bank, k))
+            nc.scalar.copy(out=cd_pair[k][:, rows_cd(k) - 1], in_=view(bank, k))
             if rows_cd(k) == 3:
-                nc.scalar.mul(cd[k][:, 0], view(bank, k), -1.0)
+                nc.scalar.mul(cd_pair[k][:, 0], view(bank, k), -1.0)
+
+        def copy_wide(k):
+            rows = rows_cd(k)
+            tile = at("cd%d" % k, [2, 2, rows, BLK, 2], F32, cd_at[k])
+            s, first = divmod(k * BLK, SLICE)
+            for c, weights in enumerate((weights_c, weights_d)):
+                for u in range(2):
+                    bank = psum.tile([P, R], F32, name="bank", tag="out")
+                    for v in range(2):
+                        m = slice((2 * u + v) * P, (2 * u + v + 1) * P)
+                        for a, (w_codes, w_scales) in enumerate(weights):
+                            nc.tensor.matmul_mx(out=bank[:, v * 2 * BLK : (v + 1) * 2 * BLK], lhsT=w_codes[:, m].bitcast(FP8X4),
+                                                lhsT_scale=w_scales[:, m],
+                                                rhs=r_words[s][:, a, 2 * first : 2 * (first + 2 * BLK)].bitcast(FP4X4),
+                                                rhs_scale=r_planes[:, a * J + k * BLK : a * J + (k + 2) * BLK],
+                                                start=(a == 0), stop=(a == 1))
+                    sums = bank[:].rearrange("p (v i n) -> p i n v", v=2, i=2)
+                    nc.scalar.copy(out=tile[:, u, :, rows - 2 + c], in_=sums)
+                    if c == 1 and rows == 3:
+                        nc.scalar.mul(tile[:, u, :, 0], sums, -1.0)
+            for i in range(2):
+                cd[k + i] = tile[:, :, i].rearrange("p u c n v -> p c n u v")
 
         def copy_cd(*blocks):
             for k in blocks:
-                copy_c(k)
-                copy_d(k)
-
-        ring = [CAST_A + 4, RAW_C + 3, TAB1, TAB1 + 8, TAB2, TAB2 + 8, EXTRA, EXTRA + 8, RAW_A, RAW_B]
-        taken, placed = [], {}
-
-        def product_tile(name, kib=None):
-            if kib is None:
-                kib = ring[len(taken) % len(ring)]
-                taken.append(name)
-            placed[name] = kib
-            return at(name, [2, 2, BLK, PACK], F32, kib)
+                if k in WIDE:
+                    copy_wide(k)
+                else:
+                    copy_c(k)
+                    copy_d(k)
 
         a_bank, b_bank, pa, pb = {}, {}, {}, {}
 
-        def tiles_pair(k, a_at=None, b_at=None):
-            both_a = product_tile("pa%d" % k, a_at)
-            both_b = product_tile("pb%d" % k, b_at)
-            for i in range(2):
-                pa[k + i], pb[k + i] = both_a[:, i], both_b[:, i]
-            pa[k, k + 1], pb[k, k + 1] = both_a, both_b
+        def tile_run(side, k, count, kib):
+            side[k, count] = at("run%d_%d" % (k, kib), [count, 2, BLK, PACK], F32, kib)
+            for i in range(count):
+                side[k + i] = side[k, count][:, i]
 
-        def tiles_single(k):
-            both = product_tile("pab%d" % k)
+        def tiles_run(k, count, a_kib, b_kib):
+            tile_run(pa, k, count, a_kib)
+            tile_run(pb, k, count, b_kib)
+
+        def tiles_single(k, kib):
+            both = at("pab%d" % k, [2, 2, BLK, PACK], F32, kib)
             pa[k], pb[k] = both[:, 0], both[:, 1]
 
         def times_a(k):
             n = rows_cd(k)
-            nc.vector.tensor_tensor(pa[k], cd[k][:, n - 2 : n], twice(view(a_bank[k], k)), MULT)
+            nc.vector.tensor_tensor(split(pa[k]), cd[k][:, n - 2 : n], split(twice(view(a_bank[k], k))), MULT)
 
         def times_b(k):
             if k in TURNED and rows_cd(k) == 2:
                 flat = lambda ap: ap.rearrange("p n t -> p (n t)")
-                nc.vector.scalar_tensor_tensor(flat(pb[k][:, 0]), flat(cd[k][:, 1]), -1.0, b_bank[k][:], MULT, MULT)
-                nc.vector.tensor_tensor(flat(pb[k][:, 1]), flat(cd[k][:, 0]), b_bank[k][:], MULT)
+                nc.vector.scalar_tensor_tensor(flat(pb[k][:, 0]), flat(cd_pair[k][:, 1]), -1.0, b_bank[k][:], MULT, MULT)
+                nc.vector.tensor_tensor(flat(pb[k][:, 1]), flat(cd_pair[k][:, 0]), b_bank[k][:], MULT)
             else:
-                nc.vector.tensor_tensor(pb[k], cd[k][:, 0:2], twice(view(b_bank[k], k)), MULT)
+                nc.vector.tensor_tensor(split(pb[k]), cd[k][:, 0:2], split(twice(view(b_bank[k], k))), MULT)
 
         def times(*blocks):
             for k in blocks:
@@ -277,7 +296,7 @@ def tile_list_ckg_none_kernel(
             nc.scalar.copy(out=a_sb[k][:], in_=view(a_bank[k], k))
 
         def times_a_gpsimd(k):
-            nc.gpsimd.tensor_tensor(pa[k], cd[k][:], twice(a_sb[k][:]), MULT)
+            nc.gpsimd.tensor_tensor(split(pa[k]), cd[k], split(twice(a_sb[k][:])), MULT)
 
         h = {}
 
@@ -291,11 +310,14 @@ def tile_list_ckg_none_kernel(
             tile, i, width = h[k]
             return tile[:, (c * width + i) * R : (c * width + i + count) * R]
 
-        def sum_pair(k):
+        def sum_run(k, count):
             for c, op in enumerate((SUB, ADD)):
-                nc.gpsimd.tensor_tensor(h_part(k, c, 2).rearrange("p (i x) -> p i x", i=2),
-                                        pa[k, k + 1][:, :, c].rearrange("p i n t -> p i (n t)"),
-                                        pb[k, k + 1][:, :, 1 - c].rearrange("p i n t -> p i (n t)"), op)
+                nc.gpsimd.tensor_tensor(h_part(k, c, count).rearrange("p (i x) -> p i x", i=count),
+                                        pa[k, count][:, :, c].rearrange("p i n t -> p i (n t)"),
+                                        pb[k, count][:, :, 1 - c].rearrange("p i n t -> p i (n t)"), op)
+
+        def sum_single(engine, k):
+            engine.tensor_tensor(h[k][0][:], pa[k].rearrange("p c n t -> p (c n t)"), pb[k].rearrange("p c n t -> p (c n t)"), ADD)
 
         def sum_turned(k):
             for c in range(2):
@@ -336,132 +358,103 @@ def tile_list_ckg_none_kernel(
                     y = at("y%d" % len(staged), [per_bank * width], F32, (SMALL, EXTRA + 16)[len(staged) // 4 % 2] + 2 * (len(staged) % 4))
                     nc.scalar.copy(out=y[:], in_=bank[:])
                 else:
-                    y = at("y%d" % len(staged), [per_bank * width], F32, CAST_B + 6 + b)
+                    y = at("y%d" % len(staged), [per_bank * width], F32, RAW_C + 3 + b)
                     copies[b](y[:], bank[:])
                 staged.append(y)
                 nc.sync.dma_start(out=out_v[:, b * per_bank : (b + 1) * per_bank, first * BLK : first * BLK + width],
                                   in_=y[:].rearrange("p (t n) -> p t n", t=per_bank))
 
-        def pass_a(*blocks):
-            for k in blocks:
-                a_bank[k] = entity("er", k)
+        order = ([("a", k) for k in (0, 1, 2, 4)] + [("b", k) for k in (2, 0, 1)]
+                 + [("a", 5), ("b", 4), ("b", 5), ("a", 6), ("a", 7), ("b", 6), ("b", 7), ("a", 3), ("b", 3)]
+                 + [("a", 8), ("a", 9), ("b", 8), ("b", 9), ("a", 10), ("b", 10), ("a", 11), ("b", 11)]
+                 + [("a", 12), ("a", 13), ("b", 12), ("b", 13)] + [(side, k) for k in (14, 15) for side in "ab"])
+        issued = []
 
-        def pass_b(*blocks):
-            for k in blocks:
-                b_bank[k] = entity("ei", k)
+        def passes_to(side, k):
+            for s, j in order[len(issued) : order.index((side, k)) + 1]:
+                (a_bank if s == "a" else b_bank)[j] = entity("er" if s == "a" else "ei", j)
+                issued.append(j)
 
-        for k in range(GROUP):
-            copy_c(k)
-        for k in (2, 0, 1, 3):
-            copy_d(k)
-        copy_cd(4, 5)
-        pass_a(0, 1, 2, 4)
+        copy_cd(2, 0, 1, 3)
+        passes_to("a", 4)
         h0 = h_tile("h0", 0, GROUP, H_A)
-        tiles_pair(0)
-        tiles_single(2)
-        tiles_single(3)
-        tiles_pair(4)
+        h1 = h_tile("h1", GROUP, GROUP, H_B)
+        tiles_run(0, 2, CAST_B + 3, EXTRA + 24)
+        tiles_single(2, CAST_B - 7)
+        tiles_run(4, 4, TAB2, TAB1)
         for k in (0, 1):
             copy_a(k)
             times_a_gpsimd(k)
+        passes_to("b", 5)
+        copy_cd(4)
         copy_a(4)
-        nc.gpsimd.tensor_tensor(pa[4][:, 0], cd[4][:, 0], a_sb[4][:], MULT)
-        pass_b(2, 0, 1)
-        pass_a(3)
-        copy_cd(6, 7)
+        times_a_gpsimd(4)
         times_a(2)
-        nc.vector.tensor_tensor(pa[4][:, 1], cd[4][:, 1], view(a_bank[4], 4), MULT)
         times_b(2)
-        pass_b(3)
-        copy_cd(8)
-        sum_turned(2)
         times_b(0)
-        pass_a(5)
+        copy_cd(6)
         times_b(1)
-        pass_b(4)
-        sum_pair(0)
-        times_a(3)
-        pass_b(5)
-        copy_cd(9)
-        times_b(3)
-        pass_a(6)
-        sum_turned(3)
+        sum_run(0, 2)
+        sum_turned(2)
+        passes_to("a", 9)
         times_a(5)
-        pass_a(7)
         times_b(4)
-        pass_b(6)
         times_b(5)
-        pass_b(7)
-        copy_cd(10)
-        tiles_pair(6)
+        copy_cd(8)
         times_a(6)
-        pass_a(8)
-        q0 = quantise(h0, GROUP)
-        h1 = h_tile("h1", GROUP, GROUP, H_A)
-        sum_pair(4)
-        copy_cd(11)
         times_a(7)
-        pass_a(9)
         times_b(6)
-        pass_b(8)
-        copy_cd(12)
         times_b(7)
-        pass_b(9)
-        sum_pair(6)
-        copy_cd(13)
-        tiles_pair(8)
+        sum_run(4, 4)
+        copy_cd(10)
+        tiles_single(3, EXTRA)
+        times(3)
+        passes_to("b", 9)
+        sum_turned(3)
+        passes_to("b", 11)
+        copy_cd(11, 12)
+        tiles_run(8, 2, RAW_A, EXTRA + 8)
         times_a(8)
-        pass_a(10)
         times_a(9)
-        pass_b(10)
         times_b(8)
-        pass_a(12)
         times_b(9)
-        pass_a(13)
-        score(q0, 0, GROUP, 1)
+        tiles_single(10, CAST_A)
+        times(10)
+        passes_to("a", 13)
         copy_cd(14)
-        tiles_single(10)
-        times_a(10)
-        pass_b(12)
-        times_b(10)
-        pass_b(13)
-        q1 = quantise(h1, GROUP)
-        h2 = h_tile("h2", 2 * GROUP, GROUP, H_A)
-        sum_pair(8)
-        sum_turned(10)
-        copy_cd(15)
-        h12 = h_tile("h12", 12, 2, H_B)
-        h14 = h_tile("h14", 14, 1, H_B + 4)
-        h15 = h_tile("h15", 15, 1, H_B + 6)
-        tiles_pair(12)
-        times_a(12)
-        pass_a(11)
-        times_a(13)
-        pass_b(11)
-        score(q1, GROUP, GROUP, 1)
-        times_b(12)
-        pass_a(14)
-        times_b(13)
-        pass_b(14)
-        sum_pair(12)
-        tiles_single(11)
+        tiles_single(11, EXTRA)
         times_a(11)
-        pass_a(15)
+        q0 = quantise(h0, GROUP, TAB1)
+        q1 = quantise(h1, GROUP)
+        h2 = h_tile("h2", 2 * GROUP, GROUP, H_A + 4)
+        sum_run(8, 2)
+        sum_turned(10)
+        passes_to("b", 13)
         times_b(11)
-        pass_b(15)
         sum_turned(11)
-        tiles_single(14)
-        times(14)
-        sum_turned(14)
-        tiles_single(LAST)
-        times_a(LAST)
-        q2 = quantise(h2, GROUP, placed["pb12"])
-        q12 = quantise(h12, 2)
+        passes_to("b", 15)
+        score(q0, 0, GROUP, 1)
+        score(q1, GROUP, GROUP, 1)
+        tiles_run(12, 2, TAB2, TAB2 + 8)
+        times_a(12)
+        times_a(13)
+        times_b(12)
+        times_b(13)
+        q2 = quantise(h2, GROUP)
+        h12 = h_tile("h12", 12, 2, H_A + 4)
+        sum_run(12, 2)
         score(q2, 2 * GROUP, GROUP, 1)
+        tiles_single(14, TAB1 + 8)
+        times(14)
+        tiles_single(LAST, CAST_A)
+        times(LAST)
+        q12 = quantise(h12, 2)
         score(q12, 12, 2, 2)
-        times_b(LAST)
+        h14 = h_tile("h14", 14, 1, H_A + 4)
+        h15 = h_tile("h15", 15, 1, H_A + 6)
+        sum_single(nc.vector, 14)
+        sum_single(nc.vector, LAST)
         q14 = quantise(h14, 1)
-        score(q14, 14, 1, 4)
-        nc.vector.tensor_tensor(h15[:], pa[LAST].rearrange("p c n t -> p (c n t)"), pb[LAST].rearrange("p c n t -> p (c n t)"), ADD)
         q15 = quantise(h15, 1)
+        score(q14, 14, 1, 4)
         score(q15, LAST, 1, 2, (nc.scalar.copy, nc.vector.tensor_copy))

@@ -25,8 +25,8 @@ NBLK = J // BLK
 SLICE = 512
 GROUP = 4
 KIB = 1024
-TURNED = (2, 3, 10, 11)
-WIDE = (4, 6, 8, 12, 14)
+TURNED = (2, 3, 12, 13)
+WIDE = (4, 6, 8, 10, 14)
 LAST = NBLK - 1
 
 
@@ -355,7 +355,7 @@ def tile_list_ckg_none_kernel(
                                         lhsT_scale=n_planes[:, N + t * P : N + (t + 1) * P],
                                         rhs=hq[:, width:].bitcast(FP8X4), rhs_scale=hs[:, width:], start=False, stop=True)
                 if copies is None:
-                    y = at("y%d" % len(staged), [per_bank * width], F32, (SMALL, EXTRA + 16)[len(staged) // 4 % 2] + 2 * (len(staged) % 4))
+                    y = at("y%d" % len(staged), [per_bank * width], F32, (TAB2, EXTRA + 16)[len(staged) // 4 % 2] + 2 * (len(staged) % 4))
                     nc.scalar.copy(out=y[:], in_=bank[:])
                 else:
                     y = at("y%d" % len(staged), [per_bank * width], F32, RAW_C + 3 + b)
@@ -364,10 +364,10 @@ def tile_list_ckg_none_kernel(
                 nc.sync.dma_start(out=out_v[:, b * per_bank : (b + 1) * per_bank, first * BLK : first * BLK + width],
                                   in_=y[:].rearrange("p (t n) -> p t n", t=per_bank))
 
-        order = ([("a", k) for k in (0, 1, 2, 4)] + [("b", k) for k in (2, 0, 1)]
+        order = ([("a", k) for k in (0, 1, 2, 4)] + [("b", k) for k in (0, 1, 2)]
                  + [("a", 5), ("b", 4), ("b", 5), ("a", 6), ("a", 7), ("b", 6), ("b", 7), ("a", 3), ("b", 3)]
-                 + [("a", 8), ("a", 9), ("b", 8), ("b", 9), ("a", 10), ("b", 10), ("a", 11), ("b", 11)]
-                 + [("a", 12), ("a", 13), ("b", 12), ("b", 13)] + [(side, k) for k in (14, 15) for side in "ab"])
+                 + [("a", 8), ("a", 9), ("b", 8), ("b", 9), ("a", 10), ("a", 11), ("b", 10), ("b", 11)]
+                 + [(side, k) for k in (12, 13, 14, 15) for side in "ab"])
         issued = []
 
         def passes_to(side, k):
@@ -381,80 +381,81 @@ def tile_list_ckg_none_kernel(
         h1 = h_tile("h1", GROUP, GROUP, H_B)
         tiles_run(0, 2, CAST_B + 3, EXTRA + 24)
         tiles_single(2, CAST_B - 7)
-        tiles_run(4, 4, TAB2, TAB1)
+        tiles_run(4, 2, TAB2, TAB1)
+        tiles_run(6, 2, TAB2 + 8, TAB1 + 8)
         for k in (0, 1):
             copy_a(k)
             times_a_gpsimd(k)
         passes_to("b", 5)
         copy_cd(4)
-        copy_a(4)
-        times_a_gpsimd(4)
         times_a(2)
-        times_b(2)
         times_b(0)
-        copy_cd(6)
         times_b(1)
         sum_run(0, 2)
+        copy_cd(6)
+        times_b(2)
         sum_turned(2)
         passes_to("a", 9)
+        times_a(4)
         times_a(5)
         times_b(4)
         times_b(5)
+        sum_run(4, 2)
         copy_cd(8)
         times_a(6)
         times_a(7)
         times_b(6)
         times_b(7)
-        sum_run(4, 4)
+        sum_run(6, 2)
         copy_cd(10)
         tiles_single(3, EXTRA)
         times(3)
         passes_to("b", 9)
         sum_turned(3)
         passes_to("b", 11)
-        copy_cd(11, 12)
+        copy_cd(12, 13, 14)
         tiles_run(8, 2, RAW_A, EXTRA + 8)
         times_a(8)
         times_a(9)
         times_b(8)
         times_b(9)
-        tiles_single(10, CAST_A)
-        times(10)
-        passes_to("a", 13)
-        copy_cd(14)
-        tiles_single(11, EXTRA)
-        times_a(11)
-        q0 = quantise(h0, GROUP, TAB1)
+        q0 = quantise(h0, GROUP, TAB1 + 8)
         q1 = quantise(h1, GROUP)
         h2 = h_tile("h2", 2 * GROUP, GROUP, H_A + 4)
         sum_run(8, 2)
-        sum_turned(10)
         passes_to("b", 13)
-        times_b(11)
-        sum_turned(11)
-        passes_to("b", 15)
         score(q0, 0, GROUP, 1)
+        tiles_run(10, 2, H_B + 4, H_A - 7)
+        times_a(10)
+        times_a(11)
+        times_b(10)
+        times_b(11)
+        sum_run(10, 2)
         score(q1, GROUP, GROUP, 1)
-        tiles_run(12, 2, TAB2, TAB2 + 8)
-        times_a(12)
-        times_a(13)
-        times_b(12)
-        times_b(13)
+        h12 = h_tile("h12", 12, 2, H_C + 4)
+        tiles_single(12, EXTRA)
+        times(12)
+        passes_to("b", 14)
+        sum_turned(12)
+        passes_to("b", 15)
+        tiles_single(13, TAB2 + 8)
+        times(13)
+        sum_turned(13)
+        tile_run(pa, 14, 1, TAB1)
+        times_a(14)
         q2 = quantise(h2, GROUP)
-        h12 = h_tile("h12", 12, 2, H_A + 4)
-        sum_run(12, 2)
         score(q2, 2 * GROUP, GROUP, 1)
-        tiles_single(14, TAB1 + 8)
-        times(14)
-        tiles_single(LAST, CAST_A)
-        times(LAST)
-        q12 = quantise(h12, 2)
-        score(q12, 12, 2, 2)
+        tile_run(pb, 14, 1, H_A + 6)
+        times_b(14)
         h14 = h_tile("h14", 14, 1, H_A + 4)
-        h15 = h_tile("h15", 15, 1, H_A + 6)
-        sum_single(nc.vector, 14)
-        sum_single(nc.vector, LAST)
+        sum_single(nc.gpsimd, 14)
+        tiles_single(LAST, H_A + 10)
+        times(LAST)
+        q12 = quantise(h12, 2, TAB1)
         q14 = quantise(h14, 1)
-        q15 = quantise(h15, 1)
+        score(q12, 12, 2, 2)
         score(q14, 14, 1, 4)
+        h15 = h_tile("h15", 15, 1, H_A + 4)
+        sum_single(nc.vector, LAST)
+        q15 = quantise(h15, 1)
         score(q15, LAST, 1, 2, (nc.scalar.copy, nc.vector.tensor_copy))

@@ -50,7 +50,7 @@ def tile_list_ckg_none_kernel(
         list1 = keep.tile([P, J // 16], U16, name="list1")
         list2 = keep.tile([P, J // 16], U16, name="list2")
         ident = held("ident", [P], F32)
-        e_words = [held("e_words%d" % s, [SLICE], U32) for s in range(J // SLICE)]
+        e_words = [held("e_words%d" % s, [2 * SLICE], U32) for s in range(2)]
         e_plane = held("e_plane", [J], U8)
         r_planes = held("r_planes", [2 * J], U8)
         r_words = [held("r_words%d" % s, [2, 2 * SLICE], U8) for s in range(J // SLICE)]
@@ -149,13 +149,13 @@ def tile_list_ckg_none_kernel(
                 nc.sync.dma_start(out=n_planes[r:P:32, i * N : (i + 1) * N].bitcast(I32), in_=rows[0][r:16:4, :].bitcast(I32))
 
         def gather_entity(s):
-            nc.vector.tensor_copy(e_words[s][:], t1_words[:].bitcast(U32).indirect(offsets(list1, s)))
+            nc.vector.tensor_copy(e_words[s][:], t1_words[:].bitcast(U32).indirect(list1[:, s * SLICE // 8 : (s + 1) * SLICE // 8]))
 
         wb_er = at("wb_er", [PACK * R], BF16, CAST_A)
         wb_ei = at("wb_ei", [PACK * R], BF16, CAST_B)
         cast(wb_er[:], raw_er[:])
         quantise_weight("er", wb_er[:])
-        for s in range(J // SLICE):
+        for s in range(2):
             gather_entity(s)
         for h in range(2):
             nc.scalar.copy(out=wb_ei[:].rearrange("p (t m j) -> p m j t", t=PACK, j=PACK)[:, h * P // 2 : (h + 1) * P // 2],
@@ -180,7 +180,7 @@ def tile_list_ckg_none_kernel(
 
         def entity(n, k):
             tok = slice(k * BLK, (k + 1) * BLK)
-            return project([(wq[n][:], ws[n][:], e_words[k // GROUP][:, k % GROUP * BLK : (k % GROUP + 1) * BLK].bitcast(FP8X4), e_plane[:, tok])], k, "ab")
+            return project([(wq[n][:], ws[n][:], e_words[k // (2 * GROUP)][:, k % (2 * GROUP) * BLK : (k % (2 * GROUP) + 1) * BLK].bitcast(FP8X4), e_plane[:, tok])], k, "ab")
 
         weights_c = [(wq["rr"][:, a * R : (a + 1) * R], ws["rr"][:, a * R : (a + 1) * R]) for a in range(2)]
         weights_d = [(wq[n][:], ws[n][:]) for n in ("ri0", "ri1")]
@@ -383,12 +383,14 @@ def tile_list_ckg_none_kernel(
         tiles_single(2, CAST_B - 7)
         tiles_run(4, 2, TAB2, TAB1)
         tiles_run(6, 2, TAB2 + 8, TAB1 + 8)
-        for k in (0, 1):
-            copy_a(k)
-            times_a_gpsimd(k)
+        copy_a(0)
+        times_a_gpsimd(0)
+        copy_a(1)
+        nc.gpsimd.tensor_tensor(pa[1][:, 0], cd_pair[1][:, 0], a_sb[1][:], MULT)
         passes_to("b", 5)
         copy_cd(4)
         times_a(2)
+        nc.vector.tensor_tensor(pa[1][:, 1], cd_pair[1][:, 1], view(a_bank[1], 1), MULT)
         times_b(0)
         times_b(1)
         sum_run(0, 2)

@@ -285,8 +285,8 @@ def tile_list_ckg_none_kernel(
 
         def times(*blocks):
             for k in blocks:
-                times_a(k)
                 times_b(k)
+                times_a(k)
 
         a_sb, a_at = {}, {}
 
@@ -391,23 +391,23 @@ def tile_list_ckg_none_kernel(
         copy_cd(4)
         times_a(2)
         nc.vector.tensor_tensor(pa[1][:, 1], cd_pair[1][:, 1], view(a_bank[1], 1), MULT)
-        times_b(0)
         times_b(1)
+        times_b(0)
         sum_run(0, 2)
         copy_cd(6)
         times_b(2)
         sum_turned(2)
         passes_to("a", 9)
-        times_a(4)
         times_a(5)
-        times_b(4)
+        times_a(4)
         times_b(5)
+        times_b(4)
         sum_run(4, 2)
         copy_cd(8)
-        times_a(6)
         times_a(7)
-        times_b(6)
+        times_a(6)
         times_b(7)
+        times_b(6)
         sum_run(6, 2)
         copy_cd(10)
         tiles_single(3, EXTRA)
@@ -417,10 +417,10 @@ def tile_list_ckg_none_kernel(
         passes_to("b", 11)
         copy_cd(12, 13, 14)
         tiles_run(8, 2, RAW_A, EXTRA + 8)
-        times_a(8)
         times_a(9)
-        times_b(8)
+        times_a(8)
         times_b(9)
+        times_b(8)
         q0 = quantise(h0, GROUP, TAB1 + 8)
         q1 = quantise(h1, GROUP)
         h2 = h_tile("h2", 2 * GROUP, GROUP, H_A + 4)
@@ -428,10 +428,10 @@ def tile_list_ckg_none_kernel(
         passes_to("b", 13)
         score(q0, 0, GROUP, 1)
         tiles_run(10, 2, H_B + 4, H_A - 7)
-        times_a(10)
         times_a(11)
-        times_b(10)
+        times_a(10)
         times_b(11)
+        times_b(10)
         sum_run(10, 2)
         score(q1, GROUP, GROUP, 1)
         h12 = h_tile("h12", 12, 2, H_C + 4)
@@ -443,12 +443,10 @@ def tile_list_ckg_none_kernel(
         tiles_single(13, TAB2 + 8)
         times(13)
         sum_turned(13)
-        tile_run(pa, 14, 1, TAB1)
-        times_a(14)
+        tiles_single(14, TAB1)
+        times(14)
         q2 = quantise(h2, GROUP)
         score(q2, 2 * GROUP, GROUP, 1)
-        tile_run(pb, 14, 1, H_A + 6)
-        times_b(14)
         h14 = h_tile("h14", 14, 1, H_A + 4)
         sum_single(nc.gpsimd, 14)
         tiles_single(LAST, H_A + 10)

@@ -329,13 +329,17 @@ def tile_list_ckg_none_kernel(
                                          is_transpose=True, start=(i == 0), stop=(i == 1))
                 nc.scalar.copy(out=h_part(k, c).rearrange("p (n t) -> p n t", t=PACK), in_=woven(bank))
 
-        def quantise(tile, count, scales_at=None):
+        def quantise(tile, count, scales_at=None, calls=1):
             hq = codes.tile([P, 2 * count * BLK], U32, name="hq", align_bytes=64)
             if scales_at is None:
                 hs = codes.tile([P, 2 * count * BLK], U8, name="hs", align_bytes=64)
             else:
                 hs = at("hs_held", [2 * count * BLK], U8, scales_at)
-            nc.vector.quantize_mx(out=hq[:].bitcast(FP8X4), scales=hs[:], in_=tile[:])
+            width = 2 * count * BLK // calls
+            for i in range(calls):
+                words = slice(i * width, (i + 1) * width)
+                nc.vector.quantize_mx(out=hq[:, words].bitcast(FP8X4), scales=hs[:, words],
+                                      in_=tile[:, i * width * PACK : (i + 1) * width * PACK])
             return hq, hs
 
         out_v = out.rearrange("(t p) j -> p t j", p=P)
@@ -451,11 +455,13 @@ def tile_list_ckg_none_kernel(
         sum_single(nc.gpsimd, 14)
         tiles_single(LAST, H_A + 10)
         times(LAST)
-        q12 = quantise(h12, 2, TAB1)
         q14 = quantise(h14, 1)
-        score(q12, 12, 2, 2)
+        q12 = quantise(h12, 2, TAB1)
         score(q14, 14, 1, 4)
-        h15 = h_tile("h15", 15, 1, H_A + 4)
-        sum_single(nc.vector, LAST)
-        q15 = quantise(h15, 1)
+        score(q12, 12, 2, 2)
+        h15 = h_tile("h15", 15, 1, TAB1 + 2)
+        for c in range(2):
+            nc.vector.tensor_tensor(h_part(LAST, c), pa[LAST][:, c].rearrange("p n t -> p (n t)"),
+                                    pb[LAST][:, c].rearrange("p n t -> p (n t)"), ADD)
+        q15 = quantise(h15, 1, calls=2)
         score(q15, LAST, 1, 2, (nc.scalar.copy, nc.vector.tensor_copy))

@@ -387,14 +387,12 @@ def tile_list_ckg_none_kernel(
         tiles_single(2, CAST_B - 7)
         tiles_run(4, 2, TAB2, TAB1)
         tiles_run(6, 2, TAB2 + 8, TAB1 + 8)
-        copy_a(0)
-        times_a_gpsimd(0)
-        copy_a(1)
-        nc.gpsimd.tensor_tensor(pa[1][:, 0], cd_pair[1][:, 0], a_sb[1][:], MULT)
+        for k in (0, 1):
+            copy_a(k)
+            times_a_gpsimd(k)
         passes_to("b", 5)
         copy_cd(4)
         times_a(2)
-        nc.vector.tensor_tensor(pa[1][:, 1], cd_pair[1][:, 1], view(a_bank[1], 1), MULT)
         times_b(1)
         times_b(0)
         sum_run(0, 2)

from contextlib import ExitStack

import concourse.mybir as mybir
from concourse.masks import make_identity

K, L, R, N, T, J = 512, 1024, 512, 512, 4096, 2048
FLOPS = 2 * J * R * (2 * K + 2 * L + 2 * N)

F32 = mybir.dt.float32
BF16 = mybir.dt.bfloat16
I32 = mybir.dt.int32
U32 = mybir.dt.uint32
U16 = mybir.dt.uint16
U8 = mybir.dt.uint8
FP8X4 = mybir.dt.float8_e4m3fn_x4
FP4X4 = mybir.dt.float4_e2m1fn_x4
MULT = mybir.AluOpType.mult
ADD = mybir.AluOpType.add
SUB = mybir.AluOpType.subtract

P = 128
PACK = 4
BLK = 128
NBLK = J // BLK
SLICE = 512
GROUP = 4
KIB = 1024
TURNED = (2, 3, 12, 13)
WIDE = (4, 6, 8, 10, 14)
LAST = NBLK - 1


def tile_list_ckg_none_kernel(
    tc, tab_words, tab_scales, tab2_words, tab2_scales, wer, wei, wrr, wri,
    nr_words, nr_scales, ni_words, ni_scales, offs, offs2, out,
):
    nc = tc.nc
    with ExitStack() as ctx:
        keep = ctx.enter_context(tc.tile_pool(name="keep", bufs=1))
        arena = ctx.enter_context(tc.tile_pool(name="arena", bufs=1))
        codes = ctx.enter_context(tc.tile_pool(name="codes", bufs=3))
        psum = ctx.enter_context(tc.psum_pool(name="psum", bufs=4))

        def at(name, shape, dtype, kib):
            return arena.tile([P] + shape, dtype, name=name, align_bytes=64, offset=kib * KIB)

        def held(name, shape, dtype):
            return keep.tile([P] + shape, dtype, name=name, align_bytes=64)

        list1 = keep.tile([P, J // 16], U16, name="list1")
        list2 = keep.tile([P, J // 16], U16, name="list2")
        ident = held("ident", [P], F32)
        e_words = [held("e_words%d" % s, [2 * SLICE], U32) for s in range(2)]
        e_plane = held("e_plane", [J], U8)
        r_planes = held("r_planes", [2 * J], U8)
        r_words = [held("r_words%d" % s, [2, 2 * SLICE], U8) for s in range(J // SLICE)]
        wq = {n: held("wq_" + n, [w], U32) for n, w in (("rr", 2 * R), ("ri0", R), ("ri1", R), ("er", R), ("ei", R))}
        ws = {n: held("ws_" + n, [w], U8) for n, w in (("rr", 2 * R), ("ri0", R), ("ri1", R), ("er", R), ("ei", R))}

        RAW_A, RAW_B, RAW_C, RAW_D, TAB2, TAB1, CAST_A, CAST_B, SMALL, H_A, H_B, H_C, CD = 0, 8, 16, 24, 32, 48, 64, 72, 80, 88, 96, 104, 112

        t2_rows = at("t2_rows", [T], U8, RAW_D)
        t2_words = at("t2_words", [T], I32, TAB2)
        t1_rows = at("t1_rows", [T], U8, TAB1)
        r_picked = at("r_picked", [J], U8, SMALL)
        e_picked = at("e_picked", [J], U8, SMALL + 2)

        def rows_of(w):
            return w.rearrange("(p j) r -> p j r", j=PACK)

        def load_raw(name, w, kib):
            raw = at("raw_" + name, [PACK, R], F32, kib)
            nc.sync.dma_start(out=raw[:], in_=rows_of(w))
            return raw

        def cast(dst, raw):
            nc.scalar.copy(out=dst.rearrange("p (t m j) -> p m j t", t=PACK, j=PACK),
                           in_=raw.rearrange("p j (m t) -> p m j t", t=PACK))

        def quantise_weight(n, src):
            nc.vector.quantize_mx(out=wq[n][:].bitcast(FP8X4), scales=ws[n][:], in_=src)

        def move_rows(plane, picked, first):
            for r in range(4):
                nc.sync.dma_start(out=plane[r:P:32].bitcast(I32), in_=picked[first + r : first + 16 : 4, :].bitcast(I32))

        def words_of(words):
            return words[0].rearrange("p t i -> p (t i)").bitcast(I32)

        nc.sync.dma_start(list2[:], offs2)
        nc.sync.dma_start(out=t2_rows[96:P, :].bitcast(I32), in_=tab2_scales.rearrange("a q t -> (a q) t").bitcast(I32))
        nc.sync.dma_start(list1[:], offs)
        nc.sync.dma_start(out=t1_rows[112:P, :].bitcast(I32), in_=tab_scales[0].bitcast(I32))
        nc.vector.memset(t2_rows[0:96, :].bitcast(I32), 0)
        nc.vector.memset(r_planes[:].bitcast(I32), 0)
        nc.vector.memset(t1_rows[0:112, :].bitcast(I32), 0)
        nc.vector.memset(e_plane[:].bitcast(I32), 0)
        make_identity(nc, ident[:])
        raw_rr0 = load_raw("rr0", wrr[0:K, :], RAW_A)
        raw_rr1 = load_raw("rr1", wrr[K:L, :], RAW_B)
        raw_ri0 = load_raw("ri0", wri[0:K, :], RAW_C)
        nc.sync.dma_start(out=t2_words[:], in_=words_of(tab2_words))

        nc.vector.tensor_copy(r_picked[:], t2_rows[:].indirect(list2[:]))
        nc.vector.tensor_copy(e_picked[:], t1_rows[:].indirect(list1[:]))
        wb_rr = at("wb_rr", [2 * PACK * R], BF16, CAST_A)
        cast(wb_rr[:, 0 : PACK * R], raw_rr0[:])
        cast(wb_rr[:, PACK * R :], raw_rr1[:])
        quantise_weight("rr", wb_rr[:])

        move_rows(r_planes[:, 0:J], r_picked, 96)
        raw_ri1 = load_raw("ri1", wri[K:L, :], RAW_D)
        move_rows(r_planes[:, J:], r_picked, 112)
        raw_er = load_raw("er", wer, RAW_A)
        t1_words = at("t1_words", [T], I32, TAB1)
        nc.sync.dma_start(out=t1_words[:], in_=words_of(tab_words))
        move_rows(e_plane[:], e_picked, 112)
        raw_ei = at("raw_ei", [2, PACK, R // 2], F32, RAW_B)
        for h in range(2):
            nc.sync.dma_start(out=raw_ei[:, h], in_=rows_of(wei)[:, :, h * R // 2 : (h + 1) * R // 2])

        def offsets(lst, s):
            return lst[:, s * SLICE // 16 : (s + 1) * SLICE // 16]

        def gather_relation(s, kib):
            pairs = at("pairs%d" % s, [SLICE], U32, kib)
            nc.vector.tensor_copy(pairs[:], t2_words[:].bitcast(U32).indirect(offsets(list2, s)))
            nc.vector.tensor_copy(r_words[s][:].bitcast(U16).rearrange("p d (c i) -> p c d i", i=8),
                                  pairs[:].bitcast(U16).rearrange("p (c i d) -> p c d i", i=8, d=2))

        wb_ri0 = at("wb_ri0", [PACK * R], BF16, CAST_B)
        wb_ri1 = at("wb_ri1", [PACK * R], BF16, CAST_B + 4)
        cast(wb_ri0[:], raw_ri0[:])
        quantise_weight("ri0", wb_ri0[:])
        for s, kib in ((0, SMALL + 4), (2, SMALL + 6), (3, CAST_B)):
            gather_relation(s, kib)
        cast(wb_ri1[:], raw_ri1[:])
        quantise_weight("ri1", wb_ri1[:])
        gather_relation(1, CAST_B + 4)

        nr_w = at("nr_w", [N], I32, RAW_D + 3)
        ni_w = at("ni_w", [2 * N], U8, RAW_D + 5)
        n_planes = at("n_planes", [2 * N], U8, RAW_D + 6)
        nc.vector.memset(n_planes[:].bitcast(I32), 0)
        nc.sync.dma_start(out=nr_w[:], in_=words_of(nr_words))
        nc.sync.dma_start(out=ni_w[:].bitcast(I32), in_=ni_words[0].bitcast(I32))
        for i, rows in enumerate((nr_scales, ni_scales)):
            for r in range(4):
                nc.sync.dma_start(out=n_planes[r:P:32, i * N : (i + 1) * N].bitcast(I32), in_=rows[0][r:16:4, :].bitcast(I32))

        def gather_entity(s):
            nc.vector.tensor_copy(e_words[s][:], t1_words[:].bitcast(U32).indirect(list1[:, s * SLICE // 8 : (s + 1) * SLICE // 8]))

        wb_er = at("wb_er", [PACK * R], BF16, CAST_A)
        wb_ei = at("wb_ei", [PACK * R], BF16, CAST_B)
        cast(wb_er[:], raw_er[:])
        quantise_weight("er", wb_er[:])
        for s in range(2):
            gather_entity(s)
        for h in range(2):
            nc.scalar.copy(out=wb_ei[:].rearrange("p (t m j) -> p m j t", t=PACK, j=PACK)[:, h * P // 2 : (h + 1) * P // 2],
                           in_=raw_ei[:, h].rearrange("p j (m t) -> p m j t", t=PACK))
        quantise_weight("ei", wb_ei[:])

        def project(passes, k, tag):
            bank = psum.tile([P, R], F32, name="bank", tag=tag)
            last = len(passes) - 1
            if k in TURNED:
                for a, (w_codes, w_scales, tok_codes, tok_scales) in enumerate(passes):
                    nc.tensor.matmul_mx(out=bank[:], lhsT=tok_codes, lhsT_scale=tok_scales, rhs=w_codes.bitcast(FP8X4),
                                        rhs_scale=w_scales, start=(a == 0), stop=(a == last))
            else:
                for t in range(PACK):
                    m = slice(t * P, (t + 1) * P)
                    for a, (w_codes, w_scales, tok_codes, tok_scales) in enumerate(passes):
                        nc.tensor.matmul_mx(out=bank[:, t * BLK : (t + 1) * BLK], lhsT=w_codes[:, m].bitcast(FP8X4),
                                            lhsT_scale=w_scales[:, m], rhs=tok_codes, rhs_scale=tok_scales,
                                            start=(a == 0), stop=(a == last))
            return bank

        def entity(n, k):
            tok = slice(k * BLK, (k + 1) * BLK)
            return project([(wq[n][:], ws[n][:], e_words[k // (2 * GROUP)][:, k % (2 * GROUP) * BLK : (k % (2 * GROUP) + 1) * BLK].bitcast(FP8X4), e_plane[:, tok])], k, "ab")

        weights_c = [(wq["rr"][:, a * R : (a + 1) * R], ws["rr"][:, a * R : (a + 1) * R]) for a in range(2)]
        weights_d = [(wq[n][:], ws[n][:]) for n in ("ri0", "ri1")]

        def relation(weights, k):
            s, first = divmod(k * BLK, SLICE)
            return project([weights[a] + (r_words[s][:, a, 2 * first : 2 * (first + BLK)].bitcast(FP4X4),
                                          r_planes[:, a * J + k * BLK : a * J + (k + 1) * BLK]) for a in range(2)], k, "out")

        def woven(bank):
            return bank[:].rearrange("p (t n) -> p n t", t=PACK)

        def view(bank, k):
            return bank[:].rearrange("p (n t) -> p n t", t=PACK) if k in TURNED else woven(bank)

        def twice(ap):
            return ap.unsqueeze(1).to_broadcast([P, 2, BLK, PACK])

        def rows_cd(k):
            return 3 if k >= NBLK - 2 else 2

        cd, cd_pair, cd_at, free = {}, {}, {2: RAW_A, 0: RAW_A + 4, 4: RAW_B + 7}, CD
        for k in range(NBLK):
            if k == 3 * GROUP:
                free = CD + 4
            if k not in cd_at and k - 1 not in WIDE:
                cd_at[k] = free
                free = free + rows_cd(k) * (4 if k in WIDE else 2)
        EXTRA = CD + 32

        def split(ap):
            return ap.rearrange("p c n (u v) -> p c n u v", v=2)

        def copy_c(k):
            tile = at("cd%d" % k, [rows_cd(k), BLK, PACK], F32, cd_at[k])
            cd[k] = split(tile[:])
            nc.scalar.copy(out=tile[:, rows_cd(k) - 2], in_=view(relation(weights_c, k), k))
            cd_pair[k] = tile

        def copy_d(k):
            bank = relation(weights_d, k)
            nc.scalar.copy(out=cd_pair[k][:, rows_cd(k) - 1], in_=view(bank, k))
            if rows_cd(k) == 3:
                nc.scalar.mul(cd_pair[k][:, 0], view(bank, k), -1.0)

        def copy_wide(k):
            rows = rows_cd(k)
            tile = at("cd%d" % k, [2, 2, rows, BLK, 2], F32, cd_at[k])
            s, first = divmod(k * BLK, SLICE)
            for c, weights in enumerate((weights_c, weights_d)):
                for u in range(2):
                    bank = psum.tile([P, R], F32, name="bank", tag="out")
                    for v in range(2):
                        m = slice((2 * u + v) * P, (2 * u + v + 1) * P)
                        for a, (w_codes, w_scales) in enumerate(weights):
                            nc.tensor.matmul_mx(out=bank[:, v * 2 * BLK : (v + 1) * 2 * BLK], lhsT=w_codes[:, m].bitcast(FP8X4),
                                                lhsT_scale=w_scales[:, m],
                                                rhs=r_words[s][:, a, 2 * first : 2 * (first + 2 * BLK)].bitcast(FP4X4),
                                                rhs_scale=r_planes[:, a * J + k * BLK : a * J + (k + 2) * BLK],
                                                start=(a == 0), stop=(a == 1))
                    sums = bank[:].rearrange("p (v i n) -> p i n v", v=2, i=2)
                    nc.scalar.copy(out=tile[:, u, :, rows - 2 + c], in_=sums)
                    if c == 1 and rows == 3:
                        nc.scalar.mul(tile[:, u, :, 0], sums, -1.0)
            for i in range(2):
                cd[k + i] = tile[:, :, i].rearrange("p u c n v -> p c n u v")

        def copy_cd(*blocks):
            for k in blocks:
                if k in WIDE:
                    copy_wide(k)
                else:
                    copy_c(k)
                    copy_d(k)

        a_bank, b_bank, pa, pb = {}, {}, {}, {}

        def tile_run(side, k, count, kib):
            side[k, count] = at("run%d_%d" % (k, kib), [count, 2, BLK, PACK], F32, kib)
            for i in range(count):
                side[k + i] = side[k, count][:, i]

        def tiles_run(k, count, a_kib, b_kib):
            tile_run(pa, k, count, a_kib)
            tile_run(pb, k, count, b_kib)

        def tiles_single(k, kib):
            both = at("pab%d" % k, [2, 2, BLK, PACK], F32, kib)
            pa[k], pb[k] = both[:, 0], both[:, 1]

        def times_a(k):
            n = rows_cd(k)
            nc.vector.tensor_tensor(split(pa[k]), cd[k][:, n - 2 : n], split(twice(view(a_bank[k], k))), MULT)

        def times_b(k):
            if k in TURNED and rows_cd(k) == 2:
                flat = lambda ap: ap.rearrange("p n t -> p (n t)")
                nc.vector.scalar_tensor_tensor(flat(pb[k][:, 0]), flat(cd_pair[k][:, 1]), -1.0, b_bank[k][:], MULT, MULT)
                nc.vector.tensor_tensor(flat(pb[k][:, 1]), flat(cd_pair[k][:, 0]), b_bank[k][:], MULT)
            else:
                nc.vector.tensor_tensor(split(pb[k]), cd[k][:, 0:2], split(twice(view(b_bank[k], k))), MULT)

        def times(*blocks):
            for k in blocks:
                times_b(k)
                times_a(k)

        a_sb, a_at = {}, {}

        def copy_a(k):
            a_at[k] = RAW_B + 1 + 2 * len(a_at)
            a_sb[k] = at("a_sb%d" % k, [BLK, PACK], F32, a_at[k])
            nc.scalar.copy(out=a_sb[k][:], in_=view(a_bank[k], k))

        def times_a_gpsimd(k):
            nc.gpsimd.tensor_tensor(split(pa[k]), cd[k], split(twice(a_sb[k][:])), MULT)

        h = {}

        def h_tile(name, first, count, kib):
            tile = at(name, [2 * count * R], BF16, kib)
            for i in range(count):
                h[first + i] = (tile, i, count)
            return tile

        def h_part(k, c, count=1):
            tile, i, width = h[k]
            return tile[:, (c * width + i) * R : (c * width + i + count) * R]

        def sum_run(k, count):
            for c, op in enumerate((SUB, ADD)):
                nc.gpsimd.tensor_tensor(h_part(k, c, count).rearrange("p (i x) -> p i x", i=count),
                                        pa[k, count][:, :, c].rearrange("p i n t -> p i (n t)"),
                                        pb[k, count][:, :, 1 - c].rearrange("p i n t -> p i (n t)"), op)

        def sum_single(engine, k):
            engine.tensor_tensor(h[k][0][:], pa[k].rearrange("p c n t -> p (c n t)"), pb[k].rearrange("p c n t -> p (c n t)"), ADD)

        def sum_turned(k):
            for c in range(2):
                bank = psum.tile([P, R], F32, name="bank", tag="out")
                terms = [p[k][:, c].rearrange("p n t -> p (n t)") for p in (pb, pa)]
                for t in range(PACK):
                    for i, term in enumerate(terms):
                        nc.tensor.matmul(bank[:, t * BLK : (t + 1) * BLK], lhsT=term[:, t * P : (t + 1) * P], rhs=ident[:],
                                         is_transpose=True, start=(i == 0), stop=(i == 1))
                nc.scalar.copy(out=h_part(k, c).rearrange("p (n t) -> p n t", t=PACK), in_=woven(bank))

        def quantise(tile, count, scales_at=None, calls=1):
            hq = codes.tile([P, 2 * count * BLK], U32, name="hq", align_bytes=64)
            if scales_at is None:
                hs = codes.tile([P, 2 * count * BLK], U8, name="hs", align_bytes=64)
            else:
                hs = at("hs_held", [2 * count * BLK], U8, scales_at)
            width = 2 * count * BLK // calls
            for i in range(calls):
                words = slice(i * width, (i + 1) * width)
                nc.vector.quantize_mx(out=hq[:, words].bitcast(FP8X4), scales=hs[:, words],
                                      in_=tile[:, i * width * PACK : (i + 1) * width * PACK])
            return hq, hs

        out_v = out.rearrange("(t p) j -> p t j", p=P)
        staged = []

        def score(quantised, first, count, per_bank, copies=None):
            hq, hs = quantised
            width = count * BLK
            for b in range(N // P // per_bank):
                bank = psum.tile([P, per_bank * width], F32, name="bank", tag="out")
                for i in range(per_bank):
                    t = b * per_bank + i
                    o = bank[:, i * width : (i + 1) * width]
                    nc.tensor.matmul_mx(out=o, lhsT=nr_w[:, t * P : (t + 1) * P].bitcast(FP8X4), lhsT_scale=n_planes[:, t * P : (t + 1) * P],
                                        rhs=hq[:, 0:width].bitcast(FP8X4), rhs_scale=hs[:, 0:width], start=True, stop=False)
                    nc.tensor.matmul_mx(out=o, lhsT=ni_w[:, 2 * t * P : 2 * (t + 1) * P].bitcast(FP4X4),
                                        lhsT_scale=n_planes[:, N + t * P : N + (t + 1) * P],
                                        rhs=hq[:, width:].bitcast(FP8X4), rhs_scale=hs[:, width:], start=False, stop=True)
                if copies is None:
                    y = at("y%d" % len(staged), [per_bank * width], F32, (TAB2, EXTRA + 16)[len(staged) // 4 % 2] + 2 * (len(staged) % 4))
                    nc.scalar.copy(out=y[:], in_=bank[:])
                else:
                    y = at("y%d" % len(staged), [per_bank * width], F32, RAW_C + 3 + b)
                    copies[b](y[:], bank[:])
                staged.append(y)
                nc.sync.dma_start(out=out_v[:, b * per_bank : (b + 1) * per_bank, first * BLK : first * BLK + width],
                                  in_=y[:].rearrange("p (t n) -> p t n", t=per_bank))

        order = ([("a", k) for k in (0, 1, 2, 4)] + [("b", k) for k in (0, 1, 2)]
                 + [("a", 5), ("b", 4), ("b", 5), ("a", 6), ("a", 7), ("b", 6), ("b", 7), ("a", 3), ("b", 3)]
                 + [("a", 8), ("a", 9), ("b", 8), ("b", 9), ("a", 10), ("a", 11), ("b", 10), ("b", 11)]
                 + [(side, k) for k in (12, 13, 14, 15) for side in "ab"])
        issued = []

        def passes_to(side, k):
            for s, j in order[len(issued) : order.index((side, k)) + 1]:
                (a_bank if s == "a" else b_bank)[j] = entity("er" if s == "a" else "ei", j)
                issued.append(j)

        copy_cd(2, 0, 1, 3)
        passes_to("a", 4)
        h0 = h_tile("h0", 0, GROUP, H_A)
        h1 = h_tile("h1", GROUP, GROUP, H_B)
        tiles_run(0, 2, CAST_B + 3, EXTRA + 24)
        tiles_single(2, CAST_B - 7)
        tiles_run(4, 2, TAB2, TAB1)
        tiles_run(6, 2, TAB2 + 8, TAB1 + 8)
        for k in (0, 1):
            copy_a(k)
            times_a_gpsimd(k)
        passes_to("b", 5)
        copy_cd(4)
        times_a(2)
        times_b(1)
        times_b(0)
        sum_run(0, 2)
        copy_cd(6)
        times_b(2)
        sum_turned(2)
        passes_to("a", 9)
        times_a(5)
        times_a(4)
        times_b(5)
        times_b(4)
        sum_run(4, 2)
        copy_cd(8)
        times_a(7)
        times_a(6)
        times_b(7)
        times_b(6)
        sum_run(6, 2)
        copy_cd(10)
        tiles_single(3, EXTRA)
        times(3)
        passes_to("b", 9)
        sum_turned(3)
        passes_to("b", 11)
        copy_cd(12, 13, 14)
        tiles_run(8, 2, RAW_A, EXTRA + 8)
        times_a(9)
        times_a(8)
        times_b(9)
        times_b(8)
        q0 = quantise(h0, GROUP, TAB1 + 8)
        q1 = quantise(h1, GROUP)
        h2 = h_tile("h2", 2 * GROUP, GROUP, H_A + 4)
        sum_run(8, 2)
        passes_to("b", 13)
        score(q0, 0, GROUP, 1)
        tiles_run(10, 2, H_B + 4, H_A - 7)
        times_a(11)
        times_a(10)
        times_b(11)
        times_b(10)
        sum_run(10, 2)
        score(q1, GROUP, GROUP, 1)
        h12 = h_tile("h12", 12, 2, H_C + 4)
        tiles_single(12, EXTRA)
        times(12)
        passes_to("b", 14)
        sum_turned(12)
        passes_to("b", 15)
        tiles_single(13, TAB2 + 8)
        times(13)
        sum_turned(13)
        tiles_single(14, TAB1)
        times(14)
        q2 = quantise(h2, GROUP)
        score(q2, 2 * GROUP, GROUP, 1)
        h14 = h_tile("h14", 14, 1, H_A + 4)
        sum_single(nc.gpsimd, 14)
        tiles_single(LAST, H_A + 10)
        times(LAST)
        q14 = quantise(h14, 1)
        q12 = quantise(h12, 2, TAB1)
        score(q14, 14, 1, 4)
        score(q12, 12, 2, 2)
        h15 = h_tile("h15", 15, 1, TAB1 + 2)
        for c in range(2):
            nc.vector.tensor_tensor(h_part(LAST, c), pa[LAST][:, c].rearrange("p n t -> p (n t)"),
                                    pb[LAST][:, c].rearrange("p n t -> p (n t)"), ADD)
        q15 = quantise(h15, 1, calls=2)
        score(q15, LAST, 1, 2, (nc.scalar.copy, nc.vector.tensor_copy))
